import numpy as np
import ml_dtypes


def mxq(x, axis, fmt="e4m3"):
    dtype, down = {"e4m3": (ml_dtypes.float8_e4m3fn, 7), "e5m2": (ml_dtypes.float8_e5m2, 14)}[fmt]
    v = np.moveaxis(np.asarray(x, np.float32).astype(ml_dtypes.bfloat16).astype(np.float64), axis, -1)
    blocks = v.reshape(v.shape[:-1] + (-1, 32))
    amax = np.abs(blocks).max(-1, keepdims=True)
    byte = np.maximum(np.where(amax > 0, np.frexp(amax)[1] - 1 + 127, 0) - down, 1)
    scale = np.exp2(byte - 127.0)
    codes = (blocks / scale).astype(np.float32).astype(dtype).astype(np.float64)
    return np.moveaxis((codes * scale).reshape(v.shape), -1, axis)


WIDE = False


def mx_kscale(k):
    if not WIDE:
        return np.ones(k)
    levels = np.array([10, -10, 5, -5, 0])
    if k % 512:
        return np.exp2(np.random.permutation(np.resize(levels, k // 32))).repeat(32)
    a = np.empty((k // 512, 16))
    for p in range(k // 512):
        a[p, :8] = np.random.permutation(np.resize(levels, 8))
        for g in range(8):
            far = levels[np.abs(levels - a[p, g]) >= 10]
            a[p, g + 8] = far[np.random.randint(len(far))]
    return np.exp2(a.ravel()).repeat(32)


def f64(x):
    return np.asarray(x).astype(np.float64)


def striped(idx):
    return np.tile(idx.reshape(-1, 16).T, (8, 1)).astype(np.uint16)


def unstriped(offs):
    return offs[:16].T.reshape(-1).astype(np.int64)


E2M1 = np.array([0.0, 0.5, 1.0, 1.5, 2.0, 3.0, 4.0, 6.0, -0.0, -0.5, -1.0, -1.5, -2.0, -3.0, -4.0, -6.0])


def pack_weight(w, fmt):
    k, n = w.shape
    w = f64(np.asarray(w, np.float32).astype(ml_dtypes.bfloat16)).reshape(k // 32, 32, n)
    amax = np.abs(w).max(1)
    if fmt == "e4m3":
        byte = np.frexp(amax)[1] - 1 + 127 - 7
    else:
        mant, ex = np.frexp(amax / 6.0)
        byte = np.where(mant > 0.5, ex, ex - 1) + 127
    byte = np.clip(np.where(amax > 0, byte, 1), 1, 254)
    scaled = (w * np.exp2(127.0 - byte)[:, None, :]).reshape(k, n).astype(np.float32)
    by_word = np.ascontiguousarray(scaled.reshape(k // 512, 128, 4, n).transpose(0, 1, 3, 2))
    if fmt == "e4m3":
        words = by_word.astype(ml_dtypes.float8_e4m3fn).view(np.uint8)
    else:
        c = by_word.astype(ml_dtypes.float4_e2m1fn).view(np.uint8) & 0xF
        words = (c[..., 0::2] | (c[..., 1::2] << 4)).reshape(k // 512, 128, 2 * n)
    return np.ascontiguousarray(words), np.ascontiguousarray(byte.astype(np.uint8).reshape(k // 512, 16, n))


def unpack_weight(words, scales, fmt):
    g, _, n = scales.shape
    words = np.ascontiguousarray(words).reshape(g, 128, n, -1)
    if fmt == "e4m3":
        vals = words.view(ml_dtypes.float8_e4m3fn).astype(np.float64)
    else:
        nib = np.empty((g, 128, n, 4), np.uint8)
        nib[..., 0::2] = words & 0xF
        nib[..., 1::2] = words >> 4
        vals = E2M1[nib]
    vals = vals * np.repeat(np.exp2(scales.astype(np.float64) - 127.0), 8, axis=1)[..., None]
    return vals.transpose(0, 1, 3, 2).reshape(g * 512, n)


def gelu(v):
    return 0.5 * v * (1.0 + np.tanh(np.sqrt(2.0 / np.pi) * (v + 0.044715 * v**3)))


def bf(x):
    return np.asarray(x, np.float32).astype(ml_dtypes.bfloat16)

def planes(Y):
    n, m = Y.shape
    b = f64(bf(Y)).reshape(n // 32, 32, m)
    amax = np.abs(b).max(1)
    byte = np.clip(np.where(amax > 0, np.frexp(amax)[1] - 1 + 127 - 7, 1), 1, 254)
    codes = (b * np.exp2(127.0 - byte)[:, None, :]).reshape(n, m).astype(np.float32).astype(ml_dtypes.float8_e4m3fn).view(np.uint8)
    words = codes.reshape(n // 512, 128, 4, m).transpose(0, 1, 3, 2)
    return np.ascontiguousarray(words), np.ascontiguousarray(byte.astype(np.uint8).reshape(n // 512, 16, m))


K, T, S, H, N = 1536, 4096, 1024, 512, 1024

def setup_inputs():
    n = np.random.standard_normal
    s = mx_kscale(K)[:, None]
    u = mx_kscale(H)[:, None]
    gain = np.exp(0.8 * n(N))[None, :]
    tab_words, tab_scales = pack_weight(n((K, T)) * s, "e4m3")
    ws_words, ws_scales = pack_weight(0.45 * n((K, H)) / np.sqrt(K) / s, "e2m1")
    wc = 0.3 * n((K, H)) / np.sqrt(K) / s
    ds = 1.5 * n((H, N)) / np.sqrt(H) * gain / u
    dc_words, dc_scales = pack_weight(n((H, N)) / np.sqrt(H) * gain / u, "e4m3")
    return {
        "tab_words": tab_words, "tab_scales": tab_scales,
        "offs": striped(np.random.permutation(T)[:S]),
        "ws_words": ws_words, "ws_scales": ws_scales,
        "wc": wc.astype(np.float32),
        "phase": np.random.uniform(-1.2, 1.2, H).astype(np.float32),
        "gs": (np.exp(0.3 * n(H)) * u[:, 0]).astype(np.float32),
        "gc": (np.exp(0.3 * n(H)) * u[:, 0]).astype(np.float32),
        "ds": ds.astype(np.float32),
        "dc_words": dc_words, "dc_scales": dc_scales,
    }

def reference(tab_words, tab_scales, offs, ws_words, ws_scales, wc, phase, gs, gc, ds, dc_words, dc_scales):
    v = unpack_weight(tab_words, tab_scales, "e4m3")[:, unstriped(offs)]
    ps = unpack_weight(ws_words, ws_scales, "e2m1").T @ v
    pc = mxq(f64(wc), 0, "e4m3").T @ v
    hs = np.sin(ps) * f64(gs)[:, None]
    hc = np.cos(pc + f64(phase)[:, None]) * f64(gc)[:, None]
    y = (mxq(f64(ds), 0, "e4m3").T @ mxq(hs, 0, "e4m3")
              + unpack_weight(dc_words, dc_scales, "e4m3").T @ mxq(hc, 0, "e4m3"))
    words, scales = planes(y)
    return y, words, scales

@@ -1,0 +1,315 @@
+from contextlib import ExitStack
+
+import concourse.mybir as mybir
+
+K, T, S, H, N = 1536, 4096, 1024, 512, 1024
+FLOPS = 2 * (2 * K * H * S + 2 * H * N * S)
+
+F32 = mybir.dt.float32
+BF16 = mybir.dt.bfloat16
+I32 = mybir.dt.int32
+U32 = mybir.dt.uint32
+U16 = mybir.dt.uint16
+U8 = mybir.dt.uint8
+FP8X4 = mybir.dt.float8_e4m3fn_x4
+FP4X4 = mybir.dt.float4_e2m1fn_x4
+ACT = mybir.ActivationFunctionType
+ALU = mybir.AluOpType
+
+P = 128
+PACK = 4
+PASSES = K // (P * PACK)
+GROUPS = N // (P * PACK)
+HALF = 512
+CHUNK = 256
+ROW_BASE = (0, 16, 64)
+
+
+def tile_list_tile_location_codes_kernel(
+    tc, tab_words, tab_scales, offs, ws_words, ws_scales, wc, phase, gs, gc, ds, dc_words, dc_scales,
+    out_0, out_1, out_2,
+):
+    nc = tc.nc
+    halves = S // HALF
+    chunks = S // CHUNK
+
+    with ExitStack() as ctx:
+        keep = ctx.enter_context(tc.tile_pool(name="keep", bufs=1))
+        ring = ctx.enter_context(tc.tile_pool(name="ring", bufs=3))
+        psum = ctx.enter_context(tc.psum_pool(name="psum", bufs=4))
+
+        offsets = keep.tile([P, S // 16], U16, name="offsets")
+        nc.sync.dma_start(offsets[:], offs)
+
+        tab_rows = keep.tile([P, T], U8, name="tab_rows", tag="rows", align_bytes=64)
+        ws_rows = keep.tile([P, H], U8, name="ws_rows", tag="picked0", align_bytes=64)
+        planes = [keep.tile([P, S + H], U8, name="plane%d" % a, align_bytes=64) for a in range(PASSES)]
+        warm = keep.tile([P, 8], F32, name="warm")
+        warm_out = keep.tile([P, 8], F32, name="warm_out")
+        nc.vector.memset(tab_rows[64:128, :].bitcast(I32), 0)
+        nc.vector.memset(ws_rows[64:128, :].bitcast(I32), 0)
+        nc.vector.memset(tab_rows[32:64, :].bitcast(I32), 0)
+        nc.vector.memset(ws_rows[32:64, :].bitcast(I32), 0)
+        nc.vector.memset(warm[:], 0.0)
+        for a in range(PASSES):
+            nc.vector.memset(planes[a][:].bitcast(I32), 0)
+
+        tab_flat = tab_scales.rearrange("a q t -> (a q) t").bitcast(I32)
+        ws_flat = ws_scales.rearrange("a q c -> (a q) c").bitcast(I32)
+        nc.sync.dma_start(tab_rows[0:32, :].bitcast(I32), tab_flat[0:32, :])
+        nc.scalar.dma_start(tab_rows[64:80, :].bitcast(I32), tab_flat[32:48, :])
+        nc.sync.dma_start(ws_rows[0:32, :].bitcast(I32), ws_flat[0:32, :])
+        nc.scalar.dma_start(ws_rows[64:80, :].bitcast(I32), ws_flat[32:48, :])
+        nc.scalar.activation(warm_out[:], warm[:], ACT.Sin)
+
+        gs_sb = keep.tile([P, PACK], F32, name="gs_sb")
+        gc_sb = keep.tile([P, PACK], F32, name="gc_sb")
+        phase_sb = keep.tile([P, PACK], F32, name="phase_sb", tag="table1", align_bytes=64)
+        nc.gpsimd.dma_start(phase_sb[:], phase.rearrange("(p t) -> p t", t=PACK))
+        nc.gpsimd.dma_start(gc_sb[:], gc.rearrange("(p t) -> p t", t=PACK))
+        nc.gpsimd.dma_start(gs_sb[:], gs.rearrange("(p t) -> p t", t=PACK))
+        half_phase = keep.tile([P, PACK], F32, name="half_phase")
+        minus_2gc = keep.tile([P, PACK], F32, name="minus_2gc")
+        nc.vector.tensor_scalar(half_phase[:], phase_sb[:], 0.5, None, ALU.mult)
+        nc.vector.tensor_scalar(minus_2gc[:], gc_sb[:], -2.0, None, ALU.mult)
+
+        ws_raw = keep.tile([P, PASSES, 2 * H], U8, name="ws_raw", align_bytes=64)
+
+        def load_table(a):
+            words = keep.tile([P, T], I32, name="table%d" % a, tag="table%d" % (a % 2), align_bytes=64)
+            nc.sync.dma_start(words[:], tab_words[a].rearrange("p t i -> p (t i)").bitcast(I32))
+            return words
+
+        nc.sync.dma_start(ws_raw[:].bitcast(I32), ws_words.rearrange("a p c -> p a c").bitcast(I32))
+        table = [load_table(0), load_table(1)]
+
+        picked_rows = keep.tile([P, S], U8, name="picked_rows", align_bytes=64)
+        staged = keep.tile([P, S + H], U8, name="staged", tag="raw0", align_bytes=64)
+        nc.vector.tensor_copy(picked_rows[:], tab_rows[:].indirect(offsets[:]))
+        nc.vector.tensor_copy(
+            staged[:, S:].rearrange("p (t m) -> p t m", t=PACK), ws_rows[:].rearrange("p (m t) -> p t m", t=PACK)
+        )
+        nc.vector.tensor_copy(staged[:, :S].bitcast(I32), picked_rows[:].bitcast(I32))
+        for a in range(PASSES):
+            for q in range(4):
+                row = ROW_BASE[a] + 4 * q
+                nc.scalar.dma_start(planes[a][32 * q : 32 * q + 4, :].bitcast(I32), staged[row : row + 4, :].bitcast(I32))
+        dc_plane_raw = keep.tile([P, N], U8, name="dc_plane_raw", tag="rows", align_bytes=64)
+        nc.vector.memset(dc_plane_raw[:].bitcast(I32), 0)
+        for q in range(4):
+            nc.gpsimd.dma_start(dc_plane_raw[32 * q : 32 * q + 4, :].bitcast(I32), dc_scales[0, 4 * q : 4 * q + 4, :].bitcast(I32))
+
+        ws_codes = keep.tile([P, PASSES, 2 * H], U8, name="ws_codes", tag="raw1", align_bytes=64)
+        for a in range(PASSES):
+            nc.vector.tensor_copy(
+                ws_codes[:, a, :].bitcast(U16).rearrange("p (t m) -> p t m", t=PACK),
+                ws_raw[:, a, :].bitcast(U16).rearrange("p (m t) -> p t m", t=PACK),
+            )
+
+        def load_weight(rows, name, tag):
+            raw = keep.tile([P, PACK, P * PACK], F32, name=name, tag=tag, align_bytes=64)
+            nc.sync.dma_start(raw[:], rows.rearrange("(p j) c -> p j c", j=PACK))
+            return raw
+
+
+        def round_weight(raw, on_scalar):
+            grouped = ring.tile([P, PACK, P, PACK], BF16, name="grouped", tag="grouped", align_bytes=64)
+            dst = grouped[:].rearrange("p t m j -> p m j t")
+            src = raw.rearrange("p j (m t) -> p m j t", t=PACK)
+            if on_scalar:
+                nc.scalar.copy(dst, src)
+            else:
+                nc.vector.tensor_copy(dst, src)
+            return grouped
+
+        def quantize(codes, scales, grouped_flat):
+            nc.vector.quantize_mx(out=codes.bitcast(FP8X4), scales=scales, in_=grouped_flat)
+
+        picked = []
+
+        def gather_words(a):
+            window = table[a][:].bitcast(U32)
+            if a + 1 < PASSES:
+                both = keep.tile([P, S], U32, name="picked%d" % a, align_bytes=64)
+                nc.vector.tensor_copy(both[:], window.indirect(offsets[:]))
+                return [both[:, HALF * h : HALF * (h + 1)] for h in range(halves)]
+            parts = [keep.tile([P, HALF], U32, name="picked_last%d" % h, align_bytes=64) for h in range(halves)]
+            for h in range(halves):
+                nc.vector.tensor_copy(parts[h][:], window.indirect(offsets[:, 32 * h : 32 * (h + 1)]))
+            return [part[:] for part in parts]
+
+        def first_pass(bank, lhsT, lhsT_scale, a, h):
+            nc.tensor.matmul_mx(
+                out=bank[:], lhsT=lhsT, lhsT_scale=lhsT_scale,
+                rhs=picked[a][h].bitcast(FP8X4), rhs_scale=planes[a][:, HALF * h : HALF * (h + 1)],
+                start=(a == 0), stop=(a == PASSES - 1),
+            )
+
+        sin_banks = [[psum.tile([P, HALF], F32, name="bank", tag="banks%d" % h) for t in range(PACK)] for h in range(halves)]
+        for a in range(PASSES):
+            picked.append(gather_words(a))
+            if a == 0:
+                table.append(load_table(2))
+            for h in range(halves):
+                for t in range(PACK):
+                    first_pass(
+                        sin_banks[h][t], ws_codes[:, a, 2 * P * t : 2 * P * (t + 1)].bitcast(FP4X4),
+                        planes[a][:, S + P * t : S + P * (t + 1)], a, h,
+                    )
+
+        wc_raw = [load_weight(wc[0:512, :], "wc_raw0", "raw0")[:]]
+        wc_rest = keep.tile([P, PASSES - 1, PACK, H], F32, name="wc_rest", tag="table1", align_bytes=64)
+        for a in range(1, PASSES):
+            nc.sync.dma_start(wc_rest[:, a - 1, :, :], wc[512 * a : 512 * (a + 1), :].rearrange("(p j) c -> p j c", j=PACK))
+            wc_raw.append(wc_rest[:, a - 1, :, :])
+        wc_codes = [keep.tile([P, H], U32, name="wc_codes%d" % a, align_bytes=64) for a in range(PASSES)]
+        wc_planes = [keep.tile([P, H], U8, name="wc_plane%d" % a, align_bytes=64) for a in range(PASSES)]
+        hs_codes = [keep.tile([P, CHUNK], U32, name="hs_codes%d" % c, align_bytes=64) for c in range(chunks)]
+        hs_planes = [keep.tile([P, CHUNK], U8, name="hs_plane%d" % c, align_bytes=64) for c in range(chunks)]
+        hc_codes = [keep.tile([P, CHUNK], U32, name="hc_codes%d" % c, align_bytes=64) for c in range(chunks)]
+        hc_planes = [keep.tile([P, CHUNK], U8, name="hc_plane%d" % c, align_bytes=64) for c in range(chunks)]
+        sines = [keep.tile([P, PACK, HALF], F32, name="sines%d" % h) for h in range(halves)]
+
+        def sine_half(h):
+            for t in range(PACK):
+                nc.scalar.activation(sines[h][:, t, :], sin_banks[h][t][:], ACT.Sin)
+
+        def hs_round(c):
+            h, c0 = divmod(c * CHUNK, HALF)
+            feat = ring.tile([P, CHUNK, PACK], BF16, name="feat", tag="feat", align_bytes=64)
+            nc.vector.tensor_tensor(
+                feat[:].rearrange("p (c i) t -> p c t i", i=2),
+                sines[h][:, :, c0 : c0 + CHUNK].rearrange("p t (c i) -> p c t i", i=2),
+                gs_sb[:].unsqueeze(1).unsqueeze(3).to_broadcast([P, CHUNK // 2, PACK, 2]),
+                ALU.mult,
+            )
+            return feat
+
+        def quantize_feat(feat, codes, plane):
+            quantize(codes[:], plane[:], feat[:].rearrange("p n t -> p (n t)"))
+
+        def quantize_weight(grouped, codes, plane):
+            quantize(codes, plane, grouped[:].rearrange("p t m j -> p (t m j)"))
+
+        cos_banks = [[None] * PACK for h in range(halves)]
+
+        def cos_pass(a, h):
+            for t in range(PACK):
+                if a == 0:
+                    cos_banks[h][t] = psum.tile([P, HALF], F32, name="bank", tag="banks%d" % h)
+                first_pass(
+                    cos_banks[h][t], wc_codes[a][:, P * t : P * (t + 1)].bitcast(FP8X4),
+                    wc_planes[a][:, P * t : P * (t + 1)], a, h,
+                )
+
+        sine_half(0)
+        g0 = round_weight(wc_raw[0], False)
+        g1 = round_weight(wc_raw[1], True)
+        quantize_weight(g0, wc_codes[0][:], wc_planes[0][:])
+        sine_half(1)
+        g2 = round_weight(wc_raw[2], False)
+        quantize_weight(g1, wc_codes[1][:], wc_planes[1][:])
+        quantize_weight(g2, wc_codes[2][:], wc_planes[2][:])
+        for h in range(halves):
+            for a in range(PASSES):
+                cos_pass(a, h)
+
+        ds_raw = [load_weight(ds[:, 0:512], "ds_raw0", "raw0")]
+        dc_raw = keep.tile([P, N], I32, name="dc_raw", tag="table0", align_bytes=64)
+        nc.sync.dma_start(dc_raw[:], dc_words[0].rearrange("p c i -> p (c i)").bitcast(I32))
+        ds_raw.append(load_weight(ds[:, 512:1024], "ds_raw1", "raw1"))
+
+        def cos_chunk(c):
+            h, c0 = divmod(c * CHUNK, HALF)
+            half_sine = ring.tile([P, PACK, CHUNK], F32, name="half_sine", tag="half_sine", bufs=2)
+            for t in range(PACK):
+                nc.scalar.activation(
+                    half_sine[:, t, :], cos_banks[h][t][:, c0 : c0 + CHUNK], ACT.Sin, bias=half_phase[:, t : t + 1], scale=0.5
+                )
+            squared = ring.tile([P, CHUNK, PACK], F32, name="squared", tag="squared", bufs=2)
+            nc.scalar.activation(
+                squared[:].rearrange("p (c i) t -> p c t i", i=4),
+                half_sine[:].rearrange("p t (c i) -> p c t i", i=4),
+                ACT.Square,
+            )
+            return squared
+
+        def hc_round(squared):
+            feat = ring.tile([P, CHUNK, PACK], BF16, name="feat", tag="feat", align_bytes=64)
+            nc.vector.scalar_tensor_tensor(
+                feat[:], squared[:], -0.5, minus_2gc[:].unsqueeze(1).to_broadcast([P, CHUNK, PACK]), ALU.add, ALU.mult
+            )
+            return feat
+
+        ds_codes = [keep.tile([P, 512], U32, name="ds_codes%d" % g, align_bytes=64) for g in range(GROUPS)]
+        ds_plane = [keep.tile([P, 512], U8, name="ds_plane%d" % g, align_bytes=64) for g in range(GROUPS)]
+        dc_codes = [keep.tile([P, 512], I32, name="dc_codes%d" % g, align_bytes=64) for g in range(GROUPS)]
+        dc_plane = [keep.tile([P, 512], U8, name="dc_plane%d" % g, align_bytes=64) for g in range(GROUPS)]
+        y_codes = keep.tile([P, GROUPS, S], I32, name="y_codes", align_bytes=64)
+        y_plane = keep.tile([P, GROUPS, S], U8, name="y_plane", align_bytes=64)
+
+        def second_weights(g):
+            n_cols = slice(512 * g, 512 * (g + 1))
+            gd = round_weight(ds_raw[g][:], g == 1)
+            for dealt, raw in ((dc_plane[g], dc_plane_raw), (dc_codes[g], dc_raw)):
+                nc.vector.tensor_copy(
+                    dealt[:].rearrange("p (t m) -> p t m", t=PACK), raw[:, n_cols].rearrange("p (m t) -> p t m", t=PACK)
+                )
+            quantize_weight(gd, ds_codes[g][:], ds_plane[g][:])
+
+        out_rows = out_0.rearrange("(g p t) j -> g p t j", g=GROUPS, t=PACK)
+        out_words = out_1.rearrange("g p m t -> p g (m t)").bitcast(I32)
+
+        def second_stage(c, g):
+            cols = slice(CHUNK * c, CHUNK * (c + 1))
+            y = ring.tile([P, PACK, CHUNK], F32, name="y", tag="y", bufs=4)
+            for pair in range(PACK // 2):
+                bank = psum.tile([P, 2, CHUNK], F32, name="bank", tag="banks%d" % (c == chunks - 1))
+                for u in range(2):
+                    n0 = P * (2 * pair + u)
+                    nc.tensor.matmul_mx(
+                        out=bank[:, u, :], lhsT=ds_codes[g][:, n0 : n0 + P].bitcast(FP8X4), lhsT_scale=ds_plane[g][:, n0 : n0 + P],
+                        rhs=hs_codes[c][:].bitcast(FP8X4), rhs_scale=hs_planes[c][:], start=True, stop=False,
+                    )
+                    nc.tensor.matmul_mx(
+                        out=bank[:, u, :], lhsT=dc_codes[g][:, n0 : n0 + P].bitcast(FP8X4), lhsT_scale=dc_plane[g][:, n0 : n0 + P],
+                        rhs=hc_codes[c][:].bitcast(FP8X4), rhs_scale=hc_planes[c][:], start=False, stop=True,
+                    )
+                nc.scalar.copy(y[:, 2 * pair : 2 * pair + 2, :], bank[:])
+            nc.sync.dma_start(out_rows[g, :, :, cols], y[:])
+            return y
+
+        def y_round(y):
+            yb = ring.tile([P, CHUNK, PACK], BF16, name="yb", tag="yb", align_bytes=64)
+            nc.vector.tensor_copy(
+                yb[:].rearrange("p (c i) t -> p c t i", i=4), y[:].rearrange("p t (c i) -> p c t i", i=4)
+            )
+            return yb
+
+        fs = [hs_round(c) for c in range(2)]
+        for c in range(2):
+            quantize_feat(fs[c], hs_codes[c], hs_planes[c])
+        sq = [cos_chunk(0)]
+        for c in range(chunks):
+            cols = slice(CHUNK * c, CHUNK * (c + 1))
+            fc = hc_round(sq[c])
+            if c == 0:
+                second_weights(0)
+            if c + 1 < chunks:
+                sq.append(cos_chunk(c + 1))
+            quantize_feat(fc, hc_codes[c], hc_planes[c])
+            if c == 0:
+                second_weights(1)
+            ys = [second_stage(c, g) for g in range(GROUPS)]
+            if c + 2 < chunks:
+                f = hs_round(c + 2)
+            ybs = [y_round(y) for y in ys]
+            if c + 2 < chunks:
+                quantize_feat(f, hs_codes[c + 2], hs_planes[c + 2])
+            for g in range(GROUPS):
+                quantize(y_codes[:, g, cols], y_plane[:, g, cols], ybs[g][:].rearrange("p n t -> p (n t)"))
+            nc.sync.dma_start(out_words[:, :, cols], y_codes[:, :, cols])
+
+        out_planes = out_2.rearrange("g q m -> q g m").bitcast(I32)
+        for q in range(4):
+            nc.sync.dma_start(out_planes[4 * q : 4 * q + 4, :, :], y_plane[32 * q : 32 * q + 4, :, :].bitcast(I32))

@@ -41,79 +41,80 @@ def tile_list_tile_location_codes_kernel(
         offsets = keep.tile([P, S // 16], U16, name="offsets")
         nc.sync.dma_start(offsets[:], offs)
 
-        tab_rows = keep.tile([P, T], U8, name="tab_rows", tag="rows", align_bytes=64)
-        ws_rows = keep.tile([P, H], U8, name="ws_rows", tag="picked0", align_bytes=64)
+        tab_flat = tab_scales.rearrange("a q t -> (a q) t").bitcast(I32)
+        ws_flat = ws_scales.rearrange("a q c -> (a q) c").bitcast(I32)
+        tab_rows = keep.tile([P, T], U8, name="tab_rows", align_bytes=64)
+        ws_rows = keep.tile([P, H], U8, name="ws_rows", align_bytes=64)
         planes = [keep.tile([P, S + H], U8, name="plane%d" % a, align_bytes=64) for a in range(PASSES)]
+        dc_plane_raw = keep.tile([P, N], U8, name="dc_plane_raw", align_bytes=64)
         warm = keep.tile([P, 8], F32, name="warm")
         warm_out = keep.tile([P, 8], F32, name="warm_out")
-        nc.vector.memset(tab_rows[64:128, :].bitcast(I32), 0)
-        nc.vector.memset(ws_rows[64:128, :].bitcast(I32), 0)
-        nc.vector.memset(tab_rows[32:64, :].bitcast(I32), 0)
-        nc.vector.memset(ws_rows[32:64, :].bitcast(I32), 0)
+        for part in (slice(64, 128), slice(32, 64)):
+            for rows in (tab_rows, ws_rows):
+                nc.vector.memset(rows[part, :].bitcast(I32), 0)
         nc.vector.memset(warm[:], 0.0)
+        nc.vector.memset(dc_plane_raw[:].bitcast(I32), 0)
         for a in range(PASSES):
             nc.vector.memset(planes[a][:].bitcast(I32), 0)
 
-        tab_flat = tab_scales.rearrange("a q t -> (a q) t").bitcast(I32)
-        ws_flat = ws_scales.rearrange("a q c -> (a q) c").bitcast(I32)
-        nc.sync.dma_start(tab_rows[0:32, :].bitcast(I32), tab_flat[0:32, :])
-        nc.scalar.dma_start(tab_rows[64:80, :].bitcast(I32), tab_flat[32:48, :])
-        nc.sync.dma_start(ws_rows[0:32, :].bitcast(I32), ws_flat[0:32, :])
-        nc.scalar.dma_start(ws_rows[64:80, :].bitcast(I32), ws_flat[32:48, :])
-        nc.scalar.activation(warm_out[:], warm[:], ACT.Sin)
+        ws_raw = keep.tile([P, PASSES, 2 * H], U8, name="ws_raw", align_bytes=64)
+        nc.sync.dma_start(ws_raw[:].bitcast(I32), ws_words.rearrange("a p c -> p a c").bitcast(I32))
+        for rows, flat in ((tab_rows, tab_flat), (ws_rows, ws_flat)):
+            nc.sync.dma_start(rows[0:32, :].bitcast(I32), flat[0:32, :])
+            nc.sync.dma_start(rows[64:80, :].bitcast(I32), flat[32:48, :])
 
         gs_sb = keep.tile([P, PACK], F32, name="gs_sb")
         gc_sb = keep.tile([P, PACK], F32, name="gc_sb")
-        phase_sb = keep.tile([P, PACK], F32, name="phase_sb", tag="table1", align_bytes=64)
+        phase_sb = keep.tile([P, PACK], F32, name="phase_sb")
+        nc.scalar.activation(warm_out[:], warm[:], ACT.Sin)
+        nc.gpsimd.dma_start(gs_sb[:], gs.rearrange("(p t) -> p t", t=PACK))
         nc.gpsimd.dma_start(phase_sb[:], phase.rearrange("(p t) -> p t", t=PACK))
         nc.gpsimd.dma_start(gc_sb[:], gc.rearrange("(p t) -> p t", t=PACK))
-        nc.gpsimd.dma_start(gs_sb[:], gs.rearrange("(p t) -> p t", t=PACK))
+        for q in range(4):
+            nc.gpsimd.dma_start(dc_plane_raw[32 * q : 32 * q + 4, :].bitcast(I32), dc_scales[0, 4 * q : 4 * q + 4, :].bitcast(I32))
         half_phase = keep.tile([P, PACK], F32, name="half_phase")
         minus_2gc = keep.tile([P, PACK], F32, name="minus_2gc")
-        nc.vector.tensor_scalar(half_phase[:], phase_sb[:], 0.5, None, ALU.mult)
-        nc.vector.tensor_scalar(minus_2gc[:], gc_sb[:], -2.0, None, ALU.mult)
+        nc.gpsimd.tensor_scalar(half_phase[:], phase_sb[:], 0.5, None, ALU.mult)
+        nc.gpsimd.tensor_scalar(minus_2gc[:], gc_sb[:], -2.0, None, ALU.mult)
 
-        ws_raw = keep.tile([P, PASSES, 2 * H], U8, name="ws_raw", align_bytes=64)
+        table = [keep.tile([P, T], I32, name="table%d" % a, align_bytes=64) for a in range(PASSES)]
+        dc_raw = keep.tile([P, N], I32, name="dc_raw", align_bytes=64)
+        nc.sync.dma_start(dc_raw[:], dc_words[0].rearrange("p c i -> p (c i)").bitcast(I32))
 
         def load_table(a):
-            words = keep.tile([P, T], I32, name="table%d" % a, tag="table%d" % (a % 2), align_bytes=64)
-            nc.sync.dma_start(words[:], tab_words[a].rearrange("p t i -> p (t i)").bitcast(I32))
-            return words
+            nc.sync.dma_start(table[a][:], tab_words[a].rearrange("p t i -> p (t i)").bitcast(I32))
 
-        nc.sync.dma_start(ws_raw[:].bitcast(I32), ws_words.rearrange("a p c -> p a c").bitcast(I32))
-        table = [load_table(0), load_table(1)]
+        load_table(0)
 
         picked_rows = keep.tile([P, S], U8, name="picked_rows", align_bytes=64)
-        staged = keep.tile([P, S + H], U8, name="staged", tag="raw0", align_bytes=64)
+        staged = keep.tile([P, S + H], U8, name="staged", align_bytes=64)
         nc.vector.tensor_copy(picked_rows[:], tab_rows[:].indirect(offsets[:]))
         nc.vector.tensor_copy(
             staged[:, S:].rearrange("p (t m) -> p t m", t=PACK), ws_rows[:].rearrange("p (m t) -> p t m", t=PACK)
         )
         nc.vector.tensor_copy(staged[:, :S].bitcast(I32), picked_rows[:].bitcast(I32))
-        for a in range(PASSES):
-            for q in range(4):
+        moves = [(a, q) for a in range(PASSES) for q in range(4)]
+        for b in range(2):
+            for a, q in moves[6 * b : 6 * b + 6]:
                 row = ROW_BASE[a] + 4 * q
-                nc.scalar.dma_start(planes[a][32 * q : 32 * q + 4, :].bitcast(I32), staged[row : row + 4, :].bitcast(I32))
-        dc_plane_raw = keep.tile([P, N], U8, name="dc_plane_raw", tag="rows", align_bytes=64)
-        nc.vector.memset(dc_plane_raw[:].bitcast(I32), 0)
-        for q in range(4):
-            nc.gpsimd.dma_start(dc_plane_raw[32 * q : 32 * q + 4, :].bitcast(I32), dc_scales[0, 4 * q : 4 * q + 4, :].bitcast(I32))
+                nc.sync.dma_start(planes[a][32 * q : 32 * q + 4, :].bitcast(I32), staged[row : row + 4, :].bitcast(I32))
+            load_table(b + 1)
 
-        ws_codes = keep.tile([P, PASSES, 2 * H], U8, name="ws_codes", tag="raw1", align_bytes=64)
+        ws_codes = keep.tile([P, PASSES, 2 * H], U8, name="ws_codes", align_bytes=64)
         for a in range(PASSES):
             nc.vector.tensor_copy(
                 ws_codes[:, a, :].bitcast(U16).rearrange("p (t m) -> p t m", t=PACK),
                 ws_raw[:, a, :].bitcast(U16).rearrange("p (m t) -> p t m", t=PACK),
             )
 
-        def load_weight(rows, name, tag):
-            raw = keep.tile([P, PACK, P * PACK], F32, name=name, tag=tag, align_bytes=64)
+        def load_weight(rows, name):
+            raw = keep.tile([P, PACK, P * PACK], F32, name=name, align_bytes=64)
             nc.sync.dma_start(raw[:], rows.rearrange("(p j) c -> p j c", j=PACK))
             return raw
 
 
-        def round_weight(raw, on_scalar):
-            grouped = ring.tile([P, PACK, P, PACK], BF16, name="grouped", tag="grouped", align_bytes=64)
+        def round_weight(raw, on_scalar, tag="grouped"):
+            grouped = ring.tile([P, PACK, P, PACK], BF16, name="grouped", tag=tag, bufs=2 if tag == "grouped" else 1, align_bytes=64)
             dst = grouped[:].rearrange("p t m j -> p m j t")
             src = raw.rearrange("p j (m t) -> p m j t", t=PACK)
             if on_scalar:
@@ -148,8 +149,6 @@ def tile_list_tile_location_codes_kernel(
         sin_banks = [[psum.tile([P, HALF], F32, name="bank", tag="banks%d" % h) for t in range(PACK)] for h in range(halves)]
         for a in range(PASSES):
             picked.append(gather_words(a))
-            if a == 0:
-                table.append(load_table(2))
             for h in range(halves):
                 for t in range(PACK):
                     first_pass(
@@ -157,11 +156,7 @@ def tile_list_tile_location_codes_kernel(
                         planes[a][:, S + P * t : S + P * (t + 1)], a, h,
                     )
 
-        wc_raw = [load_weight(wc[0:512, :], "wc_raw0", "raw0")[:]]
-        wc_rest = keep.tile([P, PASSES - 1, PACK, H], F32, name="wc_rest", tag="table1", align_bytes=64)
-        for a in range(1, PASSES):
-            nc.sync.dma_start(wc_rest[:, a - 1, :, :], wc[512 * a : 512 * (a + 1), :].rearrange("(p j) c -> p j c", j=PACK))
-            wc_raw.append(wc_rest[:, a - 1, :, :])
+        wc_raw = [load_weight(wc[512 * a : 512 * (a + 1), :], "wc_raw%d" % a)[:] for a in range(PASSES)]
         wc_codes = [keep.tile([P, H], U32, name="wc_codes%d" % a, align_bytes=64) for a in range(PASSES)]
         wc_planes = [keep.tile([P, H], U8, name="wc_plane%d" % a, align_bytes=64) for a in range(PASSES)]
         hs_codes = [keep.tile([P, CHUNK], U32, name="hs_codes%d" % c, align_bytes=64) for c in range(chunks)]
@@ -176,7 +171,7 @@ def tile_list_tile_location_codes_kernel(
 
         def hs_round(c):
             h, c0 = divmod(c * CHUNK, HALF)
-            feat = ring.tile([P, CHUNK, PACK], BF16, name="feat", tag="feat", align_bytes=64)
+            feat = ring.tile([P, CHUNK, PACK], BF16, name="feat", tag="late", bufs=1, align_bytes=64)
             nc.vector.tensor_tensor(
                 feat[:].rearrange("p (c i) t -> p c t i", i=2),
                 sines[h][:, :, c0 : c0 + CHUNK].rearrange("p t (c i) -> p c t i", i=2),
@@ -204,20 +199,17 @@ def tile_list_tile_location_codes_kernel(
 
         sine_half(0)
         g0 = round_weight(wc_raw[0], False)
-        g1 = round_weight(wc_raw[1], True)
+        g1 = round_weight(wc_raw[1], False)
         quantize_weight(g0, wc_codes[0][:], wc_planes[0][:])
         sine_half(1)
-        g2 = round_weight(wc_raw[2], False)
         quantize_weight(g1, wc_codes[1][:], wc_planes[1][:])
+        g2 = round_weight(wc_raw[2], False, "late")
         quantize_weight(g2, wc_codes[2][:], wc_planes[2][:])
         for h in range(halves):
             for a in range(PASSES):
                 cos_pass(a, h)
 
-        ds_raw = [load_weight(ds[:, 0:512], "ds_raw0", "raw0")]
-        dc_raw = keep.tile([P, N], I32, name="dc_raw", tag="table0", align_bytes=64)
-        nc.sync.dma_start(dc_raw[:], dc_words[0].rearrange("p c i -> p (c i)").bitcast(I32))
-        ds_raw.append(load_weight(ds[:, 512:1024], "ds_raw1", "raw1"))
+        ds_raw = [load_weight(ds[:, 512 * g : 512 * (g + 1)], "ds_raw%d" % g) for g in range(GROUPS)]
 
         def cos_chunk(c):
             h, c0 = divmod(c * CHUNK, HALF)
@@ -244,17 +236,19 @@ def tile_list_tile_location_codes_kernel(
         ds_codes = [keep.tile([P, 512], U32, name="ds_codes%d" % g, align_bytes=64) for g in range(GROUPS)]
         ds_plane = [keep.tile([P, 512], U8, name="ds_plane%d" % g, align_bytes=64) for g in range(GROUPS)]
         dc_codes = [keep.tile([P, 512], I32, name="dc_codes%d" % g, align_bytes=64) for g in range(GROUPS)]
-        dc_plane = [keep.tile([P, 512], U8, name="dc_plane%d" % g, align_bytes=64) for g in range(GROUPS)]
+        dc_plane = keep.tile([P, GROUPS, 512], U8, name="dc_plane", tag="staged", align_bytes=64)
+        nc.vector.tensor_copy(
+            dc_plane[:].rearrange("p g (t m) -> p g t m", t=PACK), dc_plane_raw[:].rearrange("p (g m t) -> p g t m", g=GROUPS, t=PACK)
+        )
         y_codes = keep.tile([P, GROUPS, S], I32, name="y_codes", align_bytes=64)
         y_plane = keep.tile([P, GROUPS, S], U8, name="y_plane", align_bytes=64)
 
         def second_weights(g):
             n_cols = slice(512 * g, 512 * (g + 1))
             gd = round_weight(ds_raw[g][:], g == 1)
-            for dealt, raw in ((dc_plane[g], dc_plane_raw), (dc_codes[g], dc_raw)):
-                nc.vector.tensor_copy(
-                    dealt[:].rearrange("p (t m) -> p t m", t=PACK), raw[:, n_cols].rearrange("p (m t) -> p t m", t=PACK)
-                )
+            nc.vector.tensor_copy(
+                dc_codes[g][:].rearrange("p (t m) -> p m t", t=PACK), dc_raw[:, n_cols].rearrange("p (m t) -> p m t", t=PACK)
+            )
             quantize_weight(gd, ds_codes[g][:], ds_plane[g][:])
 
         out_rows = out_0.rearrange("(g p t) j -> g p t j", g=GROUPS, t=PACK)
@@ -272,7 +266,7 @@ def tile_list_tile_location_codes_kernel(
                         rhs=hs_codes[c][:].bitcast(FP8X4), rhs_scale=hs_planes[c][:], start=True, stop=False,
                     )
                     nc.tensor.matmul_mx(
-                        out=bank[:, u, :], lhsT=dc_codes[g][:, n0 : n0 + P].bitcast(FP8X4), lhsT_scale=dc_plane[g][:, n0 : n0 + P],
+                        out=bank[:, u, :], lhsT=dc_codes[g][:, n0 : n0 + P].bitcast(FP8X4), lhsT_scale=dc_plane[:, g, n0 : n0 + P],
                         rhs=hc_codes[c][:].bitcast(FP8X4), rhs_scale=hc_planes[c][:], start=False, stop=True,
                     )
                 nc.scalar.copy(y[:, 2 * pair : 2 * pair + 2, :], bank[:])
@@ -286,9 +280,7 @@ def tile_list_tile_location_codes_kernel(
             )
             return yb
 
-        fs = [hs_round(c) for c in range(2)]
-        for c in range(2):
-            quantize_feat(fs[c], hs_codes[c], hs_planes[c])
+        quantize_feat(hs_round(0), hs_codes[0], hs_planes[0])
         sq = [cos_chunk(0)]
         for c in range(chunks):
             cols = slice(CHUNK * c, CHUNK * (c + 1))
@@ -301,11 +293,11 @@ def tile_list_tile_location_codes_kernel(
             if c == 0:
                 second_weights(1)
             ys = [second_stage(c, g) for g in range(GROUPS)]
-            if c + 2 < chunks:
-                f = hs_round(c + 2)
+            if c + 1 < chunks:
+                f = hs_round(c + 1)
             ybs = [y_round(y) for y in ys]
-            if c + 2 < chunks:
-                quantize_feat(f, hs_codes[c + 2], hs_planes[c + 2])
+            if c + 1 < chunks:
+                quantize_feat(f, hs_codes[c + 1], hs_planes[c + 1])
             for g in range(GROUPS):
                 quantize(y_codes[:, g, cols], y_plane[:, g, cols], ybs[g][:].rearrange("p n t -> p (n t)"))
             nc.sync.dma_start(out_words[:, :, cols], y_codes[:, :, cols])

@@ -63,19 +63,7 @@ def tile_list_tile_location_codes_kernel(
             nc.sync.dma_start(rows[0:32, :].bitcast(I32), flat[0:32, :])
             nc.sync.dma_start(rows[64:80, :].bitcast(I32), flat[32:48, :])
 
-        gs_sb = keep.tile([P, PACK], F32, name="gs_sb")
-        gc_sb = keep.tile([P, PACK], F32, name="gc_sb")
-        phase_sb = keep.tile([P, PACK], F32, name="phase_sb")
         nc.scalar.activation(warm_out[:], warm[:], ACT.Sin)
-        nc.gpsimd.dma_start(gs_sb[:], gs.rearrange("(p t) -> p t", t=PACK))
-        nc.gpsimd.dma_start(phase_sb[:], phase.rearrange("(p t) -> p t", t=PACK))
-        nc.gpsimd.dma_start(gc_sb[:], gc.rearrange("(p t) -> p t", t=PACK))
-        for q in range(4):
-            nc.gpsimd.dma_start(dc_plane_raw[32 * q : 32 * q + 4, :].bitcast(I32), dc_scales[0, 4 * q : 4 * q + 4, :].bitcast(I32))
-        half_phase = keep.tile([P, PACK], F32, name="half_phase")
-        minus_2gc = keep.tile([P, PACK], F32, name="minus_2gc")
-        nc.gpsimd.tensor_scalar(half_phase[:], phase_sb[:], 0.5, None, ALU.mult)
-        nc.gpsimd.tensor_scalar(minus_2gc[:], gc_sb[:], -2.0, None, ALU.mult)
 
         table = [keep.tile([P, T], I32, name="table%d" % a, align_bytes=64) for a in range(PASSES)]
         dc_raw = keep.tile([P, N], I32, name="dc_raw", align_bytes=64)
@@ -99,6 +87,17 @@ def tile_list_tile_location_codes_kernel(
                 row = ROW_BASE[a] + 4 * q
                 nc.sync.dma_start(planes[a][32 * q : 32 * q + 4, :].bitcast(I32), staged[row : row + 4, :].bitcast(I32))
             load_table(b + 1)
+
+        gs_sb = keep.tile([P, PACK], F32, name="gs_sb")
+        gc_sb = keep.tile([P, PACK], F32, name="gc_sb")
+        phase_sb = keep.tile([P, PACK], F32, name="phase_sb")
+        nc.sync.dma_start(gs_sb[:], gs.rearrange("(p t) -> p t", t=PACK))
+        nc.sync.dma_start(phase_sb[:], phase.rearrange("(p t) -> p t", t=PACK))
+        nc.sync.dma_start(gc_sb[:], gc.rearrange("(p t) -> p t", t=PACK))
+        half_phase = keep.tile([P, PACK], F32, name="half_phase")
+        minus_2gc = keep.tile([P, PACK], F32, name="minus_2gc")
+        nc.scalar.mul(half_phase[:], phase_sb[:], 0.5)
+        nc.scalar.mul(minus_2gc[:], gc_sb[:], -2.0)
 
         ws_codes = keep.tile([P, PASSES, 2 * H], U8, name="ws_codes", align_bytes=64)
         for a in range(PASSES):
@@ -156,7 +155,10 @@ def tile_list_tile_location_codes_kernel(
                         planes[a][:, S + P * t : S + P * (t + 1)], a, h,
                     )
 
-        wc_raw = [load_weight(wc[512 * a : 512 * (a + 1), :], "wc_raw%d" % a)[:] for a in range(PASSES)]
+        wc_raw = [load_weight(wc[512 * a : 512 * (a + 1), :], "wc_raw%d" % a)[:] for a in range(2)]
+        for q in range(4):
+            nc.sync.dma_start(dc_plane_raw[32 * q : 32 * q + 4, :].bitcast(I32), dc_scales[0, 4 * q : 4 * q + 4, :].bitcast(I32))
+        wc_raw.append(load_weight(wc[1024:1536, :], "wc_raw2")[:])
         wc_codes = [keep.tile([P, H], U32, name="wc_codes%d" % a, align_bytes=64) for a in range(PASSES)]
         wc_planes = [keep.tile([P, H], U8, name="wc_plane%d" % a, align_bytes=64) for a in range(PASSES)]
         hs_codes = [keep.tile([P, CHUNK], U32, name="hs_codes%d" % c, align_bytes=64) for c in range(chunks)]
@@ -236,7 +238,7 @@ def tile_list_tile_location_codes_kernel(
         ds_codes = [keep.tile([P, 512], U32, name="ds_codes%d" % g, align_bytes=64) for g in range(GROUPS)]
         ds_plane = [keep.tile([P, 512], U8, name="ds_plane%d" % g, align_bytes=64) for g in range(GROUPS)]
         dc_codes = [keep.tile([P, 512], I32, name="dc_codes%d" % g, align_bytes=64) for g in range(GROUPS)]
-        dc_plane = keep.tile([P, GROUPS, 512], U8, name="dc_plane", tag="staged", align_bytes=64)
+        dc_plane = keep.tile([P, GROUPS, 512], U8, name="dc_plane", align_bytes=64)
         nc.vector.tensor_copy(
             dc_plane[:].rearrange("p g (t m) -> p g t m", t=PACK), dc_plane_raw[:].rearrange("p (g m t) -> p g t m", g=GROUPS, t=PACK)
         )

@@ -22,7 +22,7 @@ PASSES = K // (P * PACK)
 GROUPS = N // (P * PACK)
 HALF = 512
 CHUNK = 256
-ROW_BASE = (0, 16, 64)
+ROW_BASE = (80, 96, 112)
 
 
 def tile_list_tile_location_codes_kernel(
@@ -45,48 +45,54 @@ def tile_list_tile_location_codes_kernel(
         ws_flat = ws_scales.rearrange("a q c -> (a q) c").bitcast(I32)
         tab_rows = keep.tile([P, T], U8, name="tab_rows", align_bytes=64)
         ws_rows = keep.tile([P, H], U8, name="ws_rows", align_bytes=64)
-        planes = [keep.tile([P, S + H], U8, name="plane%d" % a, align_bytes=64) for a in range(PASSES)]
-        dc_plane_raw = keep.tile([P, N], U8, name="dc_plane_raw", align_bytes=64)
+        dc_rows = keep.tile([P, N], U8, name="dc_rows", align_bytes=64)
+        widths = [S + H, S + H, S + H + N]
+        planes = [keep.tile([P, widths[a]], U8, name="plane%d" % a, align_bytes=64) for a in range(PASSES)]
         warm = keep.tile([P, 8], F32, name="warm")
         warm_out = keep.tile([P, 8], F32, name="warm_out")
-        for part in (slice(64, 128), slice(32, 64)):
-            for rows in (tab_rows, ws_rows):
-                nc.vector.memset(rows[part, :].bitcast(I32), 0)
+        for rows, flat in ((tab_rows, tab_flat), (ws_rows, ws_flat)):
+            nc.sync.dma_start(rows[96:128, :].bitcast(I32), flat[16:48, :])
+            nc.sync.dma_start(rows[80:96, :].bitcast(I32), flat[0:16, :])
+        nc.sync.dma_start(dc_rows[112:128, :].bitcast(I32), dc_scales[0].bitcast(I32))
         nc.vector.memset(warm[:], 0.0)
-        nc.vector.memset(dc_plane_raw[:].bitcast(I32), 0)
+        for rows in (tab_rows, ws_rows):
+            nc.vector.memset(rows[0:80, :].bitcast(I32), 0)
+        nc.vector.memset(dc_rows[0:112, :].bitcast(I32), 0)
         for a in range(PASSES):
             nc.vector.memset(planes[a][:].bitcast(I32), 0)
 
-        ws_raw = keep.tile([P, PASSES, 2 * H], U8, name="ws_raw", align_bytes=64)
-        nc.sync.dma_start(ws_raw[:].bitcast(I32), ws_words.rearrange("a p c -> p a c").bitcast(I32))
-        for rows, flat in ((tab_rows, tab_flat), (ws_rows, ws_flat)):
-            nc.sync.dma_start(rows[0:32, :].bitcast(I32), flat[0:32, :])
-            nc.sync.dma_start(rows[64:80, :].bitcast(I32), flat[32:48, :])
-
         nc.scalar.activation(warm_out[:], warm[:], ACT.Sin)
 
-        table = [keep.tile([P, T], I32, name="table%d" % a, align_bytes=64) for a in range(PASSES)]
-        dc_raw = keep.tile([P, N], I32, name="dc_raw", align_bytes=64)
-        nc.sync.dma_start(dc_raw[:], dc_words[0].rearrange("p c i -> p (c i)").bitcast(I32))
+        table = [keep.tile([P, T], I32, name="table%d" % a, tag="table%d" % a, align_bytes=64) for a in range(PASSES)]
 
-        def load_table(a):
-            nc.sync.dma_start(table[a][:], tab_words[a].rearrange("p t i -> p (t i)").bitcast(I32))
+        def load_table(a, cols):
+            nc.sync.dma_start(table[a][:, cols], tab_words[a].rearrange("p t i -> p (t i)").bitcast(I32)[:, cols])
 
-        load_table(0)
+        load_table(0, slice(0, T))
+        ws_raw = keep.tile([P, PASSES, 2 * H], U8, name="ws_raw", align_bytes=64)
+        nc.sync.dma_start(ws_raw[:].bitcast(I32), ws_words.rearrange("a p c -> p a c").bitcast(I32))
+        load_table(1, slice(0, T // 4))
 
         picked_rows = keep.tile([P, S], U8, name="picked_rows", align_bytes=64)
-        staged = keep.tile([P, S + H], U8, name="staged", align_bytes=64)
+        staged = keep.tile([P, S + H + N], U8, name="staged", align_bytes=64)
         nc.vector.tensor_copy(picked_rows[:], tab_rows[:].indirect(offsets[:]))
         nc.vector.tensor_copy(
-            staged[:, S:].rearrange("p (t m) -> p t m", t=PACK), ws_rows[:].rearrange("p (m t) -> p t m", t=PACK)
+            staged[:, S : S + H].rearrange("p (t m) -> p t m", t=PACK), ws_rows[:].rearrange("p (m t) -> p t m", t=PACK)
         )
         nc.vector.tensor_copy(staged[:, :S].bitcast(I32), picked_rows[:].bitcast(I32))
+        nc.vector.tensor_copy(
+            staged[:, S + H :].rearrange("p (g t m) -> p g t m", g=GROUPS, t=PACK),
+            dc_rows[:].rearrange("p (g m t) -> p g t m", g=GROUPS, t=PACK),
+        )
         moves = [(a, q) for a in range(PASSES) for q in range(4)]
         for b in range(2):
             for a, q in moves[6 * b : 6 * b + 6]:
                 row = ROW_BASE[a] + 4 * q
-                nc.sync.dma_start(planes[a][32 * q : 32 * q + 4, :].bitcast(I32), staged[row : row + 4, :].bitcast(I32))
-            load_table(b + 1)
+                nc.sync.dma_start(
+                    planes[a][32 * q : 32 * q + 4, :].bitcast(I32), staged[row : row + 4, : widths[a]].bitcast(I32)
+                )
+            load_table(b + 1, slice(T // 4, T) if b == 0 else slice(0, T))
+        dc_plane = planes[PASSES - 1][:, S + H :]
 
         gs_sb = keep.tile([P, PACK], F32, name="gs_sb")
         gc_sb = keep.tile([P, PACK], F32, name="gc_sb")
@@ -107,20 +113,15 @@ def tile_list_tile_location_codes_kernel(
             )
 
         def load_weight(rows, name):
-            raw = keep.tile([P, PACK, P * PACK], F32, name=name, align_bytes=64)
+            raw = keep.tile([P, PACK, rows.shape[1]], F32, name=name, tag=name, align_bytes=64)
             nc.sync.dma_start(raw[:], rows.rearrange("(p j) c -> p j c", j=PACK))
             return raw
 
+        def grouped_tile():
+            return ring.tile([P, PACK, P, PACK], BF16, name="grouped", tag="grouped", bufs=3, align_bytes=64)
 
-        def round_weight(raw, on_scalar, tag="grouped"):
-            grouped = ring.tile([P, PACK, P, PACK], BF16, name="grouped", tag=tag, bufs=2 if tag == "grouped" else 1, align_bytes=64)
-            dst = grouped[:].rearrange("p t m j -> p m j t")
-            src = raw.rearrange("p j (m t) -> p m j t", t=PACK)
-            if on_scalar:
-                nc.scalar.copy(dst, src)
-            else:
-                nc.vector.tensor_copy(dst, src)
-            return grouped
+        def round_weight(engine_copy, grouped_part, raw):
+            engine_copy(grouped_part.rearrange("p t m j -> p m j t"), raw[:].rearrange("p j (m t) -> p m j t", t=PACK))
 
         def quantize(codes, scales, grouped_flat):
             nc.vector.quantize_mx(out=codes.bitcast(FP8X4), scales=scales, in_=grouped_flat)
@@ -155,25 +156,29 @@ def tile_list_tile_location_codes_kernel(
                         planes[a][:, S + P * t : S + P * (t + 1)], a, h,
                     )
 
-        wc_raw = [load_weight(wc[512 * a : 512 * (a + 1), :], "wc_raw%d" % a)[:] for a in range(2)]
-        for q in range(4):
-            nc.sync.dma_start(dc_plane_raw[32 * q : 32 * q + 4, :].bitcast(I32), dc_scales[0, 4 * q : 4 * q + 4, :].bitcast(I32))
-        wc_raw.append(load_weight(wc[1024:1536, :], "wc_raw2")[:])
+        wc_raw = [load_weight(wc[512 * a : 512 * (a + 1), :], "wc_raw%d" % a) for a in range(2)]
+        wc_last = [load_weight(wc[1024:1536, 256 * u : 256 * (u + 1)], "wc_last%d" % u) for u in range(2)]
+        ds_raw = [load_weight(ds[:, 0:512], "ds_raw0")]
+        dc_raw = keep.tile([P, N], I32, name="dc_raw", align_bytes=64)
+        nc.sync.dma_start(dc_raw[:], dc_words[0].rearrange("p c i -> p (c i)").bitcast(I32))
+        ds_raw.append(load_weight(ds[:, 512:1024], "ds_raw1"))
+
         wc_codes = [keep.tile([P, H], U32, name="wc_codes%d" % a, align_bytes=64) for a in range(PASSES)]
         wc_planes = [keep.tile([P, H], U8, name="wc_plane%d" % a, align_bytes=64) for a in range(PASSES)]
         hs_codes = [keep.tile([P, CHUNK], U32, name="hs_codes%d" % c, align_bytes=64) for c in range(chunks)]
         hs_planes = [keep.tile([P, CHUNK], U8, name="hs_plane%d" % c, align_bytes=64) for c in range(chunks)]
         hc_codes = [keep.tile([P, CHUNK], U32, name="hc_codes%d" % c, align_bytes=64) for c in range(chunks)]
         hc_planes = [keep.tile([P, CHUNK], U8, name="hc_plane%d" % c, align_bytes=64) for c in range(chunks)]
-        sines = [keep.tile([P, PACK, HALF], F32, name="sines%d" % h) for h in range(halves)]
+        sines = [keep.tile([P, PACK, HALF], F32, name="sines%d" % h, tag="table%d" % h, align_bytes=64) for h in range(halves)]
+        half_sines = [keep.tile([P, PACK, HALF], F32, name="half_sines%d" % h) for h in range(halves)]
 
         def sine_half(h):
             for t in range(PACK):
                 nc.scalar.activation(sines[h][:, t, :], sin_banks[h][t][:], ACT.Sin)
 
-        def hs_round(c):
+        def hs_round(c, tag):
             h, c0 = divmod(c * CHUNK, HALF)
-            feat = ring.tile([P, CHUNK, PACK], BF16, name="feat", tag="late", bufs=1, align_bytes=64)
+            feat = keep.tile([P, CHUNK, PACK], BF16, name="feat", tag=tag, align_bytes=64)
             nc.vector.tensor_tensor(
                 feat[:].rearrange("p (c i) t -> p c t i", i=2),
                 sines[h][:, :, c0 : c0 + CHUNK].rearrange("p t (c i) -> p c t i", i=2),
@@ -186,7 +191,7 @@ def tile_list_tile_location_codes_kernel(
             quantize(codes[:], plane[:], feat[:].rearrange("p n t -> p (n t)"))
 
         def quantize_weight(grouped, codes, plane):
-            quantize(codes, plane, grouped[:].rearrange("p t m j -> p (t m j)"))
+            quantize(codes[:], plane[:], grouped[:].rearrange("p t m j -> p (t m j)"))
 
         cos_banks = [[None] * PACK for h in range(halves)]
 
@@ -200,30 +205,35 @@ def tile_list_tile_location_codes_kernel(
                 )
 
         sine_half(0)
-        g0 = round_weight(wc_raw[0], False)
-        g1 = round_weight(wc_raw[1], False)
-        quantize_weight(g0, wc_codes[0][:], wc_planes[0][:])
         sine_half(1)
-        quantize_weight(g1, wc_codes[1][:], wc_planes[1][:])
-        g2 = round_weight(wc_raw[2], False, "late")
-        quantize_weight(g2, wc_codes[2][:], wc_planes[2][:])
-        for h in range(halves):
-            for a in range(PASSES):
-                cos_pass(a, h)
+        g0 = grouped_tile()
+        round_weight(nc.vector.tensor_copy, g0[:], wc_raw[0])
+        quantize_weight(g0, wc_codes[0], wc_planes[0])
+        g1 = grouped_tile()
+        round_weight(nc.vector.tensor_copy, g1[:], wc_raw[1])
+        g2 = grouped_tile()
+        round_weight(nc.vector.tensor_copy, g2[:, :, 0:64, :], wc_last[0])
+        round_weight(nc.scalar.copy, g2[:, :, 64:128, :], wc_last[1])
+        quantize_weight(g1, wc_codes[1], wc_planes[1])
+        f0 = hs_round(0, "wc_last0")
+        quantize_weight(g2, wc_codes[2], wc_planes[2])
+        quantize_feat(f0, hs_codes[0], hs_planes[0])
+        f1 = hs_round(1, "wc_last1")
+        for a, h in ((0, 0), (0, 1), (1, 0), (2, 0), (1, 1), (2, 1)):
+            cos_pass(a, h)
 
-        ds_raw = [load_weight(ds[:, 512 * g : 512 * (g + 1)], "ds_raw%d" % g) for g in range(GROUPS)]
-
-        def cos_chunk(c):
-            h, c0 = divmod(c * CHUNK, HALF)
-            half_sine = ring.tile([P, PACK, CHUNK], F32, name="half_sine", tag="half_sine", bufs=2)
+        def half_sine(h):
             for t in range(PACK):
                 nc.scalar.activation(
-                    half_sine[:, t, :], cos_banks[h][t][:, c0 : c0 + CHUNK], ACT.Sin, bias=half_phase[:, t : t + 1], scale=0.5
+                    half_sines[h][:, t, :], cos_banks[h][t][:], ACT.Sin, bias=half_phase[:, t : t + 1], scale=0.5
                 )
+
+        def square(c):
+            h, c0 = divmod(c * CHUNK, HALF)
             squared = ring.tile([P, CHUNK, PACK], F32, name="squared", tag="squared", bufs=2)
             nc.scalar.activation(
                 squared[:].rearrange("p (c i) t -> p c t i", i=4),
-                half_sine[:].rearrange("p t (c i) -> p c t i", i=4),
+                half_sines[h][:, :, c0 : c0 + CHUNK].rearrange("p t (c i) -> p c t i", i=4),
                 ACT.Square,
             )
             return squared
@@ -238,29 +248,23 @@ def tile_list_tile_location_codes_kernel(
         ds_codes = [keep.tile([P, 512], U32, name="ds_codes%d" % g, align_bytes=64) for g in range(GROUPS)]
         ds_plane = [keep.tile([P, 512], U8, name="ds_plane%d" % g, align_bytes=64) for g in range(GROUPS)]
         dc_codes = [keep.tile([P, 512], I32, name="dc_codes%d" % g, align_bytes=64) for g in range(GROUPS)]
-        dc_plane = keep.tile([P, GROUPS, 512], U8, name="dc_plane", align_bytes=64)
-        nc.vector.tensor_copy(
-            dc_plane[:].rearrange("p g (t m) -> p g t m", t=PACK), dc_plane_raw[:].rearrange("p (g m t) -> p g t m", g=GROUPS, t=PACK)
-        )
         y_codes = keep.tile([P, GROUPS, S], I32, name="y_codes", align_bytes=64)
         y_plane = keep.tile([P, GROUPS, S], U8, name="y_plane", align_bytes=64)
 
-        def second_weights(g):
+        def deal_dc(g):
             n_cols = slice(512 * g, 512 * (g + 1))
-            gd = round_weight(ds_raw[g][:], g == 1)
             nc.vector.tensor_copy(
                 dc_codes[g][:].rearrange("p (t m) -> p m t", t=PACK), dc_raw[:, n_cols].rearrange("p (m t) -> p m t", t=PACK)
             )
-            quantize_weight(gd, ds_codes[g][:], ds_plane[g][:])
 
         out_rows = out_0.rearrange("(g p t) j -> g p t j", g=GROUPS, t=PACK)
         out_words = out_1.rearrange("g p m t -> p g (m t)").bitcast(I32)
 
-        def second_stage(c, g):
+        def second_stage(c, g, banks):
             cols = slice(CHUNK * c, CHUNK * (c + 1))
             y = ring.tile([P, PACK, CHUNK], F32, name="y", tag="y", bufs=4)
             for pair in range(PACK // 2):
-                bank = psum.tile([P, 2, CHUNK], F32, name="bank", tag="banks%d" % (c == chunks - 1))
+                bank = psum.tile([P, 2, CHUNK], F32, name="bank", tag="banks%d" % banks)
                 for u in range(2):
                     n0 = P * (2 * pair + u)
                     nc.tensor.matmul_mx(
@@ -268,7 +272,8 @@ def tile_list_tile_location_codes_kernel(
                         rhs=hs_codes[c][:].bitcast(FP8X4), rhs_scale=hs_planes[c][:], start=True, stop=False,
                     )
                     nc.tensor.matmul_mx(
-                        out=bank[:, u, :], lhsT=dc_codes[g][:, n0 : n0 + P].bitcast(FP8X4), lhsT_scale=dc_plane[:, g, n0 : n0 + P],
+                        out=bank[:, u, :], lhsT=dc_codes[g][:, n0 : n0 + P].bitcast(FP8X4),
+                        lhsT_scale=dc_plane[:, 512 * g + n0 : 512 * g + n0 + P],
                         rhs=hc_codes[c][:].bitcast(FP8X4), rhs_scale=hc_planes[c][:], start=False, stop=True,
                     )
                 nc.scalar.copy(y[:, 2 * pair : 2 * pair + 2, :], bank[:])
@@ -282,27 +287,48 @@ def tile_list_tile_location_codes_kernel(
             )
             return yb
 
-        quantize_feat(hs_round(0), hs_codes[0], hs_planes[0])
-        sq = [cos_chunk(0)]
-        for c in range(chunks):
+        def y_quantize(c, g, yb):
             cols = slice(CHUNK * c, CHUNK * (c + 1))
-            fc = hc_round(sq[c])
-            if c == 0:
-                second_weights(0)
-            if c + 1 < chunks:
-                sq.append(cos_chunk(c + 1))
-            quantize_feat(fc, hc_codes[c], hc_planes[c])
-            if c == 0:
-                second_weights(1)
-            ys = [second_stage(c, g) for g in range(GROUPS)]
-            if c + 1 < chunks:
-                f = hs_round(c + 1)
-            ybs = [y_round(y) for y in ys]
-            if c + 1 < chunks:
-                quantize_feat(f, hs_codes[c + 1], hs_planes[c + 1])
-            for g in range(GROUPS):
-                quantize(y_codes[:, g, cols], y_plane[:, g, cols], ybs[g][:].rearrange("p n t -> p (n t)"))
-            nc.sync.dma_start(out_words[:, :, cols], y_codes[:, :, cols])
+            quantize(y_codes[:, g, cols], y_plane[:, g, cols], yb[:].rearrange("p n t -> p (n t)"))
+            nc.sync.dma_start(out_words[:, g, cols], y_codes[:, g, cols])
+
+        half_sine(0)
+        sq0 = square(0)
+        sq1 = square(1)
+        gd0 = grouped_tile()
+        round_weight(nc.vector.tensor_copy, gd0[:], ds_raw[0])
+        quantize_feat(f1, hs_codes[1], hs_planes[1])
+        f2 = hs_round(2, "ds_raw0")
+        quantize_weight(gd0, ds_codes[0], ds_plane[0])
+        quantize_feat(f2, hs_codes[2], hs_planes[2])
+        deal_dc(0)
+        fc = hc_round(sq0)
+        deal_dc(1)
+        quantize_feat(fc, hc_codes[0], hc_planes[0])
+        gd1 = grouped_tile()
+        round_weight(nc.vector.tensor_copy, gd1[:], ds_raw[1])
+        fc = hc_round(sq1)
+        quantize_weight(gd1, ds_codes[1], ds_plane[1])
+        quantize_feat(fc, hc_codes[1], hc_planes[1])
+        half_sine(1)
+        y00 = second_stage(0, 0, 0)
+        sq2 = square(2)
+        y10 = second_stage(1, 0, 0)
+        sq3 = square(3)
+        f3 = hs_round(3, "ds_raw1")
+        fc = hc_round(sq2)
+        quantize_feat(f3, hs_codes[3], hs_planes[3])
+        quantize_feat(fc, hc_codes[2], hc_planes[2])
+        yb = y_round(y00)
+        fc = hc_round(sq3)
+        y_quantize(0, 0, yb)
+        quantize_feat(fc, hc_codes[3], hc_planes[3])
+        pending = (1, 0, y_round(y10))
+        for c, g, banks in ((0, 1, 1), (1, 1, 1), (2, 0, 0), (2, 1, 0), (3, 0, 1), (3, 1, 1)):
+            yb = y_round(second_stage(c, g, banks))
+            y_quantize(*pending)
+            pending = (c, g, yb)
+        y_quantize(*pending)
 
         out_planes = out_2.rearrange("g q m -> q g m").bitcast(I32)
         for q in range(4):

@@ -1,3 +1,4 @@
+import math
 from contextlib import ExitStack
 
 import concourse.mybir as mybir
@@ -87,9 +88,9 @@ def tile_list_tile_location_codes_kernel(
         moves = [(a, q) for a in range(PASSES) for q in range(4)]
         for b in range(2):
             for a, q in moves[6 * b : 6 * b + 6]:
-                row = ROW_BASE[a] + 4 * q
                 nc.sync.dma_start(
-                    planes[a][32 * q : 32 * q + 4, :].bitcast(I32), staged[row : row + 4, : widths[a]].bitcast(I32)
+                    planes[a][q:P:32, :].bitcast(I32),
+                    staged[ROW_BASE[a] + q : ROW_BASE[a] + 16 : 4, : widths[a]].bitcast(I32),
                 )
             load_table(b + 1, slice(T // 4, T) if b == 0 else slice(0, T))
         dc_plane = planes[PASSES - 1][:, S + H :]
@@ -100,10 +101,6 @@ def tile_list_tile_location_codes_kernel(
         nc.sync.dma_start(gs_sb[:], gs.rearrange("(p t) -> p t", t=PACK))
         nc.sync.dma_start(phase_sb[:], phase.rearrange("(p t) -> p t", t=PACK))
         nc.sync.dma_start(gc_sb[:], gc.rearrange("(p t) -> p t", t=PACK))
-        half_phase = keep.tile([P, PACK], F32, name="half_phase")
-        minus_2gc = keep.tile([P, PACK], F32, name="minus_2gc")
-        nc.scalar.mul(half_phase[:], phase_sb[:], 0.5)
-        nc.scalar.mul(minus_2gc[:], gc_sb[:], -2.0)
 
         ws_codes = keep.tile([P, PASSES, 2 * H], U8, name="ws_codes", align_bytes=64)
         for a in range(PASSES):
@@ -121,7 +118,10 @@ def tile_list_tile_location_codes_kernel(
             return ring.tile([P, PACK, P, PACK], BF16, name="grouped", tag="grouped", bufs=3, align_bytes=64)
 
         def round_weight(engine_copy, grouped_part, raw):
-            engine_copy(grouped_part.rearrange("p t m j -> p m j t"), raw[:].rearrange("p j (m t) -> p m j t", t=PACK))
+            engine_copy(
+                grouped_part.rearrange("p (u e) m j -> p u m j e", e=2),
+                raw[:].rearrange("p j (m u e) -> p u m j e", u=2, e=2),
+            )
 
         def quantize(codes, scales, grouped_flat):
             nc.vector.quantize_mx(out=codes.bitcast(FP8X4), scales=scales, in_=grouped_flat)
@@ -225,23 +225,22 @@ def tile_list_tile_location_codes_kernel(
         def half_sine(h):
             for t in range(PACK):
                 nc.scalar.activation(
-                    half_sines[h][:, t, :], cos_banks[h][t][:], ACT.Sin, bias=half_phase[:, t : t + 1], scale=0.5
+                    half_sines[h][:, t, :], cos_banks[h][t][:], ACT.Abs, bias=phase_sb[:, t : t + 1]
                 )
 
         def square(c):
             h, c0 = divmod(c * CHUNK, HALF)
-            squared = ring.tile([P, CHUNK, PACK], F32, name="squared", tag="squared", bufs=2)
-            nc.scalar.activation(
-                squared[:].rearrange("p (c i) t -> p c t i", i=4),
-                half_sines[h][:, :, c0 : c0 + CHUNK].rearrange("p t (c i) -> p c t i", i=4),
-                ACT.Square,
-            )
+            squared = ring.tile([P, PACK, CHUNK], F32, name="squared", tag="squared", bufs=2)
+            nc.scalar.activation(squared[:], half_sines[h][:, :, c0 : c0 + CHUNK], ACT.Sin, bias=math.pi / 2, scale=-1.0)
             return squared
 
         def hc_round(squared):
             feat = ring.tile([P, CHUNK, PACK], BF16, name="feat", tag="feat", align_bytes=64)
-            nc.vector.scalar_tensor_tensor(
-                feat[:], squared[:], -0.5, minus_2gc[:].unsqueeze(1).to_broadcast([P, CHUNK, PACK]), ALU.add, ALU.mult
+            nc.vector.tensor_tensor(
+                feat[:].rearrange("p (c i) t -> p c t i", i=2),
+                squared[:].rearrange("p t (c i) -> p c t i", i=2),
+                gc_sb[:].unsqueeze(1).unsqueeze(3).to_broadcast([P, CHUNK // 2, PACK, 2]),
+                ALU.mult,
             )
             return feat
 
@@ -254,7 +253,8 @@ def tile_list_tile_location_codes_kernel(
         def deal_dc(g):
             n_cols = slice(512 * g, 512 * (g + 1))
             nc.vector.tensor_copy(
-                dc_codes[g][:].rearrange("p (t m) -> p m t", t=PACK), dc_raw[:, n_cols].rearrange("p (m t) -> p m t", t=PACK)
+                dc_codes[g][:].rearrange("p (u e m) -> p u m e", u=2, e=2),
+                dc_raw[:, n_cols].rearrange("p (m u e) -> p u m e", u=2, e=2),
             )
 
         out_rows = out_0.rearrange("(g p t) j -> g p t j", g=GROUPS, t=PACK)
@@ -330,6 +330,6 @@ def tile_list_tile_location_codes_kernel(
             pending = (c, g, yb)
         y_quantize(*pending)
 
-        out_planes = out_2.rearrange("g q m -> q g m").bitcast(I32)
-        for q in range(4):
-            nc.sync.dma_start(out_planes[4 * q : 4 * q + 4, :, :], y_plane[32 * q : 32 * q + 4, :, :].bitcast(I32))
+        out_planes = out_2.rearrange("g (q r) m -> r q g m", r=4).bitcast(I32)
+        for r in range(4):
+            nc.sync.dma_start(out_planes[r], y_plane[r:P:32, :, :].bitcast(I32))

@@ -120,7 +120,7 @@ def tile_list_tile_location_codes_kernel(
         def round_weight(engine_copy, grouped_part, raw):
             engine_copy(
                 grouped_part.rearrange("p (u e) m j -> p u m j e", e=2),
-                raw[:].rearrange("p j (m u e) -> p u m j e", u=2, e=2),
+                raw.rearrange("p j (m u e) -> p u m j e", u=2, e=2),
             )
 
         def quantize(codes, scales, grouped_flat):
@@ -156,8 +156,7 @@ def tile_list_tile_location_codes_kernel(
                         planes[a][:, S + P * t : S + P * (t + 1)], a, h,
                     )
 
-        wc_raw = [load_weight(wc[512 * a : 512 * (a + 1), :], "wc_raw%d" % a) for a in range(2)]
-        wc_last = [load_weight(wc[1024:1536, 256 * u : 256 * (u + 1)], "wc_last%d" % u) for u in range(2)]
+        wc_raw = [load_weight(wc[512 * a : 512 * (a + 1), :], "wc_raw%d" % a) for a in range(PASSES)]
         ds_raw = [load_weight(ds[:, 0:512], "ds_raw0")]
         dc_raw = keep.tile([P, N], I32, name="dc_raw", align_bytes=64)
         nc.sync.dma_start(dc_raw[:], dc_words[0].rearrange("p c i -> p (c i)").bitcast(I32))
@@ -165,30 +164,29 @@ def tile_list_tile_location_codes_kernel(
 
         wc_codes = [keep.tile([P, H], U32, name="wc_codes%d" % a, align_bytes=64) for a in range(PASSES)]
         wc_planes = [keep.tile([P, H], U8, name="wc_plane%d" % a, align_bytes=64) for a in range(PASSES)]
-        hs_codes = [keep.tile([P, CHUNK], U32, name="hs_codes%d" % c, align_bytes=64) for c in range(chunks)]
-        hs_planes = [keep.tile([P, CHUNK], U8, name="hs_plane%d" % c, align_bytes=64) for c in range(chunks)]
-        hc_codes = [keep.tile([P, CHUNK], U32, name="hc_codes%d" % c, align_bytes=64) for c in range(chunks)]
-        hc_planes = [keep.tile([P, CHUNK], U8, name="hc_plane%d" % c, align_bytes=64) for c in range(chunks)]
+        hs_codes = [keep.tile([P, HALF], U32, name="hs_codes%d" % h, align_bytes=64) for h in range(halves)]
+        hs_planes = [keep.tile([P, HALF], U8, name="hs_plane%d" % h, align_bytes=64) for h in range(halves)]
+        hc_codes = [keep.tile([P, HALF], U32, name="hc_codes%d" % h, align_bytes=64) for h in range(halves)]
+        hc_planes = [keep.tile([P, HALF], U8, name="hc_plane%d" % h, align_bytes=64) for h in range(halves)]
         sines = [keep.tile([P, PACK, HALF], F32, name="sines%d" % h, tag="table%d" % h, align_bytes=64) for h in range(halves)]
-        half_sines = [keep.tile([P, PACK, HALF], F32, name="half_sines%d" % h) for h in range(halves)]
 
         def sine_half(h):
             for t in range(PACK):
                 nc.scalar.activation(sines[h][:, t, :], sin_banks[h][t][:], ACT.Sin)
 
-        def hs_round(c, tag):
-            h, c0 = divmod(c * CHUNK, HALF)
-            feat = keep.tile([P, CHUNK, PACK], BF16, name="feat", tag=tag, align_bytes=64)
+        def apply_gain(values, gain, tag):
+            width = values.shape[2]
+            feat = keep.tile([P, width, PACK], BF16, name="feat", tag=tag, align_bytes=64)
             nc.vector.tensor_tensor(
                 feat[:].rearrange("p (c i) t -> p c t i", i=2),
-                sines[h][:, :, c0 : c0 + CHUNK].rearrange("p t (c i) -> p c t i", i=2),
-                gs_sb[:].unsqueeze(1).unsqueeze(3).to_broadcast([P, CHUNK // 2, PACK, 2]),
+                values.rearrange("p t (c i) -> p c t i", i=2),
+                gain[:].unsqueeze(1).unsqueeze(3).to_broadcast([P, width // 2, PACK, 2]),
                 ALU.mult,
             )
             return feat
 
         def quantize_feat(feat, codes, plane):
-            quantize(codes[:], plane[:], feat[:].rearrange("p n t -> p (n t)"))
+            quantize(codes, plane, feat[:].rearrange("p n t -> p (n t)"))
 
         def quantize_weight(grouped, codes, plane):
             quantize(codes[:], plane[:], grouped[:].rearrange("p t m j -> p (t m j)"))
@@ -206,43 +204,25 @@ def tile_list_tile_location_codes_kernel(
 
         sine_half(0)
         sine_half(1)
-        g0 = grouped_tile()
-        round_weight(nc.vector.tensor_copy, g0[:], wc_raw[0])
-        quantize_weight(g0, wc_codes[0], wc_planes[0])
-        g1 = grouped_tile()
-        round_weight(nc.vector.tensor_copy, g1[:], wc_raw[1])
-        g2 = grouped_tile()
-        round_weight(nc.vector.tensor_copy, g2[:, :, 0:64, :], wc_last[0])
-        round_weight(nc.scalar.copy, g2[:, :, 64:128, :], wc_last[1])
-        quantize_weight(g1, wc_codes[1], wc_planes[1])
-        f0 = hs_round(0, "wc_last0")
-        quantize_weight(g2, wc_codes[2], wc_planes[2])
-        quantize_feat(f0, hs_codes[0], hs_planes[0])
-        f1 = hs_round(1, "wc_last1")
+        grouped = [grouped_tile() for a in range(PASSES)]
+        for a in range(PASSES - 1):
+            round_weight(nc.vector.tensor_copy, grouped[a][:], wc_raw[a][:])
+            quantize_weight(grouped[a], wc_codes[a], wc_planes[a])
+        round_weight(nc.vector.tensor_copy, grouped[2][:, :, 0:64, :], wc_raw[2][:, :, 0:256])
+        round_weight(nc.scalar.copy, grouped[2][:, :, 64:128, :], wc_raw[2][:, :, 256:512])
+        quantize_weight(grouped[2], wc_codes[2], wc_planes[2])
         for a, h in ((0, 0), (0, 1), (1, 0), (2, 0), (1, 1), (2, 1)):
             cos_pass(a, h)
 
-        def half_sine(h):
+        def fold(folded, h, cols):
             for t in range(PACK):
-                nc.scalar.activation(
-                    half_sines[h][:, t, :], cos_banks[h][t][:], ACT.Abs, bias=phase_sb[:, t : t + 1]
-                )
+                nc.scalar.activation(folded[:, t, cols], cos_banks[h][t][:, cols], ACT.Abs, bias=phase_sb[:, t : t + 1])
 
-        def square(c):
-            h, c0 = divmod(c * CHUNK, HALF)
-            squared = ring.tile([P, PACK, CHUNK], F32, name="squared", tag="squared", bufs=2)
-            nc.scalar.activation(squared[:], half_sines[h][:, :, c0 : c0 + CHUNK], ACT.Sin, bias=math.pi / 2, scale=-1.0)
-            return squared
-
-        def hc_round(squared):
-            feat = ring.tile([P, CHUNK, PACK], BF16, name="feat", tag="feat", align_bytes=64)
-            nc.vector.tensor_tensor(
-                feat[:].rearrange("p (c i) t -> p c t i", i=2),
-                squared[:].rearrange("p t (c i) -> p c t i", i=2),
-                gc_sb[:].unsqueeze(1).unsqueeze(3).to_broadcast([P, CHUNK // 2, PACK, 2]),
-                ALU.mult,
-            )
-            return feat
+        def cosine(folded, cols, tag):
+            cosines = keep.tile([P, PACK, CHUNK], F32, name="cosines", tag=tag, align_bytes=64)
+            for pair in (slice(0, 2), slice(2, 4)):
+                nc.scalar.activation(cosines[:, pair, :], folded[:, pair, cols], ACT.Sin, bias=math.pi / 2, scale=-1.0)
+            return cosines
 
         ds_codes = [keep.tile([P, 512], U32, name="ds_codes%d" % g, align_bytes=64) for g in range(GROUPS)]
         ds_plane = [keep.tile([P, 512], U8, name="ds_plane%d" % g, align_bytes=64) for g in range(GROUPS)]
@@ -260,75 +240,95 @@ def tile_list_tile_location_codes_kernel(
         out_rows = out_0.rearrange("(g p t) j -> g p t j", g=GROUPS, t=PACK)
         out_words = out_1.rearrange("g p m t -> p g (m t)").bitcast(I32)
 
-        def second_stage(c, g, banks):
-            cols = slice(CHUNK * c, CHUNK * (c + 1))
-            y = ring.tile([P, PACK, CHUNK], F32, name="y", tag="y", bufs=4)
+        def product(out, g, t, h, cols):
+            n_cols = slice(P * t, P * (t + 1))
+            nc.tensor.matmul_mx(
+                out=out, lhsT=ds_codes[g][:, n_cols].bitcast(FP8X4), lhsT_scale=ds_plane[g][:, n_cols],
+                rhs=hs_codes[h][:, cols].bitcast(FP8X4), rhs_scale=hs_planes[h][:, cols], start=True, stop=False,
+            )
+            nc.tensor.matmul_mx(
+                out=out, lhsT=dc_codes[g][:, n_cols].bitcast(FP8X4), lhsT_scale=dc_plane[:, 512 * g + P * t : 512 * g + P * (t + 1)],
+                rhs=hc_codes[h][:, cols].bitcast(FP8X4), rhs_scale=hc_planes[h][:, cols], start=False, stop=True,
+            )
+
+        def narrow_unit(g, h, cols, banks, tag):
+            y = keep.tile([P, PACK, CHUNK], F32, name="y", tag=tag, align_bytes=64)
             for pair in range(PACK // 2):
-                bank = psum.tile([P, 2, CHUNK], F32, name="bank", tag="banks%d" % banks)
+                bank = psum.tile([P, 2, CHUNK], F32, name="bank", tag=banks)
                 for u in range(2):
-                    n0 = P * (2 * pair + u)
-                    nc.tensor.matmul_mx(
-                        out=bank[:, u, :], lhsT=ds_codes[g][:, n0 : n0 + P].bitcast(FP8X4), lhsT_scale=ds_plane[g][:, n0 : n0 + P],
-                        rhs=hs_codes[c][:].bitcast(FP8X4), rhs_scale=hs_planes[c][:], start=True, stop=False,
-                    )
-                    nc.tensor.matmul_mx(
-                        out=bank[:, u, :], lhsT=dc_codes[g][:, n0 : n0 + P].bitcast(FP8X4),
-                        lhsT_scale=dc_plane[:, 512 * g + n0 : 512 * g + n0 + P],
-                        rhs=hc_codes[c][:].bitcast(FP8X4), rhs_scale=hc_planes[c][:], start=False, stop=True,
-                    )
+                    product(bank[:, u, :], g, 2 * pair + u, h, cols)
                 nc.scalar.copy(y[:, 2 * pair : 2 * pair + 2, :], bank[:])
-            nc.sync.dma_start(out_rows[g, :, :, cols], y[:])
+            nc.sync.dma_start(out_rows[g, :, :, HALF * h + cols.start : HALF * h + cols.stop], y[:])
             return y
 
-        def y_round(y):
-            yb = ring.tile([P, CHUNK, PACK], BF16, name="yb", tag="yb", align_bytes=64)
-            nc.vector.tensor_copy(
-                yb[:].rearrange("p (c i) t -> p c t i", i=4), y[:].rearrange("p t (c i) -> p c t i", i=4)
-            )
-            return yb
+        def y_round(engine_copy, yb, y):
+            engine_copy(yb.rearrange("p (c i) t -> p c t i", i=4), y[:].rearrange("p t (c i) -> p c t i", i=4))
 
-        def y_quantize(c, g, yb):
-            cols = slice(CHUNK * c, CHUNK * (c + 1))
+        def y_tile():
+            return ring.tile([P, HALF, PACK], BF16, name="yb", tag="yb", bufs=4, align_bytes=64)
+
+        def y_quantize(g, h, yb):
+            cols = slice(HALF * h, HALF * (h + 1))
             quantize(y_codes[:, g, cols], y_plane[:, g, cols], yb[:].rearrange("p n t -> p (n t)"))
             nc.sync.dma_start(out_words[:, g, cols], y_codes[:, g, cols])
 
-        half_sine(0)
-        sq0 = square(0)
-        sq1 = square(1)
+        first, second = slice(0, CHUNK), slice(CHUNK, HALF)
+
+        def quantize_both(fs, fc, h, cols):
+            quantize_feat(fs, hs_codes[h][:, cols], hs_planes[h][:, cols])
+            quantize_feat(fc, hc_codes[h][:, cols], hc_planes[h][:, cols])
+
+        folded0 = keep.tile([P, PACK, HALF], F32, name="folded0", align_bytes=64)
+        fold(folded0, 0, first)
+        cos0 = cosine(folded0, first, "cos0")
+        fold(folded0, 0, second)
+        cos1 = cosine(folded0, second, "cos1")
+        fs = apply_gain(sines[0][:, :, first], gs_sb, "wc_raw2")
         gd0 = grouped_tile()
-        round_weight(nc.vector.tensor_copy, gd0[:], ds_raw[0])
-        quantize_feat(f1, hs_codes[1], hs_planes[1])
-        f2 = hs_round(2, "ds_raw0")
+        round_weight(nc.vector.tensor_copy, gd0[:], ds_raw[0][:])
+        quantize_feat(fs, hs_codes[0][:, first], hs_planes[0][:, first])
         quantize_weight(gd0, ds_codes[0], ds_plane[0])
-        quantize_feat(f2, hs_codes[2], hs_planes[2])
+        fc = apply_gain(cos0[:], gc_sb, "feat0")
         deal_dc(0)
-        fc = hc_round(sq0)
-        deal_dc(1)
-        quantize_feat(fc, hc_codes[0], hc_planes[0])
+        quantize_feat(fc, hc_codes[0][:, first], hc_planes[0][:, first])
+        y00 = narrow_unit(0, 0, first, "banks0", "y0")
+        fs = apply_gain(sines[0][:, :, second], gs_sb, "cos0")
+        fc = apply_gain(cos1[:], gc_sb, "feat1")
+        quantize_both(fs, fc, 0, second)
+        folded1 = keep.tile([P, PACK, HALF], F32, name="folded1", tag="feat0", align_bytes=64)
+        fold(folded1, 1, slice(0, HALF))
+        y10 = narrow_unit(0, 0, second, "banks0", "y1")
         gd1 = grouped_tile()
-        round_weight(nc.vector.tensor_copy, gd1[:], ds_raw[1])
-        fc = hc_round(sq1)
+        round_weight(nc.vector.tensor_copy, gd1[:], ds_raw[1][:])
+        deal_dc(1)
         quantize_weight(gd1, ds_codes[1], ds_plane[1])
-        quantize_feat(fc, hc_codes[1], hc_planes[1])
-        half_sine(1)
-        y00 = second_stage(0, 0, 0)
-        sq2 = square(2)
-        y10 = second_stage(1, 0, 0)
-        sq3 = square(3)
-        f3 = hs_round(3, "ds_raw1")
-        fc = hc_round(sq2)
-        quantize_feat(f3, hs_codes[3], hs_planes[3])
-        quantize_feat(fc, hc_codes[2], hc_planes[2])
-        yb = y_round(y00)
-        fc = hc_round(sq3)
-        y_quantize(0, 0, yb)
-        quantize_feat(fc, hc_codes[3], hc_planes[3])
-        pending = (1, 0, y_round(y10))
-        for c, g, banks in ((0, 1, 1), (1, 1, 1), (2, 0, 0), (2, 1, 0), (3, 0, 1), (3, 1, 1)):
-            yb = y_round(second_stage(c, g, banks))
-            y_quantize(*pending)
-            pending = (c, g, yb)
-        y_quantize(*pending)
+        cos2 = cosine(folded1, first, "cos2")
+        y01 = narrow_unit(1, 0, first, "banks0", "wc_raw0")
+        cos3 = cosine(folded1, second, "cos3")
+        y11 = narrow_unit(1, 0, second, "banks0", "wc_raw1")
+        fs = apply_gain(sines[1][:, :, first], gs_sb, "ds_raw1")
+        fc = apply_gain(cos2[:], gc_sb, "feat1")
+        quantize_both(fs, fc, 1, first)
+        y20 = narrow_unit(0, 1, first, "banks1", "table2")
+        y21 = narrow_unit(1, 1, first, "banks1", "tab_rows")
+        fs = apply_gain(sines[1][:, :, second], gs_sb, "cos2")
+        fc = apply_gain(cos3[:], gc_sb, "feat2")
+        quantize_both(fs, fc, 1, second)
+        y30 = narrow_unit(0, 1, second, "banks0", "dc_raw")
+        y31 = narrow_unit(1, 1, second, "banks0", "ds_raw0")
+        ybs = [y_tile() for u in range(4)]
+        y_round(nc.vector.tensor_copy, ybs[0][:, first, :], y00)
+        y_round(nc.vector.tensor_copy, ybs[0][:, second, :], y10)
+        y_round(nc.vector.tensor_copy, ybs[1][:, first, :], y01)
+        y_quantize(0, 0, ybs[0])
+        y_round(nc.vector.tensor_copy, ybs[1][:, second, :], y11)
+        y_round(nc.vector.tensor_copy, ybs[2][:, first, :], y20)
+        y_quantize(1, 0, ybs[1])
+        y_round(nc.vector.tensor_copy, ybs[3][:, first, :], y21)
+        y_round(nc.scalar.copy, ybs[2][:, second, :], y30)
+        y_round(nc.scalar.copy, ybs[3][:, second, :], y31)
+        y_quantize(0, 1, ybs[2])
+        y_quantize(1, 1, ybs[3])
 
         out_planes = out_2.rearrange("g (q r) m -> r q g m", r=4).bitcast(I32)
         for r in range(4):

@@ -19,11 +19,19 @@ ALU = mybir.AluOpType
 
 P = 128
 PACK = 4
-PASSES = K // (P * PACK)
-GROUPS = N // (P * PACK)
+SPAN = P * PACK
+BLOCKS = SPAN // 32
+QUAD = 32
+PASSES = K // SPAN
+GROUPS = N // SPAN
 HALF = 512
 CHUNK = 256
-ROW_BASE = (80, 96, 112)
+HALVES = S // HALF
+CHUNKS = S // CHUNK
+STAGE_BASE = P - PASSES * BLOCKS
+MOVES_PER_RUN = 6
+TABLE_LEAD = T // 4
+VECTOR_SHARE = 80
 
 
 def tile_list_tile_location_codes_kernel(
@@ -31,13 +39,11 @@ def tile_list_tile_location_codes_kernel(
     out_0, out_1, out_2,
 ):
     nc = tc.nc
-    halves = S // HALF
-    chunks = S // CHUNK
+    first, second, whole = slice(0, CHUNK), slice(CHUNK, HALF), slice(0, HALF)
 
     with ExitStack() as ctx:
         keep = ctx.enter_context(tc.tile_pool(name="keep", bufs=1))
-        ring = ctx.enter_context(tc.tile_pool(name="ring", bufs=3))
-        psum = ctx.enter_context(tc.psum_pool(name="psum", bufs=4))
+        psum = ctx.enter_context(tc.psum_pool(name="psum", bufs=PACK))
 
         offsets = keep.tile([P, S // 16], U16, name="offsets")
         nc.sync.dma_start(offsets[:], offs)
@@ -47,22 +53,17 @@ def tile_list_tile_location_codes_kernel(
         tab_rows = keep.tile([P, T], U8, name="tab_rows", align_bytes=64)
         ws_rows = keep.tile([P, H], U8, name="ws_rows", align_bytes=64)
         dc_rows = keep.tile([P, N], U8, name="dc_rows", align_bytes=64)
-        widths = [S + H, S + H, S + H + N]
+        widths = [S + H] * (PASSES - 1) + [S + H + N]
         planes = [keep.tile([P, widths[a]], U8, name="plane%d" % a, align_bytes=64) for a in range(PASSES)]
-        warm = keep.tile([P, 8], F32, name="warm")
-        warm_out = keep.tile([P, 8], F32, name="warm_out")
         for rows, flat in ((tab_rows, tab_flat), (ws_rows, ws_flat)):
-            nc.sync.dma_start(rows[96:128, :].bitcast(I32), flat[16:48, :])
-            nc.sync.dma_start(rows[80:96, :].bitcast(I32), flat[0:16, :])
-        nc.sync.dma_start(dc_rows[112:128, :].bitcast(I32), dc_scales[0].bitcast(I32))
-        nc.vector.memset(warm[:], 0.0)
+            nc.sync.dma_start(rows[STAGE_BASE + BLOCKS :, :].bitcast(I32), flat[BLOCKS:, :])
+            nc.sync.dma_start(rows[STAGE_BASE : STAGE_BASE + BLOCKS, :].bitcast(I32), flat[:BLOCKS, :])
+        nc.sync.dma_start(dc_rows[P - BLOCKS :, :].bitcast(I32), dc_scales[0].bitcast(I32))
         for rows in (tab_rows, ws_rows):
-            nc.vector.memset(rows[0:80, :].bitcast(I32), 0)
-        nc.vector.memset(dc_rows[0:112, :].bitcast(I32), 0)
-        for a in range(PASSES):
-            nc.vector.memset(planes[a][:].bitcast(I32), 0)
-
-        nc.scalar.activation(warm_out[:], warm[:], ACT.Sin)
+            nc.vector.memset(rows[:STAGE_BASE, :].bitcast(I32), 0)
+        nc.vector.memset(dc_rows[: P - BLOCKS, :].bitcast(I32), 0)
+        for plane in planes:
+            nc.vector.memset(plane[:].bitcast(I32), 0)
 
         table = [keep.tile([P, T], I32, name="table%d" % a, tag="table%d" % a, align_bytes=64) for a in range(PASSES)]
 
@@ -72,7 +73,7 @@ def tile_list_tile_location_codes_kernel(
         load_table(0, slice(0, T))
         ws_raw = keep.tile([P, PASSES, 2 * H], U8, name="ws_raw", align_bytes=64)
         nc.sync.dma_start(ws_raw[:].bitcast(I32), ws_words.rearrange("a p c -> p a c").bitcast(I32))
-        load_table(1, slice(0, T // 4))
+        load_table(1, slice(0, TABLE_LEAD))
 
         picked_rows = keep.tile([P, S], U8, name="picked_rows", align_bytes=64)
         staged = keep.tile([P, S + H + N], U8, name="staged", align_bytes=64)
@@ -85,14 +86,14 @@ def tile_list_tile_location_codes_kernel(
             staged[:, S + H :].rearrange("p (g t m) -> p g t m", g=GROUPS, t=PACK),
             dc_rows[:].rearrange("p (g m t) -> p g t m", g=GROUPS, t=PACK),
         )
-        moves = [(a, q) for a in range(PASSES) for q in range(4)]
-        for b in range(2):
-            for a, q in moves[6 * b : 6 * b + 6]:
+        moves = [(a, r) for a in range(PASSES) for r in range(4)]
+        for run, rest in enumerate((slice(TABLE_LEAD, T), slice(0, T))):
+            for a, r in moves[MOVES_PER_RUN * run : MOVES_PER_RUN * (run + 1)]:
+                base = STAGE_BASE + BLOCKS * a
                 nc.sync.dma_start(
-                    planes[a][q:P:32, :].bitcast(I32),
-                    staged[ROW_BASE[a] + q : ROW_BASE[a] + 16 : 4, : widths[a]].bitcast(I32),
+                    planes[a][r:P:QUAD, :].bitcast(I32), staged[base + r : base + BLOCKS : 4, : widths[a]].bitcast(I32)
                 )
-            load_table(b + 1, slice(T // 4, T) if b == 0 else slice(0, T))
+            load_table(run + 1, rest)
         dc_plane = planes[PASSES - 1][:, S + H :]
 
         gs_sb = keep.tile([P, PACK], F32, name="gs_sb")
@@ -109,23 +110,6 @@ def tile_list_tile_location_codes_kernel(
                 ws_raw[:, a, :].bitcast(U16).rearrange("p (m t) -> p t m", t=PACK),
             )
 
-        def load_weight(rows, name):
-            raw = keep.tile([P, PACK, rows.shape[1]], F32, name=name, tag=name, align_bytes=64)
-            nc.sync.dma_start(raw[:], rows.rearrange("(p j) c -> p j c", j=PACK))
-            return raw
-
-        def grouped_tile():
-            return ring.tile([P, PACK, P, PACK], BF16, name="grouped", tag="grouped", bufs=3, align_bytes=64)
-
-        def round_weight(engine_copy, grouped_part, raw):
-            engine_copy(
-                grouped_part.rearrange("p (u e) m j -> p u m j e", e=2),
-                raw.rearrange("p j (m u e) -> p u m j e", u=2, e=2),
-            )
-
-        def quantize(codes, scales, grouped_flat):
-            nc.vector.quantize_mx(out=codes.bitcast(FP8X4), scales=scales, in_=grouped_flat)
-
         picked = []
 
         def gather_words(a):
@@ -133,203 +117,235 @@ def tile_list_tile_location_codes_kernel(
             if a + 1 < PASSES:
                 both = keep.tile([P, S], U32, name="picked%d" % a, align_bytes=64)
                 nc.vector.tensor_copy(both[:], window.indirect(offsets[:]))
-                return [both[:, HALF * h : HALF * (h + 1)] for h in range(halves)]
-            parts = [keep.tile([P, HALF], U32, name="picked_last%d" % h, align_bytes=64) for h in range(halves)]
-            for h in range(halves):
-                nc.vector.tensor_copy(parts[h][:], window.indirect(offsets[:, 32 * h : 32 * (h + 1)]))
+                return [both[:, HALF * h : HALF * (h + 1)] for h in range(HALVES)]
+            parts = [keep.tile([P, HALF], U32, name="picked_last%d" % h, align_bytes=64) for h in range(HALVES)]
+            for h in range(HALVES):
+                nc.vector.tensor_copy(parts[h][:], window.indirect(offsets[:, HALF // 16 * h : HALF // 16 * (h + 1)]))
             return [part[:] for part in parts]
 
-        def first_pass(bank, lhsT, lhsT_scale, a, h):
+        def angle_pass(bank, lhsT, lhsT_scale, a, h, last):
             nc.tensor.matmul_mx(
                 out=bank[:], lhsT=lhsT, lhsT_scale=lhsT_scale,
                 rhs=picked[a][h].bitcast(FP8X4), rhs_scale=planes[a][:, HALF * h : HALF * (h + 1)],
-                start=(a == 0), stop=(a == PASSES - 1),
+                start=(a == 0), stop=(a == last),
             )
 
-        sin_banks = [[psum.tile([P, HALF], F32, name="bank", tag="banks%d" % h) for t in range(PACK)] for h in range(halves)]
+        sin_banks = [[psum.tile([P, HALF], F32, name="bank", tag="banks%d" % h) for t in range(PACK)] for h in range(HALVES)]
         for a in range(PASSES):
             picked.append(gather_words(a))
-            for h in range(halves):
+            for h in range(HALVES):
                 for t in range(PACK):
-                    first_pass(
+                    angle_pass(
                         sin_banks[h][t], ws_codes[:, a, 2 * P * t : 2 * P * (t + 1)].bitcast(FP4X4),
-                        planes[a][:, S + P * t : S + P * (t + 1)], a, h,
+                        planes[a][:, S + P * t : S + P * (t + 1)], a, h, PASSES - 1,
                     )
 
-        wc_raw = [load_weight(wc[512 * a : 512 * (a + 1), :], "wc_raw%d" % a) for a in range(PASSES)]
-        ds_raw = [load_weight(ds[:, 0:512], "ds_raw0")]
+        def load_weight(rows, name):
+            raw = keep.tile([P, PACK, SPAN], F32, name=name, tag=name, align_bytes=64)
+            nc.sync.dma_start(raw[:], rows.rearrange("(p j) c -> p j c", j=PACK))
+            return raw
+
+        wc_raw = [load_weight(wc[SPAN * a : SPAN * (a + 1), :], "wc_raw%d" % a) for a in range(PASSES)]
+        ds_raw = [load_weight(ds[:, :SPAN], "ds_raw0")]
         dc_raw = keep.tile([P, N], I32, name="dc_raw", align_bytes=64)
         nc.sync.dma_start(dc_raw[:], dc_words[0].rearrange("p c i -> p (c i)").bitcast(I32))
-        ds_raw.append(load_weight(ds[:, 512:1024], "ds_raw1"))
+        ds_raw.append(load_weight(ds[:, SPAN:], "ds_raw1"))
 
         wc_codes = [keep.tile([P, H], U32, name="wc_codes%d" % a, align_bytes=64) for a in range(PASSES)]
         wc_planes = [keep.tile([P, H], U8, name="wc_plane%d" % a, align_bytes=64) for a in range(PASSES)]
-        hs_codes = [keep.tile([P, HALF], U32, name="hs_codes%d" % h, align_bytes=64) for h in range(halves)]
-        hs_planes = [keep.tile([P, HALF], U8, name="hs_plane%d" % h, align_bytes=64) for h in range(halves)]
-        hc_codes = [keep.tile([P, HALF], U32, name="hc_codes%d" % h, align_bytes=64) for h in range(halves)]
-        hc_planes = [keep.tile([P, HALF], U8, name="hc_plane%d" % h, align_bytes=64) for h in range(halves)]
-        sines = [keep.tile([P, PACK, HALF], F32, name="sines%d" % h, tag="table%d" % h, align_bytes=64) for h in range(halves)]
+        h_codes = [keep.tile([P, 2 * CHUNK], U32, name="h_codes%d" % c, align_bytes=64) for c in range(CHUNKS)]
+        h_planes = [keep.tile([P, 2 * CHUNK], U8, name="h_plane%d" % c, align_bytes=64) for c in range(CHUNKS)]
+        sines = [keep.tile([P, PACK, HALF], F32, name="sines%d" % h, tag="table%d" % h, align_bytes=64) for h in range(HALVES)]
 
-        def sine_half(h):
+        def quantize(codes, plane, values):
+            nc.vector.quantize_mx(out=codes.bitcast(FP8X4), scales=plane, in_=values)
+
+        def dealt_tile(tag):
+            return keep.tile([P, PACK, P, PACK], BF16, name="dealt", tag=tag, align_bytes=64)
+
+        def round_weight(engine_copy, dealt, raw):
+            engine_copy(
+                dealt.rearrange("p (u e) m j -> p u m j e", e=2),
+                raw.rearrange("p j (m u e) -> p u m j e", u=2, e=2),
+            )
+
+        def quantize_weight(dealt, codes, plane):
+            quantize(codes[:], plane[:], dealt[:].rearrange("p t m j -> p (t m j)"))
+
+        def feat_tile(width, tag):
+            return keep.tile([P, width, PACK], BF16, name="feat", tag=tag, align_bytes=64)
+
+        def apply_gain(feat, values, gain):
+            nc.vector.tensor_tensor(
+                feat.rearrange("p (c i) t -> p c t i", i=2),
+                values.rearrange("p t (c i) -> p c t i", i=2),
+                gain[:].unsqueeze(1).unsqueeze(3).to_broadcast([P, CHUNK // 2, PACK, 2]),
+                ALU.mult,
+            )
+
+        def quantize_feat(feat, c, cols):
+            quantize(h_codes[c][:, cols], h_planes[c][:, cols], feat.rearrange("p n t -> p (n t)"))
+
+        for h in range(HALVES):
             for t in range(PACK):
                 nc.scalar.activation(sines[h][:, t, :], sin_banks[h][t][:], ACT.Sin)
 
-        def apply_gain(values, gain, tag):
-            width = values.shape[2]
-            feat = keep.tile([P, width, PACK], BF16, name="feat", tag=tag, align_bytes=64)
-            nc.vector.tensor_tensor(
-                feat[:].rearrange("p (c i) t -> p c t i", i=2),
-                values.rearrange("p t (c i) -> p c t i", i=2),
-                gain[:].unsqueeze(1).unsqueeze(3).to_broadcast([P, width // 2, PACK, 2]),
-                ALU.mult,
-            )
-            return feat
+        wc_dealt = [dealt_tile(tag) for tag in ("wc_dealt0", "wc_dealt1", "lead")]
+        for a in range(PASSES - 1):
+            round_weight(nc.vector.tensor_copy, wc_dealt[a][:], wc_raw[a][:])
+            quantize_weight(wc_dealt[a], wc_codes[a], wc_planes[a])
+        round_weight(nc.vector.tensor_copy, wc_dealt[-1][:, :, :VECTOR_SHARE, :], wc_raw[-1][:, :, : PACK * VECTOR_SHARE])
+        round_weight(nc.scalar.copy, wc_dealt[-1][:, :, VECTOR_SHARE:, :], wc_raw[-1][:, :, PACK * VECTOR_SHARE :])
+        quantize_weight(wc_dealt[-1], wc_codes[-1], wc_planes[-1])
 
-        def quantize_feat(feat, codes, plane):
-            quantize(codes, plane, feat[:].rearrange("p n t -> p (n t)"))
+        cos_banks = [[None] * PACK for h in range(HALVES)]
 
-        def quantize_weight(grouped, codes, plane):
-            quantize(codes[:], plane[:], grouped[:].rearrange("p t m j -> p (t m j)"))
-
-        cos_banks = [[None] * PACK for h in range(halves)]
-
-        def cos_pass(a, h):
+        def cos_pass(a, h, last):
             for t in range(PACK):
                 if a == 0:
                     cos_banks[h][t] = psum.tile([P, HALF], F32, name="bank", tag="banks%d" % h)
-                first_pass(
+                angle_pass(
                     cos_banks[h][t], wc_codes[a][:, P * t : P * (t + 1)].bitcast(FP8X4),
-                    wc_planes[a][:, P * t : P * (t + 1)], a, h,
+                    wc_planes[a][:, P * t : P * (t + 1)], a, h, last,
                 )
 
-        sine_half(0)
-        sine_half(1)
-        grouped = [grouped_tile() for a in range(PASSES)]
-        for a in range(PASSES - 1):
-            round_weight(nc.vector.tensor_copy, grouped[a][:], wc_raw[a][:])
-            quantize_weight(grouped[a], wc_codes[a], wc_planes[a])
-        round_weight(nc.vector.tensor_copy, grouped[2][:, :, 0:64, :], wc_raw[2][:, :, 0:256])
-        round_weight(nc.scalar.copy, grouped[2][:, :, 64:128, :], wc_raw[2][:, :, 256:512])
-        quantize_weight(grouped[2], wc_codes[2], wc_planes[2])
-        for a, h in ((0, 0), (0, 1), (1, 0), (2, 0), (1, 1), (2, 1)):
-            cos_pass(a, h)
+        for h in range(HALVES):
+            cos_pass(0, h, None)
+        for a in (1, 2):
+            cos_pass(a, 0, 2)
+        for a in (2, 1):
+            cos_pass(a, 1, 1)
 
         def fold(folded, h, cols):
             for t in range(PACK):
                 nc.scalar.activation(folded[:, t, cols], cos_banks[h][t][:, cols], ACT.Abs, bias=phase_sb[:, t : t + 1])
 
-        def cosine(folded, cols, tag):
+        def cosine(folded, cols, tag, row_runs):
             cosines = keep.tile([P, PACK, CHUNK], F32, name="cosines", tag=tag, align_bytes=64)
-            for pair in (slice(0, 2), slice(2, 4)):
-                nc.scalar.activation(cosines[:, pair, :], folded[:, pair, cols], ACT.Sin, bias=math.pi / 2, scale=-1.0)
+            for rows in row_runs:
+                nc.scalar.activation(cosines[:, rows, :], folded[:, rows, cols], ACT.Sin, bias=math.pi / 2, scale=-1.0)
             return cosines
 
-        ds_codes = [keep.tile([P, 512], U32, name="ds_codes%d" % g, align_bytes=64) for g in range(GROUPS)]
-        ds_plane = [keep.tile([P, 512], U8, name="ds_plane%d" % g, align_bytes=64) for g in range(GROUPS)]
-        dc_codes = [keep.tile([P, 512], I32, name="dc_codes%d" % g, align_bytes=64) for g in range(GROUPS)]
+        def features(c, cosines, tag):
+            h, part = divmod(c, HALF // CHUNK)
+            feat = feat_tile(2 * CHUNK, tag)
+            apply_gain(feat[:, first, :], sines[h][:, :, (first, second)[part]], gs_sb)
+            apply_gain(feat[:, second, :], cosines[:], gc_sb)
+            for cols in (first, second):
+                quantize_feat(feat[:, cols, :], c, cols)
+
+        ds_codes = [keep.tile([P, SPAN], U32, name="ds_codes%d" % g, align_bytes=64) for g in range(GROUPS)]
+        ds_planes = [keep.tile([P, SPAN], U8, name="ds_plane%d" % g, align_bytes=64) for g in range(GROUPS)]
+        dc_codes = []
         y_codes = keep.tile([P, GROUPS, S], I32, name="y_codes", align_bytes=64)
         y_plane = keep.tile([P, GROUPS, S], U8, name="y_plane", align_bytes=64)
 
-        def deal_dc(g):
-            n_cols = slice(512 * g, 512 * (g + 1))
+        def deal_dc(g, tag):
+            dc_codes.append(keep.tile([P, SPAN], I32, name="dc_codes%d" % g, tag=tag, align_bytes=64))
             nc.vector.tensor_copy(
                 dc_codes[g][:].rearrange("p (u e m) -> p u m e", u=2, e=2),
-                dc_raw[:, n_cols].rearrange("p (m u e) -> p u m e", u=2, e=2),
+                dc_raw[:, SPAN * g : SPAN * (g + 1)].rearrange("p (m u e) -> p u m e", u=2, e=2),
             )
 
         out_rows = out_0.rearrange("(g p t) j -> g p t j", g=GROUPS, t=PACK)
         out_words = out_1.rearrange("g p m t -> p g (m t)").bitcast(I32)
+        out_planes = out_2.rearrange("g (q r) m -> r q g m", r=4).bitcast(I32)
 
-        def product(out, g, t, h, cols):
-            n_cols = slice(P * t, P * (t + 1))
+        def product(out, g, t, c):
+            places = slice(P * t, P * (t + 1))
             nc.tensor.matmul_mx(
-                out=out, lhsT=ds_codes[g][:, n_cols].bitcast(FP8X4), lhsT_scale=ds_plane[g][:, n_cols],
-                rhs=hs_codes[h][:, cols].bitcast(FP8X4), rhs_scale=hs_planes[h][:, cols], start=True, stop=False,
+                out=out, lhsT=ds_codes[g][:, places].bitcast(FP8X4), lhsT_scale=ds_planes[g][:, places],
+                rhs=h_codes[c][:, first].bitcast(FP8X4), rhs_scale=h_planes[c][:, first], start=True, stop=False,
             )
             nc.tensor.matmul_mx(
-                out=out, lhsT=dc_codes[g][:, n_cols].bitcast(FP8X4), lhsT_scale=dc_plane[:, 512 * g + P * t : 512 * g + P * (t + 1)],
-                rhs=hc_codes[h][:, cols].bitcast(FP8X4), rhs_scale=hc_planes[h][:, cols], start=False, stop=True,
+                out=out, lhsT=dc_codes[g][:, places].bitcast(FP8X4),
+                lhsT_scale=dc_plane[:, SPAN * g + P * t : SPAN * g + P * (t + 1)],
+                rhs=h_codes[c][:, second].bitcast(FP8X4), rhs_scale=h_planes[c][:, second], start=False, stop=True,
             )
 
-        def narrow_unit(g, h, cols, banks, tag):
+        def unit(c, g, banks, tag):
             y = keep.tile([P, PACK, CHUNK], F32, name="y", tag=tag, align_bytes=64)
             for pair in range(PACK // 2):
                 bank = psum.tile([P, 2, CHUNK], F32, name="bank", tag=banks)
                 for u in range(2):
-                    product(bank[:, u, :], g, 2 * pair + u, h, cols)
+                    product(bank[:, u, :], g, 2 * pair + u, c)
                 nc.scalar.copy(y[:, 2 * pair : 2 * pair + 2, :], bank[:])
-            nc.sync.dma_start(out_rows[g, :, :, HALF * h + cols.start : HALF * h + cols.stop], y[:])
+            nc.sync.dma_start(out_rows[g, :, :, CHUNK * c : CHUNK * (c + 1)], y[:])
             return y
 
-        def y_round(engine_copy, yb, y):
-            engine_copy(yb.rearrange("p (c i) t -> p c t i", i=4), y[:].rearrange("p t (c i) -> p c t i", i=4))
+        all_rows = (slice(0, PACK),)
+        folded = keep.tile([P, PACK, HALF], F32, name="folded0", align_bytes=64)
+        fold(folded, 0, first)
+        cos0 = cosine(folded, first, "cos0", (slice(0, 2), slice(2, PACK)))
+        fold(folded, 0, second)
+        cos1 = cosine(folded, second, "cos1", all_rows)
+        hs0 = feat_tile(CHUNK, "wc_raw2")
+        apply_gain(hs0[:], sines[0][:, :, first], gs_sb)
+        ds_dealt = dealt_tile("lead")
+        round_weight(nc.vector.tensor_copy, ds_dealt[:], ds_raw[0][:])
+        quantize_feat(hs0[:], 0, first)
+        quantize_weight(ds_dealt, ds_codes[0], ds_planes[0])
+        deal_dc(0, "wc_raw2")
+        hc0 = feat_tile(CHUNK, "lead")
+        apply_gain(hc0[:], cos0[:], gc_sb)
+        quantize_feat(hc0[:], 0, second)
+        ys = {}
+        ys[0, 0] = unit(0, 0, "banks0", "y0")
 
-        def y_tile():
-            return ring.tile([P, HALF, PACK], BF16, name="yb", tag="yb", bufs=4, align_bytes=64)
+        features(1, cos1, "cos0")
+        folded = keep.tile([P, PACK, HALF], F32, name="folded1", tag="lead", align_bytes=64)
+        fold(folded, 1, whole)
+        ys[1, 0] = unit(1, 0, "banks0", "y1")
+        ds_dealt = dealt_tile("cos1")
+        round_weight(nc.vector.tensor_copy, ds_dealt[:], ds_raw[1][:])
+        deal_dc(1, "cos0")
+        quantize_weight(ds_dealt, ds_codes[1], ds_planes[1])
+        cos2 = cosine(folded, first, "cos2", all_rows)
+        ys[0, 1] = unit(0, 1, "banks0", "wc_raw0")
+        cos3 = cosine(folded, second, "cos3", all_rows)
+        ys[1, 1] = unit(1, 1, "banks0", "wc_raw1")
 
-        def y_quantize(g, h, yb):
+        features(2, cos2, "ds_raw1")
+        ys[2, 0] = unit(2, 0, "banks1", "table2")
+        ys[2, 1] = unit(2, 1, "banks1", "tab_rows")
+        features(3, cos3, "cos2")
+        ys[3, 0] = unit(3, 0, "banks0", "dc_raw")
+        ys[3, 1] = unit(3, 1, "banks0", "ds_raw0")
+
+        tags = {(0, 0): "table1", (0, 1): "cos3", (1, 0): "rounded2", (1, 1): "rounded3"}
+        rounded = {key: keep.tile([P, HALF, PACK], BF16, name="rounded", tag=tags[key], align_bytes=64) for key in tags}
+
+        def round_y(engine_copy, c, g):
+            h, part = divmod(c, HALF // CHUNK)
+            engine_copy(
+                rounded[h, g][:, (first, second)[part], :].rearrange("p (c i) t -> p c t i", i=4),
+                ys[c, g][:].rearrange("p t (c i) -> p c t i", i=4),
+            )
+
+        def quantize_y(h, g, part):
+            cols = slice(HALF * h + part.start, HALF * h + part.stop)
+            quantize(y_codes[:, g, cols], y_plane[:, g, cols], rounded[h, g][:, part, :].rearrange("p n t -> p (n t)"))
+
+        def store_codes(h, g):
             cols = slice(HALF * h, HALF * (h + 1))
-            quantize(y_codes[:, g, cols], y_plane[:, g, cols], yb[:].rearrange("p n t -> p (n t)"))
             nc.sync.dma_start(out_words[:, g, cols], y_codes[:, g, cols])
 
-        first, second = slice(0, CHUNK), slice(CHUNK, HALF)
-
-        def quantize_both(fs, fc, h, cols):
-            quantize_feat(fs, hs_codes[h][:, cols], hs_planes[h][:, cols])
-            quantize_feat(fc, hc_codes[h][:, cols], hc_planes[h][:, cols])
-
-        folded0 = keep.tile([P, PACK, HALF], F32, name="folded0", align_bytes=64)
-        fold(folded0, 0, first)
-        cos0 = cosine(folded0, first, "cos0")
-        fold(folded0, 0, second)
-        cos1 = cosine(folded0, second, "cos1")
-        fs = apply_gain(sines[0][:, :, first], gs_sb, "wc_raw2")
-        gd0 = grouped_tile()
-        round_weight(nc.vector.tensor_copy, gd0[:], ds_raw[0][:])
-        quantize_feat(fs, hs_codes[0][:, first], hs_planes[0][:, first])
-        quantize_weight(gd0, ds_codes[0], ds_plane[0])
-        fc = apply_gain(cos0[:], gc_sb, "feat0")
-        deal_dc(0)
-        quantize_feat(fc, hc_codes[0][:, first], hc_planes[0][:, first])
-        y00 = narrow_unit(0, 0, first, "banks0", "y0")
-        fs = apply_gain(sines[0][:, :, second], gs_sb, "cos0")
-        fc = apply_gain(cos1[:], gc_sb, "feat1")
-        quantize_both(fs, fc, 0, second)
-        folded1 = keep.tile([P, PACK, HALF], F32, name="folded1", tag="feat0", align_bytes=64)
-        fold(folded1, 1, slice(0, HALF))
-        y10 = narrow_unit(0, 0, second, "banks0", "y1")
-        gd1 = grouped_tile()
-        round_weight(nc.vector.tensor_copy, gd1[:], ds_raw[1][:])
-        deal_dc(1)
-        quantize_weight(gd1, ds_codes[1], ds_plane[1])
-        cos2 = cosine(folded1, first, "cos2")
-        y01 = narrow_unit(1, 0, first, "banks0", "wc_raw0")
-        cos3 = cosine(folded1, second, "cos3")
-        y11 = narrow_unit(1, 0, second, "banks0", "wc_raw1")
-        fs = apply_gain(sines[1][:, :, first], gs_sb, "ds_raw1")
-        fc = apply_gain(cos2[:], gc_sb, "feat1")
-        quantize_both(fs, fc, 1, first)
-        y20 = narrow_unit(0, 1, first, "banks1", "table2")
-        y21 = narrow_unit(1, 1, first, "banks1", "tab_rows")
-        fs = apply_gain(sines[1][:, :, second], gs_sb, "cos2")
-        fc = apply_gain(cos3[:], gc_sb, "feat2")
-        quantize_both(fs, fc, 1, second)
-        y30 = narrow_unit(0, 1, second, "banks0", "dc_raw")
-        y31 = narrow_unit(1, 1, second, "banks0", "ds_raw0")
-        ybs = [y_tile() for u in range(4)]
-        y_round(nc.vector.tensor_copy, ybs[0][:, first, :], y00)
-        y_round(nc.vector.tensor_copy, ybs[0][:, second, :], y10)
-        y_round(nc.vector.tensor_copy, ybs[1][:, first, :], y01)
-        y_quantize(0, 0, ybs[0])
-        y_round(nc.vector.tensor_copy, ybs[1][:, second, :], y11)
-        y_round(nc.vector.tensor_copy, ybs[2][:, first, :], y20)
-        y_quantize(1, 0, ybs[1])
-        y_round(nc.vector.tensor_copy, ybs[3][:, first, :], y21)
-        y_round(nc.scalar.copy, ybs[2][:, second, :], y30)
-        y_round(nc.scalar.copy, ybs[3][:, second, :], y31)
-        y_quantize(0, 1, ybs[2])
-        y_quantize(1, 1, ybs[3])
-
-        out_planes = out_2.rearrange("g (q r) m -> r q g m", r=4).bitcast(I32)
+        round_y(nc.vector.tensor_copy, 0, 0)
+        round_y(nc.vector.tensor_copy, 1, 0)
+        round_y(nc.vector.tensor_copy, 0, 1)
+        quantize_y(0, 0, whole)
+        store_codes(0, 0)
+        round_y(nc.vector.tensor_copy, 1, 1)
+        round_y(nc.vector.tensor_copy, 2, 0)
+        quantize_y(0, 1, whole)
+        store_codes(0, 1)
+        round_y(nc.vector.tensor_copy, 2, 1)
+        quantize_y(1, 0, first)
+        for g in range(GROUPS):
+            round_y(nc.scalar.copy, 3, g)
+        quantize_y(1, 1, first)
+        for g in range(GROUPS):
+            quantize_y(1, g, second)
+            store_codes(1, g)
         for r in range(4):
-            nc.sync.dma_start(out_planes[r], y_plane[r:P:32, :, :].bitcast(I32))
+            nc.sync.dma_start(out_planes[r], y_plane[r:P:QUAD, :, :].bitcast(I32))

@@ -30,7 +30,7 @@ HALVES = S // HALF
 CHUNKS = S // CHUNK
 STAGE_BASE = P - PASSES * BLOCKS
 MOVES_PER_RUN = 6
-TABLE_LEAD = T // 4
+TABLE_LEAD = 5 * T // 16
 VECTOR_SHARE = 80
 
 
@@ -197,6 +197,10 @@ def tile_list_tile_location_codes_kernel(
         round_weight(nc.vector.tensor_copy, wc_dealt[-1][:, :, :VECTOR_SHARE, :], wc_raw[-1][:, :, : PACK * VECTOR_SHARE])
         round_weight(nc.scalar.copy, wc_dealt[-1][:, :, VECTOR_SHARE:, :], wc_raw[-1][:, :, PACK * VECTOR_SHARE :])
         quantize_weight(wc_dealt[-1], wc_codes[-1], wc_planes[-1])
+        early = keep.tile([P, 2, PACK * CHUNK], BF16, name="early", tag="wc_raw2", align_bytes=64)
+        hs1_rows = early[:, 1, :].rearrange("p (t n) -> p t n", t=PACK)
+        for t in range(PACK):
+            nc.scalar.activation(hs1_rows[:, t, :], sines[0][:, t, second], ACT.Copy, scale=gs_sb[:, t : t + 1])
 
         cos_banks = [[None] * PACK for h in range(HALVES)]
 
@@ -279,20 +283,26 @@ def tile_list_tile_location_codes_kernel(
         cos0 = cosine(folded, first, "cos0", (slice(0, 2), slice(2, PACK)))
         fold(folded, 0, second)
         cos1 = cosine(folded, second, "cos1", all_rows)
-        hs0 = feat_tile(CHUNK, "wc_raw2")
-        apply_gain(hs0[:], sines[0][:, :, first], gs_sb)
+        hs0 = early[:, 0, :].rearrange("p (n t) -> p n t", t=PACK)
+        apply_gain(hs0, sines[0][:, :, first], gs_sb)
         ds_dealt = dealt_tile("lead")
         round_weight(nc.vector.tensor_copy, ds_dealt[:], ds_raw[0][:])
-        quantize_feat(hs0[:], 0, first)
+        quantize_feat(hs0, 0, first)
         quantize_weight(ds_dealt, ds_codes[0], ds_planes[0])
-        deal_dc(0, "wc_raw2")
+        deal_dc(0, "wc_dealt0")
         hc0 = feat_tile(CHUNK, "lead")
         apply_gain(hc0[:], cos0[:], gc_sb)
         quantize_feat(hc0[:], 0, second)
         ys = {}
         ys[0, 0] = unit(0, 0, "banks0", "y0")
 
-        features(1, cos1, "cos0")
+        feat1 = feat_tile(2 * CHUNK, "cos0")
+        nc.vector.tensor_copy(
+            feat1[:, first, :].rearrange("p (c i) t -> p c t i", i=4), hs1_rows.rearrange("p t (c i) -> p c t i", i=4)
+        )
+        apply_gain(feat1[:, second, :], cos1[:], gc_sb)
+        for cols in (first, second):
+            quantize_feat(feat1[:, cols, :], 1, cols)
         folded = keep.tile([P, PACK, HALF], F32, name="folded1", tag="lead", align_bytes=64)
         fold(folded, 1, whole)
         ys[1, 0] = unit(1, 0, "banks0", "y1")
@@ -340,12 +350,12 @@ def tile_list_tile_location_codes_kernel(
         quantize_y(0, 1, whole)
         store_codes(0, 1)
         round_y(nc.vector.tensor_copy, 2, 1)
-        quantize_y(1, 0, first)
-        for g in range(GROUPS):
-            round_y(nc.scalar.copy, 3, g)
+        round_y(nc.scalar.copy, 3, 0)
+        round_y(nc.scalar.copy, 3, 1)
         quantize_y(1, 1, first)
-        for g in range(GROUPS):
-            quantize_y(1, g, second)
-            store_codes(1, g)
+        quantize_y(1, 0, whole)
+        store_codes(1, 0)
+        quantize_y(1, 1, second)
+        store_codes(1, 1)
         for r in range(4):
             nc.sync.dma_start(out_planes[r], y_plane[r:P:QUAD, :, :].bitcast(I32))

@@ -30,7 +30,7 @@ HALVES = S // HALF
 CHUNKS = S // CHUNK
 STAGE_BASE = P - PASSES * BLOCKS
 MOVES_PER_RUN = 6
-TABLE_LEAD = 5 * T // 16
+TABLE_LEAD = 7 * T // 16
 VECTOR_SHARE = 80
 
 
@@ -48,21 +48,21 @@ def tile_list_tile_location_codes_kernel(
         offsets = keep.tile([P, S // 16], U16, name="offsets")
         nc.sync.dma_start(offsets[:], offs)
 
+        ws_rows = keep.tile([P, PASSES, H], U8, name="ws_rows", align_bytes=64)
+        nc.vector.memset(ws_rows[:].bitcast(I32), 0)
         tab_flat = tab_scales.rearrange("a q t -> (a q) t").bitcast(I32)
-        ws_flat = ws_scales.rearrange("a q c -> (a q) c").bitcast(I32)
         tab_rows = keep.tile([P, T], U8, name="tab_rows", align_bytes=64)
-        ws_rows = keep.tile([P, H], U8, name="ws_rows", align_bytes=64)
+        nc.sync.dma_start(tab_rows[STAGE_BASE + BLOCKS :, :].bitcast(I32), tab_flat[BLOCKS:, :])
+        nc.sync.dma_start(tab_rows[STAGE_BASE : STAGE_BASE + BLOCKS, :].bitcast(I32), tab_flat[:BLOCKS, :])
+        ws_by_row = ws_scales.rearrange("a (q r) c -> r q a c", r=4).bitcast(I32)
+        for r in range(4):
+            nc.sync.dma_start(ws_rows[r:P:QUAD, :, :].bitcast(I32), ws_by_row[r])
         dc_rows = keep.tile([P, N], U8, name="dc_rows", align_bytes=64)
-        widths = [S + H] * (PASSES - 1) + [S + H + N]
-        planes = [keep.tile([P, widths[a]], U8, name="plane%d" % a, align_bytes=64) for a in range(PASSES)]
-        for rows, flat in ((tab_rows, tab_flat), (ws_rows, ws_flat)):
-            nc.sync.dma_start(rows[STAGE_BASE + BLOCKS :, :].bitcast(I32), flat[BLOCKS:, :])
-            nc.sync.dma_start(rows[STAGE_BASE : STAGE_BASE + BLOCKS, :].bitcast(I32), flat[:BLOCKS, :])
-        nc.sync.dma_start(dc_rows[P - BLOCKS :, :].bitcast(I32), dc_scales[0].bitcast(I32))
-        for rows in (tab_rows, ws_rows):
-            nc.vector.memset(rows[:STAGE_BASE, :].bitcast(I32), 0)
+        planes = [keep.tile([P, S], U8, name="plane%d" % a, align_bytes=64) for a in range(PASSES)]
+        dc_plane = keep.tile([P, N], U8, name="dc_plane", align_bytes=64)
+        nc.vector.memset(tab_rows[:STAGE_BASE, :].bitcast(I32), 0)
         nc.vector.memset(dc_rows[: P - BLOCKS, :].bitcast(I32), 0)
-        for plane in planes:
+        for plane in planes + [dc_plane]:
             nc.vector.memset(plane[:].bitcast(I32), 0)
 
         table = [keep.tile([P, T], I32, name="table%d" % a, tag="table%d" % a, align_bytes=64) for a in range(PASSES)]
@@ -71,30 +71,31 @@ def tile_list_tile_location_codes_kernel(
             nc.sync.dma_start(table[a][:, cols], tab_words[a].rearrange("p t i -> p (t i)").bitcast(I32)[:, cols])
 
         load_table(0, slice(0, T))
+        nc.sync.dma_start(dc_rows[P - BLOCKS :, :].bitcast(I32), dc_scales[0].bitcast(I32))
         ws_raw = keep.tile([P, PASSES, 2 * H], U8, name="ws_raw", align_bytes=64)
         nc.sync.dma_start(ws_raw[:].bitcast(I32), ws_words.rearrange("a p c -> p a c").bitcast(I32))
         load_table(1, slice(0, TABLE_LEAD))
 
         picked_rows = keep.tile([P, S], U8, name="picked_rows", align_bytes=64)
-        staged = keep.tile([P, S + H + N], U8, name="staged", align_bytes=64)
+        ws_planes = keep.tile([P, PASSES, H], U8, name="ws_planes", align_bytes=64)
+        dc_staged = keep.tile([P, N], U8, name="dc_staged", align_bytes=64)
         nc.vector.tensor_copy(picked_rows[:], tab_rows[:].indirect(offsets[:]))
-        nc.vector.tensor_copy(
-            staged[:, S : S + H].rearrange("p (t m) -> p t m", t=PACK), ws_rows[:].rearrange("p (m t) -> p t m", t=PACK)
-        )
-        nc.vector.tensor_copy(staged[:, :S].bitcast(I32), picked_rows[:].bitcast(I32))
-        nc.vector.tensor_copy(
-            staged[:, S + H :].rearrange("p (g t m) -> p g t m", g=GROUPS, t=PACK),
-            dc_rows[:].rearrange("p (g m t) -> p g t m", g=GROUPS, t=PACK),
-        )
         moves = [(a, r) for a in range(PASSES) for r in range(4)]
         for run, rest in enumerate((slice(TABLE_LEAD, T), slice(0, T))):
             for a, r in moves[MOVES_PER_RUN * run : MOVES_PER_RUN * (run + 1)]:
                 base = STAGE_BASE + BLOCKS * a
                 nc.sync.dma_start(
-                    planes[a][r:P:QUAD, :].bitcast(I32), staged[base + r : base + BLOCKS : 4, : widths[a]].bitcast(I32)
+                    planes[a][r:P:QUAD, :].bitcast(I32), picked_rows[base + r : base + BLOCKS : 4, :].bitcast(I32)
                 )
             load_table(run + 1, rest)
-        dc_plane = planes[PASSES - 1][:, S + H :]
+        for a in range(PASSES):
+            nc.vector.tensor_copy(
+                ws_planes[:, a, :].rearrange("p (t m) -> p t m", t=PACK), ws_rows[:, a, :].rearrange("p (m t) -> p t m", t=PACK)
+            )
+        nc.vector.tensor_copy(
+            dc_staged[:].rearrange("p (g t m) -> p g t m", g=GROUPS, t=PACK),
+            dc_rows[:].rearrange("p (g m t) -> p g t m", g=GROUPS, t=PACK),
+        )
 
         gs_sb = keep.tile([P, PACK], F32, name="gs_sb")
         gc_sb = keep.tile([P, PACK], F32, name="gc_sb")
@@ -137,7 +138,7 @@ def tile_list_tile_location_codes_kernel(
                 for t in range(PACK):
                     angle_pass(
                         sin_banks[h][t], ws_codes[:, a, 2 * P * t : 2 * P * (t + 1)].bitcast(FP4X4),
-                        planes[a][:, S + P * t : S + P * (t + 1)], a, h, PASSES - 1,
+                        ws_planes[:, a, P * t : P * (t + 1)], a, h, PASSES - 1,
                     )
 
         def load_weight(rows, name):
@@ -149,6 +150,8 @@ def tile_list_tile_location_codes_kernel(
         ds_raw = [load_weight(ds[:, :SPAN], "ds_raw0")]
         dc_raw = keep.tile([P, N], I32, name="dc_raw", align_bytes=64)
         nc.sync.dma_start(dc_raw[:], dc_words[0].rearrange("p c i -> p (c i)").bitcast(I32))
+        for r in range(4):
+            nc.sync.dma_start(dc_plane[r:P:QUAD, :].bitcast(I32), dc_staged[P - BLOCKS + r : P : 4, :].bitcast(I32))
         ds_raw.append(load_weight(ds[:, SPAN:], "ds_raw1"))
 
         wc_codes = [keep.tile([P, H], U32, name="wc_codes%d" % a, align_bytes=64) for a in range(PASSES)]
@@ -192,8 +195,14 @@ def tile_list_tile_location_codes_kernel(
 
         wc_dealt = [dealt_tile(tag) for tag in ("wc_dealt0", "wc_dealt1", "lead")]
         for a in range(PASSES - 1):
-            round_weight(nc.vector.tensor_copy, wc_dealt[a][:], wc_raw[a][:])
-            quantize_weight(wc_dealt[a], wc_codes[a], wc_planes[a])
+            for u in range(2):
+                nc.vector.tensor_copy(
+                    wc_dealt[a][:, 2 * u : 2 * u + 2].rearrange("p e m j -> p m j e"),
+                    wc_raw[a][:].rearrange("p j (m u e) -> p u m j e", u=2, e=2)[:, u],
+                )
+            for u in range(2):
+                cols = slice(2 * P * u, 2 * P * (u + 1))
+                quantize(wc_codes[a][:, cols], wc_planes[a][:, cols], wc_dealt[a][:, 2 * u : 2 * u + 2].rearrange("p e m j -> p (e m j)"))
         round_weight(nc.vector.tensor_copy, wc_dealt[-1][:, :, :VECTOR_SHARE, :], wc_raw[-1][:, :, : PACK * VECTOR_SHARE])
         round_weight(nc.scalar.copy, wc_dealt[-1][:, :, VECTOR_SHARE:, :], wc_raw[-1][:, :, PACK * VECTOR_SHARE :])
         quantize_weight(wc_dealt[-1], wc_codes[-1], wc_planes[-1])
@@ -289,9 +298,9 @@ def tile_list_tile_location_codes_kernel(
         round_weight(nc.vector.tensor_copy, ds_dealt[:], ds_raw[0][:])
         quantize_feat(hs0, 0, first)
         quantize_weight(ds_dealt, ds_codes[0], ds_planes[0])
-        deal_dc(0, "wc_dealt0")
         hc0 = feat_tile(CHUNK, "lead")
         apply_gain(hc0[:], cos0[:], gc_sb)
+        deal_dc(0, "wc_dealt0")
         quantize_feat(hc0[:], 0, second)
         ys = {}
         ys[0, 0] = unit(0, 0, "banks0", "y0")
@@ -347,9 +356,9 @@ def tile_list_tile_location_codes_kernel(
         store_codes(0, 0)
         round_y(nc.vector.tensor_copy, 1, 1)
         round_y(nc.vector.tensor_copy, 2, 0)
+        round_y(nc.vector.tensor_copy, 2, 1)
         quantize_y(0, 1, whole)
         store_codes(0, 1)
-        round_y(nc.vector.tensor_copy, 2, 1)
         round_y(nc.scalar.copy, 3, 0)
         round_y(nc.scalar.copy, 3, 1)
         quantize_y(1, 1, first)

@@ -28,7 +28,7 @@ HALF = 512
 CHUNK = 256
 HALVES = S // HALF
 CHUNKS = S // CHUNK
-STAGE_BASE = P - PASSES * BLOCKS
+STAGE_BASES = (48, 96, 112)
 MOVES_PER_RUN = 6
 TABLE_LEAD = 7 * T // 16
 VECTOR_SHARE = 80
@@ -48,22 +48,22 @@ def tile_list_tile_location_codes_kernel(
         offsets = keep.tile([P, S // 16], U16, name="offsets")
         nc.sync.dma_start(offsets[:], offs)
 
-        ws_rows = keep.tile([P, PASSES, H], U8, name="ws_rows", align_bytes=64)
+        ws_rows = keep.tile([P, PASSES, H], U8, name="ws_rows", tag="ws_rows", align_bytes=64)
         nc.vector.memset(ws_rows[:].bitcast(I32), 0)
         tab_flat = tab_scales.rearrange("a q t -> (a q) t").bitcast(I32)
         tab_rows = keep.tile([P, T], U8, name="tab_rows", align_bytes=64)
-        nc.sync.dma_start(tab_rows[STAGE_BASE + BLOCKS :, :].bitcast(I32), tab_flat[BLOCKS:, :])
-        nc.sync.dma_start(tab_rows[STAGE_BASE : STAGE_BASE + BLOCKS, :].bitcast(I32), tab_flat[:BLOCKS, :])
+        nc.sync.dma_start(tab_rows[STAGE_BASES[1] :, :].bitcast(I32), tab_flat[BLOCKS:, :])
+        nc.sync.dma_start(tab_rows[STAGE_BASES[0] : STAGE_BASES[0] + BLOCKS, :].bitcast(I32), tab_flat[:BLOCKS, :])
         ws_by_row = ws_scales.rearrange("a (q r) c -> r q a c", r=4).bitcast(I32)
         for r in range(4):
             nc.sync.dma_start(ws_rows[r:P:QUAD, :, :].bitcast(I32), ws_by_row[r])
         dc_rows = keep.tile([P, N], U8, name="dc_rows", align_bytes=64)
         planes = [keep.tile([P, S], U8, name="plane%d" % a, align_bytes=64) for a in range(PASSES)]
-        dc_plane = keep.tile([P, N], U8, name="dc_plane", align_bytes=64)
-        nc.vector.memset(tab_rows[:STAGE_BASE, :].bitcast(I32), 0)
-        nc.vector.memset(dc_rows[: P - BLOCKS, :].bitcast(I32), 0)
-        for plane in planes + [dc_plane]:
+        nc.vector.memset(tab_rows[: STAGE_BASES[0], :].bitcast(I32), 0)
+        nc.vector.memset(tab_rows[STAGE_BASES[0] + BLOCKS : STAGE_BASES[1], :].bitcast(I32), 0)
+        for plane in planes:
             nc.vector.memset(plane[:].bitcast(I32), 0)
+        nc.vector.memset(dc_rows[: P - BLOCKS, :].bitcast(I32), 0)
 
         table = [keep.tile([P, T], I32, name="table%d" % a, tag="table%d" % a, align_bytes=64) for a in range(PASSES)]
 
@@ -83,7 +83,7 @@ def tile_list_tile_location_codes_kernel(
         moves = [(a, r) for a in range(PASSES) for r in range(4)]
         for run, rest in enumerate((slice(TABLE_LEAD, T), slice(0, T))):
             for a, r in moves[MOVES_PER_RUN * run : MOVES_PER_RUN * (run + 1)]:
-                base = STAGE_BASE + BLOCKS * a
+                base = STAGE_BASES[a]
                 nc.sync.dma_start(
                     planes[a][r:P:QUAD, :].bitcast(I32), picked_rows[base + r : base + BLOCKS : 4, :].bitcast(I32)
                 )
@@ -97,12 +97,14 @@ def tile_list_tile_location_codes_kernel(
             dc_rows[:].rearrange("p (g m t) -> p g t m", g=GROUPS, t=PACK),
         )
 
+        dc_plane = keep.tile([P, N], U8, name="dc_plane", tag="ws_rows", align_bytes=64)
+        nc.vector.memset(dc_plane[:].bitcast(I32), 0)
+
         gs_sb = keep.tile([P, PACK], F32, name="gs_sb")
         gc_sb = keep.tile([P, PACK], F32, name="gc_sb")
         phase_sb = keep.tile([P, PACK], F32, name="phase_sb")
         nc.sync.dma_start(gs_sb[:], gs.rearrange("(p t) -> p t", t=PACK))
         nc.sync.dma_start(phase_sb[:], phase.rearrange("(p t) -> p t", t=PACK))
-        nc.sync.dma_start(gc_sb[:], gc.rearrange("(p t) -> p t", t=PACK))
 
         ws_codes = keep.tile([P, PASSES, 2 * H], U8, name="ws_codes", align_bytes=64)
         for a in range(PASSES):
@@ -150,6 +152,7 @@ def tile_list_tile_location_codes_kernel(
         ds_raw = [load_weight(ds[:, :SPAN], "ds_raw0")]
         dc_raw = keep.tile([P, N], I32, name="dc_raw", align_bytes=64)
         nc.sync.dma_start(dc_raw[:], dc_words[0].rearrange("p c i -> p (c i)").bitcast(I32))
+        nc.sync.dma_start(gc_sb[:], gc.rearrange("(p t) -> p t", t=PACK))
         for r in range(4):
             nc.sync.dma_start(dc_plane[r:P:QUAD, :].bitcast(I32), dc_staged[P - BLOCKS + r : P : 4, :].bitcast(I32))
         ds_raw.append(load_weight(ds[:, SPAN:], "ds_raw1"))

@@ -103,8 +103,6 @@ def tile_list_tile_location_codes_kernel(
         gs_sb = keep.tile([P, PACK], F32, name="gs_sb")
         gc_sb = keep.tile([P, PACK], F32, name="gc_sb")
         phase_sb = keep.tile([P, PACK], F32, name="phase_sb")
-        nc.sync.dma_start(gs_sb[:], gs.rearrange("(p t) -> p t", t=PACK))
-        nc.sync.dma_start(phase_sb[:], phase.rearrange("(p t) -> p t", t=PACK))
 
         ws_codes = keep.tile([P, PASSES, 2 * H], U8, name="ws_codes", align_bytes=64)
         for a in range(PASSES):
@@ -149,6 +147,8 @@ def tile_list_tile_location_codes_kernel(
             return raw
 
         wc_raw = [load_weight(wc[SPAN * a : SPAN * (a + 1), :], "wc_raw%d" % a) for a in range(PASSES)]
+        nc.sync.dma_start(gs_sb[:], gs.rearrange("(p t) -> p t", t=PACK))
+        nc.sync.dma_start(phase_sb[:], phase.rearrange("(p t) -> p t", t=PACK))
         ds_raw = [load_weight(ds[:, :SPAN], "ds_raw0")]
         dc_raw = keep.tile([P, N], I32, name="dc_raw", align_bytes=64)
         nc.sync.dma_start(dc_raw[:], dc_words[0].rearrange("p c i -> p (c i)").bitcast(I32))
@@ -159,7 +159,8 @@ def tile_list_tile_location_codes_kernel(
 
         wc_codes = [keep.tile([P, H], U32, name="wc_codes%d" % a, align_bytes=64) for a in range(PASSES)]
         wc_planes = [keep.tile([P, H], U8, name="wc_plane%d" % a, align_bytes=64) for a in range(PASSES)]
-        h_codes = [keep.tile([P, 2 * CHUNK], U32, name="h_codes%d" % c, align_bytes=64) for c in range(CHUNKS)]
+        code_tags = ["ds_raw0"] + ["h_codes%d" % c for c in range(1, CHUNKS)]
+        h_codes = [keep.tile([P, 2 * CHUNK], U32, name="h_codes", tag=tag, align_bytes=64) for tag in code_tags]
         h_planes = [keep.tile([P, 2 * CHUNK], U8, name="h_plane%d" % c, align_bytes=64) for c in range(CHUNKS)]
         sines = [keep.tile([P, PACK, HALF], F32, name="sines%d" % h, tag="table%d" % h, align_bytes=64) for h in range(HALVES)]
 
@@ -197,18 +198,23 @@ def tile_list_tile_location_codes_kernel(
                 nc.scalar.activation(sines[h][:, t, :], sin_banks[h][t][:], ACT.Sin)
 
         wc_dealt = [dealt_tile(tag) for tag in ("wc_dealt0", "wc_dealt1", "lead")]
+
+        def quantize_wc(a):
+            for u in range(2):
+                cols = slice(2 * P * u, 2 * P * (u + 1))
+                pair = wc_dealt[a][:, 2 * u : 2 * u + 2].rearrange("p e m j -> p (e m j)")
+                quantize(wc_codes[a][:, cols], wc_planes[a][:, cols], pair)
+
         for a in range(PASSES - 1):
             for u in range(2):
                 nc.vector.tensor_copy(
                     wc_dealt[a][:, 2 * u : 2 * u + 2].rearrange("p e m j -> p m j e"),
                     wc_raw[a][:].rearrange("p j (m u e) -> p u m j e", u=2, e=2)[:, u],
                 )
-            for u in range(2):
-                cols = slice(2 * P * u, 2 * P * (u + 1))
-                quantize(wc_codes[a][:, cols], wc_planes[a][:, cols], wc_dealt[a][:, 2 * u : 2 * u + 2].rearrange("p e m j -> p (e m j)"))
+            quantize_wc(a)
         round_weight(nc.vector.tensor_copy, wc_dealt[-1][:, :, :VECTOR_SHARE, :], wc_raw[-1][:, :, : PACK * VECTOR_SHARE])
         round_weight(nc.scalar.copy, wc_dealt[-1][:, :, VECTOR_SHARE:, :], wc_raw[-1][:, :, PACK * VECTOR_SHARE :])
-        quantize_weight(wc_dealt[-1], wc_codes[-1], wc_planes[-1])
+        quantize_wc(PASSES - 1)
         early = keep.tile([P, 2, PACK * CHUNK], BF16, name="early", tag="wc_raw2", align_bytes=64)
         hs1_rows = early[:, 1, :].rearrange("p (t n) -> p t n", t=PACK)
         for t in range(PACK):
@@ -267,24 +273,42 @@ def tile_list_tile_location_codes_kernel(
         out_words = out_1.rearrange("g p m t -> p g (m t)").bitcast(I32)
         out_planes = out_2.rearrange("g (q r) m -> r q g m", r=4).bitcast(I32)
 
-        def product(out, g, t, c):
+        def sine_pass(out, g, t, c, start):
             places = slice(P * t, P * (t + 1))
             nc.tensor.matmul_mx(
                 out=out, lhsT=ds_codes[g][:, places].bitcast(FP8X4), lhsT_scale=ds_planes[g][:, places],
-                rhs=h_codes[c][:, first].bitcast(FP8X4), rhs_scale=h_planes[c][:, first], start=True, stop=False,
+                rhs=h_codes[c][:, first].bitcast(FP8X4), rhs_scale=h_planes[c][:, first], start=start, stop=False,
             )
+
+        def cosine_pass(out, g, t, c, stop):
             nc.tensor.matmul_mx(
-                out=out, lhsT=dc_codes[g][:, places].bitcast(FP8X4),
+                out=out, lhsT=dc_codes[g][:, P * t : P * (t + 1)].bitcast(FP8X4),
                 lhsT_scale=dc_plane[:, SPAN * g + P * t : SPAN * g + P * (t + 1)],
-                rhs=h_codes[c][:, second].bitcast(FP8X4), rhs_scale=h_planes[c][:, second], start=False, stop=True,
+                rhs=h_codes[c][:, second].bitcast(FP8X4), rhs_scale=h_planes[c][:, second], start=False, stop=stop,
             )
+
+        def open_unit(c, g, tag):
+            banks = [psum.tile([P, 2, CHUNK], F32, name="bank", tag=tag) for pair in range(PACK // 2)]
+            for t in range(PACK):
+                sine_pass(banks[t // 2][:, t % 2, :], g, t, c, t % 2 == 0)
+            return banks
+
+        def close_unit(c, g, banks, tag):
+            y = keep.tile([P, PACK, CHUNK], F32, name="y", tag=tag, align_bytes=64)
+            for pair in range(PACK // 2):
+                for u in range(2):
+                    cosine_pass(banks[pair][:, u, :], g, 2 * pair + u, c, u == 1)
+                nc.scalar.copy(y[:, 2 * pair : 2 * pair + 2, :], banks[pair][:])
+            nc.sync.dma_start(out_rows[g, :, :, CHUNK * c : CHUNK * (c + 1)], y[:])
+            return y
 
         def unit(c, g, banks, tag):
             y = keep.tile([P, PACK, CHUNK], F32, name="y", tag=tag, align_bytes=64)
             for pair in range(PACK // 2):
                 bank = psum.tile([P, 2, CHUNK], F32, name="bank", tag=banks)
                 for u in range(2):
-                    product(bank[:, u, :], g, 2 * pair + u, c)
+                    sine_pass(bank[:, u, :], g, 2 * pair + u, c, True)
+                    cosine_pass(bank[:, u, :], g, 2 * pair + u, c, True)
                 nc.scalar.copy(y[:, 2 * pair : 2 * pair + 2, :], bank[:])
             nc.sync.dma_start(out_rows[g, :, :, CHUNK * c : CHUNK * (c + 1)], y[:])
             return y
@@ -301,12 +325,13 @@ def tile_list_tile_location_codes_kernel(
         round_weight(nc.vector.tensor_copy, ds_dealt[:], ds_raw[0][:])
         quantize_feat(hs0, 0, first)
         quantize_weight(ds_dealt, ds_codes[0], ds_planes[0])
+        lead_banks = open_unit(0, 0, "banks0")
         hc0 = feat_tile(CHUNK, "lead")
         apply_gain(hc0[:], cos0[:], gc_sb)
         deal_dc(0, "wc_dealt0")
         quantize_feat(hc0[:], 0, second)
         ys = {}
-        ys[0, 0] = unit(0, 0, "banks0", "y0")
+        ys[0, 0] = close_unit(0, 0, lead_banks, "y0")
 
         feat1 = feat_tile(2 * CHUNK, "cos0")
         nc.vector.tensor_copy(

@@ -326,7 +326,7 @@ def tile_list_tile_location_codes_kernel(
         quantize_feat(hs0, 0, first)
         quantize_weight(ds_dealt, ds_codes[0], ds_planes[0])
         lead_banks = open_unit(0, 0, "banks0")
-        hc0 = feat_tile(CHUNK, "lead")
+        hc0 = feat_tile(CHUNK, "wc_dealt1")
         apply_gain(hc0[:], cos0[:], gc_sb)
         deal_dc(0, "wc_dealt0")
         quantize_feat(hc0[:], 0, second)
@@ -340,7 +340,7 @@ def tile_list_tile_location_codes_kernel(
         apply_gain(feat1[:, second, :], cos1[:], gc_sb)
         for cols in (first, second):
             quantize_feat(feat1[:, cols, :], 1, cols)
-        folded = keep.tile([P, PACK, HALF], F32, name="folded1", tag="lead", align_bytes=64)
+        folded = keep.tile([P, PACK, HALF], F32, name="folded1", tag="wc_dealt1", align_bytes=64)
         fold(folded, 1, whole)
         ys[1, 0] = unit(1, 0, "banks0", "y1")
         ds_dealt = dealt_tile("cos1")
@@ -356,8 +356,6 @@ def tile_list_tile_location_codes_kernel(
         ys[2, 0] = unit(2, 0, "banks1", "table2")
         ys[2, 1] = unit(2, 1, "banks1", "tab_rows")
         features(3, cos3, "cos2")
-        ys[3, 0] = unit(3, 0, "banks0", "dc_raw")
-        ys[3, 1] = unit(3, 1, "banks0", "ds_raw0")
 
         tags = {(0, 0): "table1", (0, 1): "cos3", (1, 0): "rounded2", (1, 1): "rounded3"}
         rounded = {key: keep.tile([P, HALF, PACK], BF16, name="rounded", tag=tags[key], align_bytes=64) for key in tags}
@@ -377,13 +375,15 @@ def tile_list_tile_location_codes_kernel(
             cols = slice(HALF * h, HALF * (h + 1))
             nc.sync.dma_start(out_words[:, g, cols], y_codes[:, g, cols])
 
+        round_y(nc.scalar.copy, 2, 0)
+        ys[3, 0] = unit(3, 0, "banks0", "dc_raw")
+        ys[3, 1] = unit(3, 1, "banks0", "ds_raw0")
         round_y(nc.vector.tensor_copy, 0, 0)
         round_y(nc.vector.tensor_copy, 1, 0)
         round_y(nc.vector.tensor_copy, 0, 1)
         quantize_y(0, 0, whole)
         store_codes(0, 0)
         round_y(nc.vector.tensor_copy, 1, 1)
-        round_y(nc.vector.tensor_copy, 2, 0)
         round_y(nc.vector.tensor_copy, 2, 1)
         quantize_y(0, 1, whole)
         store_codes(0, 1)

@@ -159,9 +159,12 @@ def tile_list_tile_location_codes_kernel(
 
         wc_codes = [keep.tile([P, H], U32, name="wc_codes%d" % a, align_bytes=64) for a in range(PASSES)]
         wc_planes = [keep.tile([P, H], U8, name="wc_plane%d" % a, align_bytes=64) for a in range(PASSES)]
-        code_tags = ["ds_raw0"] + ["h_codes%d" % c for c in range(1, CHUNKS)]
-        h_codes = [keep.tile([P, 2 * CHUNK], U32, name="h_codes", tag=tag, align_bytes=64) for tag in code_tags]
-        h_planes = [keep.tile([P, 2 * CHUNK], U8, name="h_plane%d" % c, align_bytes=64) for c in range(CHUNKS)]
+        code_tags = ("ds_raw0", "h_codes1")
+        h_codes = [keep.tile([P, 2, HALF], U32, name="h_codes", tag=tag, align_bytes=64) for tag in code_tags]
+        h_planes = [keep.tile([P, 2, HALF], U8, name="h_plane%d" % h, align_bytes=64) for h in range(HALVES)]
+
+        def feature_operand(branch, h, cols):
+            return h_codes[h][:, branch, cols], h_planes[h][:, branch, cols]
         sines = [keep.tile([P, PACK, HALF], F32, name="sines%d" % h, tag="table%d" % h, align_bytes=64) for h in range(HALVES)]
 
         def quantize(codes, plane, values):
@@ -190,8 +193,9 @@ def tile_list_tile_location_codes_kernel(
                 ALU.mult,
             )
 
-        def quantize_feat(feat, c, cols):
-            quantize(h_codes[c][:, cols], h_planes[c][:, cols], feat.rearrange("p n t -> p (n t)"))
+        def quantize_feat(feat, c, branch):
+            codes, plane = feature_operand(branch, c // 2, (first, second)[c % 2])
+            quantize(codes, plane, feat.rearrange("p n t -> p (n t)"))
 
         for h in range(HALVES):
             for t in range(PACK):
@@ -253,8 +257,8 @@ def tile_list_tile_location_codes_kernel(
             feat = feat_tile(2 * CHUNK, tag)
             apply_gain(feat[:, first, :], sines[h][:, :, (first, second)[part]], gs_sb)
             apply_gain(feat[:, second, :], cosines[:], gc_sb)
-            for cols in (first, second):
-                quantize_feat(feat[:, cols, :], c, cols)
+            for branch, cols in enumerate((first, second)):
+                quantize_feat(feat[:, cols, :], c, branch)
 
         ds_codes = [keep.tile([P, SPAN], U32, name="ds_codes%d" % g, align_bytes=64) for g in range(GROUPS)]
         ds_planes = [keep.tile([P, SPAN], U8, name="ds_plane%d" % g, align_bytes=64) for g in range(GROUPS)]
@@ -273,31 +277,33 @@ def tile_list_tile_location_codes_kernel(
         out_words = out_1.rearrange("g p m t -> p g (m t)").bitcast(I32)
         out_planes = out_2.rearrange("g (q r) m -> r q g m", r=4).bitcast(I32)
 
-        def sine_pass(out, g, t, c, start):
+        def sine_pass(out, g, t, h, cols, start):
             places = slice(P * t, P * (t + 1))
+            codes, plane = feature_operand(0, h, cols)
             nc.tensor.matmul_mx(
                 out=out, lhsT=ds_codes[g][:, places].bitcast(FP8X4), lhsT_scale=ds_planes[g][:, places],
-                rhs=h_codes[c][:, first].bitcast(FP8X4), rhs_scale=h_planes[c][:, first], start=start, stop=False,
+                rhs=codes.bitcast(FP8X4), rhs_scale=plane, start=start, stop=False,
             )
 
-        def cosine_pass(out, g, t, c, stop):
+        def cosine_pass(out, g, t, h, cols, stop):
+            codes, plane = feature_operand(1, h, cols)
             nc.tensor.matmul_mx(
                 out=out, lhsT=dc_codes[g][:, P * t : P * (t + 1)].bitcast(FP8X4),
                 lhsT_scale=dc_plane[:, SPAN * g + P * t : SPAN * g + P * (t + 1)],
-                rhs=h_codes[c][:, second].bitcast(FP8X4), rhs_scale=h_planes[c][:, second], start=False, stop=stop,
+                rhs=codes.bitcast(FP8X4), rhs_scale=plane, start=False, stop=stop,
             )
 
         def open_unit(c, g, tag):
             banks = [psum.tile([P, 2, CHUNK], F32, name="bank", tag=tag) for pair in range(PACK // 2)]
             for t in range(PACK):
-                sine_pass(banks[t // 2][:, t % 2, :], g, t, c, t % 2 == 0)
+                sine_pass(banks[t // 2][:, t % 2, :], g, t, c // 2, (first, second)[c % 2], t % 2 == 0)
             return banks
 
         def close_unit(c, g, banks, tag):
             y = keep.tile([P, PACK, CHUNK], F32, name="y", tag=tag, align_bytes=64)
             for pair in range(PACK // 2):
                 for u in range(2):
-                    cosine_pass(banks[pair][:, u, :], g, 2 * pair + u, c, u == 1)
+                    cosine_pass(banks[pair][:, u, :], g, 2 * pair + u, c // 2, (first, second)[c % 2], u == 1)
                 nc.scalar.copy(y[:, 2 * pair : 2 * pair + 2, :], banks[pair][:])
             nc.sync.dma_start(out_rows[g, :, :, CHUNK * c : CHUNK * (c + 1)], y[:])
             return y
@@ -307,8 +313,8 @@ def tile_list_tile_location_codes_kernel(
             for pair in range(PACK // 2):
                 bank = psum.tile([P, 2, CHUNK], F32, name="bank", tag=banks)
                 for u in range(2):
-                    sine_pass(bank[:, u, :], g, 2 * pair + u, c, True)
-                    cosine_pass(bank[:, u, :], g, 2 * pair + u, c, True)
+                    sine_pass(bank[:, u, :], g, 2 * pair + u, c // 2, (first, second)[c % 2], True)
+                    cosine_pass(bank[:, u, :], g, 2 * pair + u, c // 2, (first, second)[c % 2], True)
                 nc.scalar.copy(y[:, 2 * pair : 2 * pair + 2, :], bank[:])
             nc.sync.dma_start(out_rows[g, :, :, CHUNK * c : CHUNK * (c + 1)], y[:])
             return y
@@ -323,13 +329,13 @@ def tile_list_tile_location_codes_kernel(
         apply_gain(hs0, sines[0][:, :, first], gs_sb)
         ds_dealt = dealt_tile("lead")
         round_weight(nc.vector.tensor_copy, ds_dealt[:], ds_raw[0][:])
-        quantize_feat(hs0, 0, first)
+        quantize_feat(hs0, 0, 0)
         quantize_weight(ds_dealt, ds_codes[0], ds_planes[0])
         lead_banks = open_unit(0, 0, "banks0")
         hc0 = feat_tile(CHUNK, "wc_dealt1")
         apply_gain(hc0[:], cos0[:], gc_sb)
         deal_dc(0, "wc_dealt0")
-        quantize_feat(hc0[:], 0, second)
+        quantize_feat(hc0[:], 0, 1)
         ys = {}
         ys[0, 0] = close_unit(0, 0, lead_banks, "y0")
 
@@ -338,8 +344,8 @@ def tile_list_tile_location_codes_kernel(
             feat1[:, first, :].rearrange("p (c i) t -> p c t i", i=4), hs1_rows.rearrange("p t (c i) -> p c t i", i=4)
         )
         apply_gain(feat1[:, second, :], cos1[:], gc_sb)
-        for cols in (first, second):
-            quantize_feat(feat1[:, cols, :], 1, cols)
+        for branch, cols in enumerate((first, second)):
+            quantize_feat(feat1[:, cols, :], 1, branch)
         folded = keep.tile([P, PACK, HALF], F32, name="folded1", tag="wc_dealt1", align_bytes=64)
         fold(folded, 1, whole)
         ys[1, 0] = unit(1, 0, "banks0", "y1")
@@ -348,9 +354,20 @@ def tile_list_tile_location_codes_kernel(
         deal_dc(1, "cos0")
         quantize_weight(ds_dealt, ds_codes[1], ds_planes[1])
         cos2 = cosine(folded, first, "cos2", all_rows)
-        ys[0, 1] = unit(0, 1, "banks0", "wc_raw0")
+        wide = keep.tile([P, PACK, HALF], F32, name="wide", tag="wc_raw0", align_bytes=64)
+
+        def wide_pair(pair):
+            rows = slice(2 * pair, 2 * pair + 2)
+            for t in range(rows.start, rows.stop):
+                bank = psum.tile([P, HALF], F32, name="bank", tag="banks0")
+                sine_pass(bank[:], 1, t, 0, whole, True)
+                cosine_pass(bank[:], 1, t, 0, whole, True)
+                nc.scalar.copy(wide[:, t, :], bank[:])
+            nc.sync.dma_start(out_rows[1, :, rows, whole], wide[:, rows, :])
+
+        wide_pair(0)
         cos3 = cosine(folded, second, "cos3", all_rows)
-        ys[1, 1] = unit(1, 1, "banks0", "wc_raw1")
+        wide_pair(1)
 
         features(2, cos2, "ds_raw1")
         ys[2, 0] = unit(2, 0, "banks1", "table2")
@@ -360,39 +377,43 @@ def tile_list_tile_location_codes_kernel(
         tags = {(0, 0): "table1", (0, 1): "cos3", (1, 0): "rounded2", (1, 1): "rounded3"}
         rounded = {key: keep.tile([P, HALF, PACK], BF16, name="rounded", tag=tags[key], align_bytes=64) for key in tags}
 
-        def round_y(engine_copy, c, g):
+        def round_y(engine_copy, c, g, cols=first):
             h, part = divmod(c, HALF // CHUNK)
             engine_copy(
-                rounded[h, g][:, (first, second)[part], :].rearrange("p (c i) t -> p c t i", i=4),
-                ys[c, g][:].rearrange("p t (c i) -> p c t i", i=4),
+                rounded[h, g][:, CHUNK * part + cols.start : CHUNK * part + cols.stop, :].rearrange("p (c i) t -> p c t i", i=4),
+                ys[c, g][:, :, cols].rearrange("p t (c i) -> p c t i", i=4),
             )
 
         def quantize_y(h, g, part):
             cols = slice(HALF * h + part.start, HALF * h + part.stop)
             quantize(y_codes[:, g, cols], y_plane[:, g, cols], rounded[h, g][:, part, :].rearrange("p n t -> p (n t)"))
 
-        def store_codes(h, g):
-            cols = slice(HALF * h, HALF * (h + 1))
+        def store_codes(h, g, part=whole):
+            cols = slice(HALF * h + part.start, HALF * h + part.stop)
             nc.sync.dma_start(out_words[:, g, cols], y_codes[:, g, cols])
 
-        round_y(nc.scalar.copy, 2, 0)
+        round_y(nc.scalar.copy, 2, 0, slice(0, P))
         ys[3, 0] = unit(3, 0, "banks0", "dc_raw")
         ys[3, 1] = unit(3, 1, "banks0", "ds_raw0")
         round_y(nc.vector.tensor_copy, 0, 0)
         round_y(nc.vector.tensor_copy, 1, 0)
-        round_y(nc.vector.tensor_copy, 0, 1)
+        round_y(nc.vector.tensor_copy, 2, 1)
         quantize_y(0, 0, whole)
         store_codes(0, 0)
-        round_y(nc.vector.tensor_copy, 1, 1)
-        round_y(nc.vector.tensor_copy, 2, 1)
+        nc.vector.tensor_copy(
+            rounded[0, 1][:].rearrange("p (c i) t -> p c t i", i=4), wide[:].rearrange("p t (c i) -> p c t i", i=4)
+        )
+        round_y(nc.vector.tensor_copy, 2, 0, slice(P, CHUNK))
+        quantize_y(1, 1, first)
         quantize_y(0, 1, whole)
         store_codes(0, 1)
+        store_codes(1, 1, first)
         round_y(nc.scalar.copy, 3, 0)
         round_y(nc.scalar.copy, 3, 1)
-        quantize_y(1, 1, first)
         quantize_y(1, 0, whole)
         store_codes(1, 0)
         quantize_y(1, 1, second)
-        store_codes(1, 1)
+        store_codes(1, 1, second)
         for r in range(4):
-            nc.sync.dma_start(out_planes[r], y_plane[r:P:QUAD, :, :].bitcast(I32))
+            queue = (nc.scalar, nc.sync)[r % 2]
+            queue.dma_start(out_planes[r], y_plane[r:P:QUAD, :, :].bitcast(I32))

@@ -304,8 +304,9 @@ def tile_list_tile_location_codes_kernel(
             for pair in range(PACK // 2):
                 for u in range(2):
                     cosine_pass(banks[pair][:, u, :], g, 2 * pair + u, c // 2, (first, second)[c % 2], u == 1)
-                nc.scalar.copy(y[:, 2 * pair : 2 * pair + 2, :], banks[pair][:])
-            nc.sync.dma_start(out_rows[g, :, :, CHUNK * c : CHUNK * (c + 1)], y[:])
+                rows = slice(2 * pair, 2 * pair + 2)
+                nc.scalar.copy(y[:, rows, :], banks[pair][:])
+                nc.sync.dma_start(out_rows[g, :, rows, CHUNK * c : CHUNK * (c + 1)], y[:, rows, :])
             return y
 
         def unit(c, g, banks, tag):
@@ -315,8 +316,9 @@ def tile_list_tile_location_codes_kernel(
                 for u in range(2):
                     sine_pass(bank[:, u, :], g, 2 * pair + u, c // 2, (first, second)[c % 2], True)
                     cosine_pass(bank[:, u, :], g, 2 * pair + u, c // 2, (first, second)[c % 2], True)
-                nc.scalar.copy(y[:, 2 * pair : 2 * pair + 2, :], bank[:])
-            nc.sync.dma_start(out_rows[g, :, :, CHUNK * c : CHUNK * (c + 1)], y[:])
+                rows = slice(2 * pair, 2 * pair + 2)
+                nc.scalar.copy(y[:, rows, :], bank[:])
+                nc.sync.dma_start(out_rows[g, :, rows, CHUNK * c : CHUNK * (c + 1)], y[:, rows, :])
             return y
 
         all_rows = (slice(0, PACK),)
@@ -363,7 +365,7 @@ def tile_list_tile_location_codes_kernel(
                 sine_pass(bank[:], 1, t, 0, whole, True)
                 cosine_pass(bank[:], 1, t, 0, whole, True)
                 nc.scalar.copy(wide[:, t, :], bank[:])
-            nc.sync.dma_start(out_rows[1, :, rows, whole], wide[:, rows, :])
+                nc.sync.dma_start(out_rows[1, :, t, whole], wide[:, t, :])
 
         wide_pair(0)
         cos3 = cosine(folded, second, "cos3", all_rows)

@@ -355,7 +355,7 @@ def tile_list_tile_location_codes_kernel(
         round_weight(nc.vector.tensor_copy, ds_dealt[:], ds_raw[1][:])
         deal_dc(1, "cos0")
         quantize_weight(ds_dealt, ds_codes[1], ds_planes[1])
-        cos2 = cosine(folded, first, "cos2", all_rows)
+        cos2 = cosine(folded, first, "cos2", (slice(0, 2), slice(2, PACK)))
         wide = keep.tile([P, PACK, HALF], F32, name="wide", tag="wc_raw0", align_bytes=64)
 
         def wide_pair(pair):
@@ -368,7 +368,7 @@ def tile_list_tile_location_codes_kernel(
                 nc.sync.dma_start(out_rows[1, :, t, whole], wide[:, t, :])
 
         wide_pair(0)
-        cos3 = cosine(folded, second, "cos3", all_rows)
+        cos3 = cosine(folded, second, "cos3", (slice(0, 2), slice(2, PACK)))
         wide_pair(1)
 
         features(2, cos2, "ds_raw1")
@@ -390,8 +390,7 @@ def tile_list_tile_location_codes_kernel(
             cols = slice(HALF * h + part.start, HALF * h + part.stop)
             quantize(y_codes[:, g, cols], y_plane[:, g, cols], rounded[h, g][:, part, :].rearrange("p n t -> p (n t)"))
 
-        def store_codes(h, g, part=whole):
-            cols = slice(HALF * h + part.start, HALF * h + part.stop)
+        def store_codes(g, cols):
             nc.sync.dma_start(out_words[:, g, cols], y_codes[:, g, cols])
 
         round_y(nc.scalar.copy, 2, 0, slice(0, P))
@@ -401,21 +400,23 @@ def tile_list_tile_location_codes_kernel(
         round_y(nc.vector.tensor_copy, 1, 0)
         round_y(nc.vector.tensor_copy, 2, 1)
         quantize_y(0, 0, whole)
-        store_codes(0, 0)
+        store_codes(0, whole)
         nc.vector.tensor_copy(
             rounded[0, 1][:].rearrange("p (c i) t -> p c t i", i=4), wide[:].rearrange("p t (c i) -> p c t i", i=4)
         )
         round_y(nc.vector.tensor_copy, 2, 0, slice(P, CHUNK))
         quantize_y(1, 1, first)
         quantize_y(0, 1, whole)
-        store_codes(0, 1)
-        store_codes(1, 1, first)
+        store_codes(1, slice(0, S - CHUNK))
         round_y(nc.scalar.copy, 3, 0)
-        round_y(nc.scalar.copy, 3, 1)
+        pieces = (slice(0, P), slice(P, CHUNK))
+        for piece in pieces:
+            round_y(nc.scalar.copy, 3, 1, piece)
         quantize_y(1, 0, whole)
-        store_codes(1, 0)
-        quantize_y(1, 1, second)
-        store_codes(1, 1, second)
+        store_codes(0, slice(HALF, S))
+        for piece in pieces:
+            quantize_y(1, 1, slice(CHUNK + piece.start, CHUNK + piece.stop))
+            store_codes(1, slice(S - CHUNK + piece.start, S - CHUNK + piece.stop))
         for r in range(4):
             queue = (nc.scalar, nc.sync)[r % 2]
             queue.dma_start(out_planes[r], y_plane[r:P:QUAD, :, :].bitcast(I32))

@@ -27,11 +27,11 @@ GROUPS = N // SPAN
 HALF = 512
 CHUNK = 256
 HALVES = S // HALF
-CHUNKS = S // CHUNK
 STAGE_BASES = (48, 96, 112)
 MOVES_PER_RUN = 6
 TABLE_LEAD = 7 * T // 16
 VECTOR_SHARE = 80
+PIECE = 128
 
 
 def tile_list_tile_location_codes_kernel(
@@ -40,6 +40,9 @@ def tile_list_tile_location_codes_kernel(
 ):
     nc = tc.nc
     first, second, whole = slice(0, CHUNK), slice(CHUNK, HALF), slice(0, HALF)
+    parts = (first, second)
+    pieces = (slice(0, PIECE), slice(PIECE, CHUNK))
+    row_pairs = (slice(0, 2), slice(2, PACK))
 
     with ExitStack() as ctx:
         keep = ctx.enter_context(tc.tile_pool(name="keep", bufs=1))
@@ -119,10 +122,10 @@ def tile_list_tile_location_codes_kernel(
                 both = keep.tile([P, S], U32, name="picked%d" % a, align_bytes=64)
                 nc.vector.tensor_copy(both[:], window.indirect(offsets[:]))
                 return [both[:, HALF * h : HALF * (h + 1)] for h in range(HALVES)]
-            parts = [keep.tile([P, HALF], U32, name="picked_last%d" % h, align_bytes=64) for h in range(HALVES)]
+            halves = [keep.tile([P, HALF], U32, name="picked_last%d" % h, align_bytes=64) for h in range(HALVES)]
             for h in range(HALVES):
-                nc.vector.tensor_copy(parts[h][:], window.indirect(offsets[:, HALF // 16 * h : HALF // 16 * (h + 1)]))
-            return [part[:] for part in parts]
+                nc.vector.tensor_copy(halves[h][:], window.indirect(offsets[:, HALF // 16 * h : HALF // 16 * (h + 1)]))
+            return [half[:] for half in halves]
 
         def angle_pass(bank, lhsT, lhsT_scale, a, h, last):
             nc.tensor.matmul_mx(
@@ -165,6 +168,7 @@ def tile_list_tile_location_codes_kernel(
 
         def feature_operand(branch, h, cols):
             return h_codes[h][:, branch, cols], h_planes[h][:, branch, cols]
+
         sines = [keep.tile([P, PACK, HALF], F32, name="sines%d" % h, tag="table%d" % h, align_bytes=64) for h in range(HALVES)]
 
         def quantize(codes, plane, values):
@@ -194,7 +198,7 @@ def tile_list_tile_location_codes_kernel(
             )
 
         def quantize_feat(feat, c, branch):
-            codes, plane = feature_operand(branch, c // 2, (first, second)[c % 2])
+            codes, plane = feature_operand(branch, c // 2, parts[c % 2])
             quantize(codes, plane, feat.rearrange("p n t -> p (n t)"))
 
         for h in range(HALVES):
@@ -255,9 +259,9 @@ def tile_list_tile_location_codes_kernel(
         def features(c, cosines, tag):
             h, part = divmod(c, HALF // CHUNK)
             feat = feat_tile(2 * CHUNK, tag)
-            apply_gain(feat[:, first, :], sines[h][:, :, (first, second)[part]], gs_sb)
+            apply_gain(feat[:, first, :], sines[h][:, :, parts[part]], gs_sb)
             apply_gain(feat[:, second, :], cosines[:], gc_sb)
-            for branch, cols in enumerate((first, second)):
+            for branch, cols in enumerate(parts):
                 quantize_feat(feat[:, cols, :], c, branch)
 
         ds_codes = [keep.tile([P, SPAN], U32, name="ds_codes%d" % g, align_bytes=64) for g in range(GROUPS)]
@@ -296,27 +300,35 @@ def tile_list_tile_location_codes_kernel(
         def open_unit(c, g, tag):
             banks = [psum.tile([P, 2, CHUNK], F32, name="bank", tag=tag) for pair in range(PACK // 2)]
             for t in range(PACK):
-                sine_pass(banks[t // 2][:, t % 2, :], g, t, c // 2, (first, second)[c % 2], t % 2 == 0)
+                sine_pass(banks[t // 2][:, t % 2, :], g, t, c // 2, parts[c % 2], t % 2 == 0)
             return banks
 
         def close_unit(c, g, banks, tag):
             y = keep.tile([P, PACK, CHUNK], F32, name="y", tag=tag, align_bytes=64)
             for pair in range(PACK // 2):
                 for u in range(2):
-                    cosine_pass(banks[pair][:, u, :], g, 2 * pair + u, c // 2, (first, second)[c % 2], u == 1)
-                rows = slice(2 * pair, 2 * pair + 2)
+                    cosine_pass(banks[pair][:, u, :], g, 2 * pair + u, c // 2, parts[c % 2], u == 1)
+                rows = row_pairs[pair]
                 nc.scalar.copy(y[:, rows, :], banks[pair][:])
                 nc.sync.dma_start(out_rows[g, :, rows, CHUNK * c : CHUNK * (c + 1)], y[:, rows, :])
             return y
 
+        def pair_banks(tag):
+            return [psum.tile([P, 2, CHUNK], F32, name="bank", tag=tag) for pair in range(PACK // 2)]
+
+        def warm_up(bank):
+            nc.tensor.matmul_mx(
+                out=bank, lhsT=wc_codes[0][:, :P].bitcast(FP8X4), lhsT_scale=wc_planes[0][:, :P],
+                rhs=picked[0][0].bitcast(FP8X4), rhs_scale=planes[0][:, :HALF], start=True, stop=True,
+            )
+
         def unit(c, g, banks, tag):
             y = keep.tile([P, PACK, CHUNK], F32, name="y", tag=tag, align_bytes=64)
-            for pair in range(PACK // 2):
-                bank = psum.tile([P, 2, CHUNK], F32, name="bank", tag=banks)
+            for pair, bank in enumerate(banks):
                 for u in range(2):
-                    sine_pass(bank[:, u, :], g, 2 * pair + u, c // 2, (first, second)[c % 2], True)
-                    cosine_pass(bank[:, u, :], g, 2 * pair + u, c // 2, (first, second)[c % 2], True)
-                rows = slice(2 * pair, 2 * pair + 2)
+                    sine_pass(bank[:, u, :], g, 2 * pair + u, c // 2, parts[c % 2], True)
+                    cosine_pass(bank[:, u, :], g, 2 * pair + u, c // 2, parts[c % 2], True)
+                rows = row_pairs[pair]
                 nc.scalar.copy(y[:, rows, :], bank[:])
                 nc.sync.dma_start(out_rows[g, :, rows, CHUNK * c : CHUNK * (c + 1)], y[:, rows, :])
             return y
@@ -324,7 +336,7 @@ def tile_list_tile_location_codes_kernel(
         all_rows = (slice(0, PACK),)
         folded = keep.tile([P, PACK, HALF], F32, name="folded0", align_bytes=64)
         fold(folded, 0, first)
-        cos0 = cosine(folded, first, "cos0", (slice(0, 2), slice(2, PACK)))
+        cos0 = cosine(folded, first, "cos0", row_pairs)
         fold(folded, 0, second)
         cos1 = cosine(folded, second, "cos1", all_rows)
         hs0 = early[:, 0, :].rearrange("p (n t) -> p n t", t=PACK)
@@ -334,57 +346,61 @@ def tile_list_tile_location_codes_kernel(
         quantize_feat(hs0, 0, 0)
         quantize_weight(ds_dealt, ds_codes[0], ds_planes[0])
         lead_banks = open_unit(0, 0, "banks0")
+        next_banks = pair_banks("banks0")
+        warm_up(next_banks[0][:].rearrange("p u n -> p (u n)"))
         hc0 = feat_tile(CHUNK, "wc_dealt1")
         apply_gain(hc0[:], cos0[:], gc_sb)
         deal_dc(0, "wc_dealt0")
         quantize_feat(hc0[:], 0, 1)
         ys = {}
         ys[0, 0] = close_unit(0, 0, lead_banks, "y0")
+        wide_banks = [psum.tile([P, HALF], F32, name="bank", tag="banks0") for t in range(2)]
+        for bank in wide_banks:
+            warm_up(bank[:])
 
         feat1 = feat_tile(2 * CHUNK, "cos0")
         nc.vector.tensor_copy(
             feat1[:, first, :].rearrange("p (c i) t -> p c t i", i=4), hs1_rows.rearrange("p t (c i) -> p c t i", i=4)
         )
         apply_gain(feat1[:, second, :], cos1[:], gc_sb)
-        for branch, cols in enumerate((first, second)):
+        for branch, cols in enumerate(parts):
             quantize_feat(feat1[:, cols, :], 1, branch)
         folded = keep.tile([P, PACK, HALF], F32, name="folded1", tag="wc_dealt1", align_bytes=64)
         fold(folded, 1, whole)
-        ys[1, 0] = unit(1, 0, "banks0", "y1")
+        ys[1, 0] = unit(1, 0, next_banks, "y1")
         ds_dealt = dealt_tile("cos1")
         round_weight(nc.vector.tensor_copy, ds_dealt[:], ds_raw[1][:])
         deal_dc(1, "cos0")
         quantize_weight(ds_dealt, ds_codes[1], ds_planes[1])
-        cos2 = cosine(folded, first, "cos2", (slice(0, 2), slice(2, PACK)))
+        cos2 = cosine(folded, first, "cos2", row_pairs)
         wide = keep.tile([P, PACK, HALF], F32, name="wide", tag="wc_raw0", align_bytes=64)
 
-        def wide_pair(pair):
-            rows = slice(2 * pair, 2 * pair + 2)
-            for t in range(rows.start, rows.stop):
-                bank = psum.tile([P, HALF], F32, name="bank", tag="banks0")
+        def wide_rows(rows, banks):
+            for t, bank in zip(range(rows.start, rows.stop), banks):
                 sine_pass(bank[:], 1, t, 0, whole, True)
                 cosine_pass(bank[:], 1, t, 0, whole, True)
                 nc.scalar.copy(wide[:, t, :], bank[:])
                 nc.sync.dma_start(out_rows[1, :, t, whole], wide[:, t, :])
 
-        wide_pair(0)
-        cos3 = cosine(folded, second, "cos3", (slice(0, 2), slice(2, PACK)))
-        wide_pair(1)
+        wide_rows(row_pairs[0], wide_banks)
+        cos3 = cosine(folded, second, "cos3", row_pairs)
+        wide_rows(row_pairs[1], [psum.tile([P, HALF], F32, name="bank", tag="banks0") for t in range(2)])
 
         features(2, cos2, "ds_raw1")
-        ys[2, 0] = unit(2, 0, "banks1", "table2")
-        ys[2, 1] = unit(2, 1, "banks1", "tab_rows")
+        ys[2, 0] = unit(2, 0, pair_banks("banks1"), "table2")
+        ys[2, 1] = unit(2, 1, pair_banks("banks1"), "tab_rows")
         features(3, cos3, "cos2")
 
         tags = {(0, 0): "table1", (0, 1): "cos3", (1, 0): "rounded2", (1, 1): "rounded3"}
         rounded = {key: keep.tile([P, HALF, PACK], BF16, name="rounded", tag=tags[key], align_bytes=64) for key in tags}
 
-        def round_y(engine_copy, c, g, cols=first):
+        def round_rows(engine_copy, words, rows):
+            engine_copy(words.rearrange("p (c i) t -> p c t i", i=4), rows.rearrange("p t (c i) -> p c t i", i=4))
+
+        def round_y(engine_copy, c, g, cols=slice(0, CHUNK)):
             h, part = divmod(c, HALF // CHUNK)
-            engine_copy(
-                rounded[h, g][:, CHUNK * part + cols.start : CHUNK * part + cols.stop, :].rearrange("p (c i) t -> p c t i", i=4),
-                ys[c, g][:, :, cols].rearrange("p t (c i) -> p c t i", i=4),
-            )
+            base = CHUNK * part
+            round_rows(engine_copy, rounded[h, g][:, base + cols.start : base + cols.stop, :], ys[c, g][:, :, cols])
 
         def quantize_y(h, g, part):
             cols = slice(HALF * h + part.start, HALF * h + part.stop)
@@ -393,23 +409,20 @@ def tile_list_tile_location_codes_kernel(
         def store_codes(g, cols):
             nc.sync.dma_start(out_words[:, g, cols], y_codes[:, g, cols])
 
-        round_y(nc.scalar.copy, 2, 0, slice(0, P))
-        ys[3, 0] = unit(3, 0, "banks0", "dc_raw")
-        ys[3, 1] = unit(3, 1, "banks0", "ds_raw0")
+        round_y(nc.scalar.copy, 2, 0, pieces[0])
+        ys[3, 0] = unit(3, 0, pair_banks("banks0"), "dc_raw")
+        ys[3, 1] = unit(3, 1, pair_banks("banks0"), "ds_raw0")
         round_y(nc.vector.tensor_copy, 0, 0)
         round_y(nc.vector.tensor_copy, 1, 0)
         round_y(nc.vector.tensor_copy, 2, 1)
         quantize_y(0, 0, whole)
         store_codes(0, whole)
-        nc.vector.tensor_copy(
-            rounded[0, 1][:].rearrange("p (c i) t -> p c t i", i=4), wide[:].rearrange("p t (c i) -> p c t i", i=4)
-        )
-        round_y(nc.vector.tensor_copy, 2, 0, slice(P, CHUNK))
+        round_rows(nc.vector.tensor_copy, rounded[0, 1][:], wide[:])
+        round_y(nc.vector.tensor_copy, 2, 0, pieces[1])
         quantize_y(1, 1, first)
         quantize_y(0, 1, whole)
         store_codes(1, slice(0, S - CHUNK))
         round_y(nc.scalar.copy, 3, 0)
-        pieces = (slice(0, P), slice(P, CHUNK))
         for piece in pieces:
             round_y(nc.scalar.copy, 3, 1, piece)
         quantize_y(1, 0, whole)

import math
from contextlib import ExitStack

import concourse.mybir as mybir

K, T, S, H, N = 1536, 4096, 1024, 512, 1024
FLOPS = 2 * (2 * K * H * S + 2 * H * N * S)

F32 = mybir.dt.float32
BF16 = mybir.dt.bfloat16
I32 = mybir.dt.int32
U32 = mybir.dt.uint32
U16 = mybir.dt.uint16
U8 = mybir.dt.uint8
FP8X4 = mybir.dt.float8_e4m3fn_x4
FP4X4 = mybir.dt.float4_e2m1fn_x4
ACT = mybir.ActivationFunctionType
ALU = mybir.AluOpType

P = 128
PACK = 4
SPAN = P * PACK
BLOCKS = SPAN // 32
QUAD = 32
PASSES = K // SPAN
GROUPS = N // SPAN
HALF = 512
CHUNK = 256
HALVES = S // HALF
STAGE_BASES = (48, 96, 112)
MOVES_PER_RUN = 6
TABLE_LEAD = 7 * T // 16
VECTOR_SHARE = 80
PIECE = 128


def tile_list_tile_location_codes_kernel(
    tc, tab_words, tab_scales, offs, ws_words, ws_scales, wc, phase, gs, gc, ds, dc_words, dc_scales,
    out_0, out_1, out_2,
):
    nc = tc.nc
    first, second, whole = slice(0, CHUNK), slice(CHUNK, HALF), slice(0, HALF)
    parts = (first, second)
    pieces = (slice(0, PIECE), slice(PIECE, CHUNK))
    row_pairs = (slice(0, 2), slice(2, PACK))

    with ExitStack() as ctx:
        keep = ctx.enter_context(tc.tile_pool(name="keep", bufs=1))
        psum = ctx.enter_context(tc.psum_pool(name="psum", bufs=PACK))

        offsets = keep.tile([P, S // 16], U16, name="offsets")
        nc.sync.dma_start(offsets[:], offs)

        ws_rows = keep.tile([P, PASSES, H], U8, name="ws_rows", tag="ws_rows", align_bytes=64)
        nc.vector.memset(ws_rows[:].bitcast(I32), 0)
        tab_flat = tab_scales.rearrange("a q t -> (a q) t").bitcast(I32)
        tab_rows = keep.tile([P, T], U8, name="tab_rows", align_bytes=64)
        nc.sync.dma_start(tab_rows[STAGE_BASES[1] :, :].bitcast(I32), tab_flat[BLOCKS:, :])
        nc.sync.dma_start(tab_rows[STAGE_BASES[0] : STAGE_BASES[0] + BLOCKS, :].bitcast(I32), tab_flat[:BLOCKS, :])
        ws_by_row = ws_scales.rearrange("a (q r) c -> r q a c", r=4).bitcast(I32)
        for r in range(4):
            nc.sync.dma_start(ws_rows[r:P:QUAD, :, :].bitcast(I32), ws_by_row[r])
        dc_rows = keep.tile([P, N], U8, name="dc_rows", align_bytes=64)
        planes = [keep.tile([P, S], U8, name="plane%d" % a, align_bytes=64) for a in range(PASSES)]
        nc.vector.memset(tab_rows[: STAGE_BASES[0], :].bitcast(I32), 0)
        nc.vector.memset(tab_rows[STAGE_BASES[0] + BLOCKS : STAGE_BASES[1], :].bitcast(I32), 0)
        for plane in planes:
            nc.vector.memset(plane[:].bitcast(I32), 0)
        nc.vector.memset(dc_rows[: P - BLOCKS, :].bitcast(I32), 0)

        table = [keep.tile([P, T], I32, name="table%d" % a, tag="table%d" % a, align_bytes=64) for a in range(PASSES)]

        def load_table(a, cols):
            nc.sync.dma_start(table[a][:, cols], tab_words[a].rearrange("p t i -> p (t i)").bitcast(I32)[:, cols])

        load_table(0, slice(0, T))
        nc.sync.dma_start(dc_rows[P - BLOCKS :, :].bitcast(I32), dc_scales[0].bitcast(I32))
        ws_raw = keep.tile([P, PASSES, 2 * H], U8, name="ws_raw", align_bytes=64)
        nc.sync.dma_start(ws_raw[:].bitcast(I32), ws_words.rearrange("a p c -> p a c").bitcast(I32))
        load_table(1, slice(0, TABLE_LEAD))

        picked_rows = keep.tile([P, S], U8, name="picked_rows", align_bytes=64)
        ws_planes = keep.tile([P, PASSES, H], U8, name="ws_planes", align_bytes=64)
        dc_staged = keep.tile([P, N], U8, name="dc_staged", align_bytes=64)
        nc.vector.tensor_copy(picked_rows[:], tab_rows[:].indirect(offsets[:]))
        moves = [(a, r) for a in range(PASSES) for r in range(4)]
        for run, rest in enumerate((slice(TABLE_LEAD, T), slice(0, T))):
            for a, r in moves[MOVES_PER_RUN * run : MOVES_PER_RUN * (run + 1)]:
                base = STAGE_BASES[a]
                nc.sync.dma_start(
                    planes[a][r:P:QUAD, :].bitcast(I32), picked_rows[base + r : base + BLOCKS : 4, :].bitcast(I32)
                )
            load_table(run + 1, rest)
        for a in range(PASSES):
            nc.vector.tensor_copy(
                ws_planes[:, a, :].rearrange("p (t m) -> p t m", t=PACK), ws_rows[:, a, :].rearrange("p (m t) -> p t m", t=PACK)
            )
        nc.vector.tensor_copy(
            dc_staged[:].rearrange("p (g t m) -> p g t m", g=GROUPS, t=PACK),
            dc_rows[:].rearrange("p (g m t) -> p g t m", g=GROUPS, t=PACK),
        )

        dc_plane = keep.tile([P, N], U8, name="dc_plane", tag="ws_rows", align_bytes=64)
        nc.vector.memset(dc_plane[:].bitcast(I32), 0)

        gs_sb = keep.tile([P, PACK], F32, name="gs_sb")
        gc_sb = keep.tile([P, PACK], F32, name="gc_sb")
        phase_sb = keep.tile([P, PACK], F32, name="phase_sb")

        ws_codes = keep.tile([P, PASSES, 2 * H], U8, name="ws_codes", align_bytes=64)
        for a in range(PASSES):
            nc.vector.tensor_copy(
                ws_codes[:, a, :].bitcast(U16).rearrange("p (t m) -> p t m", t=PACK),
                ws_raw[:, a, :].bitcast(U16).rearrange("p (m t) -> p t m", t=PACK),
            )

        picked = []

        def gather_words(a):
            window = table[a][:].bitcast(U32)
            if a + 1 < PASSES:
                both = keep.tile([P, S], U32, name="picked%d" % a, align_bytes=64)
                nc.vector.tensor_copy(both[:], window.indirect(offsets[:]))
                return [both[:, HALF * h : HALF * (h + 1)] for h in range(HALVES)]
            halves = [keep.tile([P, HALF], U32, name="picked_last%d" % h, align_bytes=64) for h in range(HALVES)]
            for h in range(HALVES):
                nc.vector.tensor_copy(halves[h][:], window.indirect(offsets[:, HALF // 16 * h : HALF // 16 * (h + 1)]))
            return [half[:] for half in halves]

        def angle_pass(bank, lhsT, lhsT_scale, a, h, last):
            nc.tensor.matmul_mx(
                out=bank[:], lhsT=lhsT, lhsT_scale=lhsT_scale,
                rhs=picked[a][h].bitcast(FP8X4), rhs_scale=planes[a][:, HALF * h : HALF * (h + 1)],
                start=(a == 0), stop=(a == last),
            )

        sin_banks = [[psum.tile([P, HALF], F32, name="bank", tag="banks%d" % h) for t in range(PACK)] for h in range(HALVES)]
        for a in range(PASSES):
            picked.append(gather_words(a))
            for h in range(HALVES):
                for t in range(PACK):
                    angle_pass(
                        sin_banks[h][t], ws_codes[:, a, 2 * P * t : 2 * P * (t + 1)].bitcast(FP4X4),
                        ws_planes[:, a, P * t : P * (t + 1)], a, h, PASSES - 1,
                    )

        def load_weight(rows, name):
            raw = keep.tile([P, PACK, SPAN], F32, name=name, tag=name, align_bytes=64)
            nc.sync.dma_start(raw[:], rows.rearrange("(p j) c -> p j c", j=PACK))
            return raw

        wc_raw = [load_weight(wc[SPAN * a : SPAN * (a + 1), :], "wc_raw%d" % a) for a in range(PASSES)]
        nc.sync.dma_start(gs_sb[:], gs.rearrange("(p t) -> p t", t=PACK))
        nc.sync.dma_start(phase_sb[:], phase.rearrange("(p t) -> p t", t=PACK))
        ds_raw = [load_weight(ds[:, :SPAN], "ds_raw0")]
        dc_raw = keep.tile([P, N], I32, name="dc_raw", align_bytes=64)
        nc.sync.dma_start(dc_raw[:], dc_words[0].rearrange("p c i -> p (c i)").bitcast(I32))
        nc.sync.dma_start(gc_sb[:], gc.rearrange("(p t) -> p t", t=PACK))
        for r in range(4):
            nc.sync.dma_start(dc_plane[r:P:QUAD, :].bitcast(I32), dc_staged[P - BLOCKS + r : P : 4, :].bitcast(I32))
        ds_raw.append(load_weight(ds[:, SPAN:], "ds_raw1"))

        wc_codes = [keep.tile([P, H], U32, name="wc_codes%d" % a, align_bytes=64) for a in range(PASSES)]
        wc_planes = [keep.tile([P, H], U8, name="wc_plane%d" % a, align_bytes=64) for a in range(PASSES)]
        code_tags = ("ds_raw0", "h_codes1")
        h_codes = [keep.tile([P, 2, HALF], U32, name="h_codes", tag=tag, align_bytes=64) for tag in code_tags]
        h_planes = [keep.tile([P, 2, HALF], U8, name="h_plane%d" % h, align_bytes=64) for h in range(HALVES)]

        def feature_operand(branch, h, cols):
            return h_codes[h][:, branch, cols], h_planes[h][:, branch, cols]

        sines = [keep.tile([P, PACK, HALF], F32, name="sines%d" % h, tag="table%d" % h, align_bytes=64) for h in range(HALVES)]

        def quantize(codes, plane, values):
            nc.vector.quantize_mx(out=codes.bitcast(FP8X4), scales=plane, in_=values)

        def dealt_tile(tag):
            return keep.tile([P, PACK, P, PACK], BF16, name="dealt", tag=tag, align_bytes=64)

        def round_weight(engine_copy, dealt, raw):
            engine_copy(
                dealt.rearrange("p (u e) m j -> p u m j e", e=2),
                raw.rearrange("p j (m u e) -> p u m j e", u=2, e=2),
            )

        def quantize_weight(dealt, codes, plane):
            quantize(codes[:], plane[:], dealt[:].rearrange("p t m j -> p (t m j)"))

        def feat_tile(width, tag):
            return keep.tile([P, width, PACK], BF16, name="feat", tag=tag, align_bytes=64)

        def apply_gain(feat, values, gain):
            nc.vector.tensor_tensor(
                feat.rearrange("p (c i) t -> p c t i", i=2),
                values.rearrange("p t (c i) -> p c t i", i=2),
                gain[:].unsqueeze(1).unsqueeze(3).to_broadcast([P, CHUNK // 2, PACK, 2]),
                ALU.mult,
            )

        def quantize_feat(feat, c, branch):
            codes, plane = feature_operand(branch, c // 2, parts[c % 2])
            quantize(codes, plane, feat.rearrange("p n t -> p (n t)"))

        for h in range(HALVES):
            for t in range(PACK):
                nc.scalar.activation(sines[h][:, t, :], sin_banks[h][t][:], ACT.Sin)

        wc_dealt = [dealt_tile(tag) for tag in ("wc_dealt0", "wc_dealt1", "lead")]

        def quantize_wc(a):
            for u in range(2):
                cols = slice(2 * P * u, 2 * P * (u + 1))
                pair = wc_dealt[a][:, 2 * u : 2 * u + 2].rearrange("p e m j -> p (e m j)")
                quantize(wc_codes[a][:, cols], wc_planes[a][:, cols], pair)

        for a in range(PASSES - 1):
            for u in range(2):
                nc.vector.tensor_copy(
                    wc_dealt[a][:, 2 * u : 2 * u + 2].rearrange("p e m j -> p m j e"),
                    wc_raw[a][:].rearrange("p j (m u e) -> p u m j e", u=2, e=2)[:, u],
                )
            quantize_wc(a)
        round_weight(nc.vector.tensor_copy, wc_dealt[-1][:, :, :VECTOR_SHARE, :], wc_raw[-1][:, :, : PACK * VECTOR_SHARE])
        round_weight(nc.scalar.copy, wc_dealt[-1][:, :, VECTOR_SHARE:, :], wc_raw[-1][:, :, PACK * VECTOR_SHARE :])
        quantize_wc(PASSES - 1)
        early = keep.tile([P, 2, PACK * CHUNK], BF16, name="early", tag="wc_raw2", align_bytes=64)
        hs1_rows = early[:, 1, :].rearrange("p (t n) -> p t n", t=PACK)
        for t in range(PACK):
            nc.scalar.activation(hs1_rows[:, t, :], sines[0][:, t, second], ACT.Copy, scale=gs_sb[:, t : t + 1])

        cos_banks = [[None] * PACK for h in range(HALVES)]

        def cos_pass(a, h, last):
            for t in range(PACK):
                if a == 0:
                    cos_banks[h][t] = psum.tile([P, HALF], F32, name="bank", tag="banks%d" % h)
                angle_pass(
                    cos_banks[h][t], wc_codes[a][:, P * t : P * (t + 1)].bitcast(FP8X4),
                    wc_planes[a][:, P * t : P * (t + 1)], a, h, last,
                )

        for h in range(HALVES):
            cos_pass(0, h, None)
        for a in (1, 2):
            cos_pass(a, 0, 2)
        for a in (2, 1):
            cos_pass(a, 1, 1)

        def fold(folded, h, cols):
            for t in range(PACK):
                nc.scalar.activation(folded[:, t, cols], cos_banks[h][t][:, cols], ACT.Abs, bias=phase_sb[:, t : t + 1])

        def cosine(folded, cols, tag, row_runs):
            cosines = keep.tile([P, PACK, CHUNK], F32, name="cosines", tag=tag, align_bytes=64)
            for rows in row_runs:
                nc.scalar.activation(cosines[:, rows, :], folded[:, rows, cols], ACT.Sin, bias=math.pi / 2, scale=-1.0)
            return cosines

        def features(c, cosines, tag):
            h, part = divmod(c, HALF // CHUNK)
            feat = feat_tile(2 * CHUNK, tag)
            apply_gain(feat[:, first, :], sines[h][:, :, parts[part]], gs_sb)
            apply_gain(feat[:, second, :], cosines[:], gc_sb)
            for branch, cols in enumerate(parts):
                quantize_feat(feat[:, cols, :], c, branch)

        ds_codes = [keep.tile([P, SPAN], U32, name="ds_codes%d" % g, align_bytes=64) for g in range(GROUPS)]
        ds_planes = [keep.tile([P, SPAN], U8, name="ds_plane%d" % g, align_bytes=64) for g in range(GROUPS)]
        dc_codes = []
        y_codes = keep.tile([P, GROUPS, S], I32, name="y_codes", align_bytes=64)
        y_plane = keep.tile([P, GROUPS, S], U8, name="y_plane", align_bytes=64)

        def deal_dc(g, tag):
            dc_codes.append(keep.tile([P, SPAN], I32, name="dc_codes%d" % g, tag=tag, align_bytes=64))
            nc.vector.tensor_copy(
                dc_codes[g][:].rearrange("p (u e m) -> p u m e", u=2, e=2),
                dc_raw[:, SPAN * g : SPAN * (g + 1)].rearrange("p (m u e) -> p u m e", u=2, e=2),
            )

        out_rows = out_0.rearrange("(g p t) j -> g p t j", g=GROUPS, t=PACK)
        out_words = out_1.rearrange("g p m t -> p g (m t)").bitcast(I32)
        out_planes = out_2.rearrange("g (q r) m -> r q g m", r=4).bitcast(I32)

        def sine_pass(out, g, t, h, cols, start):
            places = slice(P * t, P * (t + 1))
            codes, plane = feature_operand(0, h, cols)
            nc.tensor.matmul_mx(
                out=out, lhsT=ds_codes[g][:, places].bitcast(FP8X4), lhsT_scale=ds_planes[g][:, places],
                rhs=codes.bitcast(FP8X4), rhs_scale=plane, start=start, stop=False,
            )

        def cosine_pass(out, g, t, h, cols, stop):
            codes, plane = feature_operand(1, h, cols)
            nc.tensor.matmul_mx(
                out=out, lhsT=dc_codes[g][:, P * t : P * (t + 1)].bitcast(FP8X4),
                lhsT_scale=dc_plane[:, SPAN * g + P * t : SPAN * g + P * (t + 1)],
                rhs=codes.bitcast(FP8X4), rhs_scale=plane, start=False, stop=stop,
            )

        def open_unit(c, g, tag):
            banks = [psum.tile([P, 2, CHUNK], F32, name="bank", tag=tag) for pair in range(PACK // 2)]
            for t in range(PACK):
                sine_pass(banks[t // 2][:, t % 2, :], g, t, c // 2, parts[c % 2], t % 2 == 0)
            return banks

        def close_unit(c, g, banks, tag):
            y = keep.tile([P, PACK, CHUNK], F32, name="y", tag=tag, align_bytes=64)
            for pair in range(PACK // 2):
                for u in range(2):
                    cosine_pass(banks[pair][:, u, :], g, 2 * pair + u, c // 2, parts[c % 2], u == 1)
                rows = row_pairs[pair]
                nc.scalar.copy(y[:, rows, :], banks[pair][:])
                nc.sync.dma_start(out_rows[g, :, rows, CHUNK * c : CHUNK * (c + 1)], y[:, rows, :])
            return y

        def pair_banks(tag):
            return [psum.tile([P, 2, CHUNK], F32, name="bank", tag=tag) for pair in range(PACK // 2)]

        def warm_up(bank):
            nc.tensor.matmul_mx(
                out=bank, lhsT=wc_codes[0][:, :P].bitcast(FP8X4), lhsT_scale=wc_planes[0][:, :P],
                rhs=picked[0][0].bitcast(FP8X4), rhs_scale=planes[0][:, :HALF], start=True, stop=True,
            )

        def unit(c, g, banks, tag):
            y = keep.tile([P, PACK, CHUNK], F32, name="y", tag=tag, align_bytes=64)
            for pair, bank in enumerate(banks):
                for u in range(2):
                    sine_pass(bank[:, u, :], g, 2 * pair + u, c // 2, parts[c % 2], True)
                    cosine_pass(bank[:, u, :], g, 2 * pair + u, c // 2, parts[c % 2], True)
                rows = row_pairs[pair]
                nc.scalar.copy(y[:, rows, :], bank[:])
                nc.sync.dma_start(out_rows[g, :, rows, CHUNK * c : CHUNK * (c + 1)], y[:, rows, :])
            return y

        all_rows = (slice(0, PACK),)
        folded = keep.tile([P, PACK, HALF], F32, name="folded0", align_bytes=64)
        fold(folded, 0, first)
        cos0 = cosine(folded, first, "cos0", row_pairs)
        fold(folded, 0, second)
        cos1 = cosine(folded, second, "cos1", all_rows)
        hs0 = early[:, 0, :].rearrange("p (n t) -> p n t", t=PACK)
        apply_gain(hs0, sines[0][:, :, first], gs_sb)
        ds_dealt = dealt_tile("lead")
        round_weight(nc.vector.tensor_copy, ds_dealt[:], ds_raw[0][:])
        quantize_feat(hs0, 0, 0)
        quantize_weight(ds_dealt, ds_codes[0], ds_planes[0])
        lead_banks = open_unit(0, 0, "banks0")
        next_banks = pair_banks("banks0")
        warm_up(next_banks[0][:].rearrange("p u n -> p (u n)"))
        hc0 = feat_tile(CHUNK, "wc_dealt1")
        apply_gain(hc0[:], cos0[:], gc_sb)
        deal_dc(0, "wc_dealt0")
        quantize_feat(hc0[:], 0, 1)
        ys = {}
        ys[0, 0] = close_unit(0, 0, lead_banks, "y0")
        wide_banks = [psum.tile([P, HALF], F32, name="bank", tag="banks0") for t in range(2)]
        for bank in wide_banks:
            warm_up(bank[:])

        feat1 = feat_tile(2 * CHUNK, "cos0")
        nc.vector.tensor_copy(
            feat1[:, first, :].rearrange("p (c i) t -> p c t i", i=4), hs1_rows.rearrange("p t (c i) -> p c t i", i=4)
        )
        apply_gain(feat1[:, second, :], cos1[:], gc_sb)
        for branch, cols in enumerate(parts):
            quantize_feat(feat1[:, cols, :], 1, branch)
        folded = keep.tile([P, PACK, HALF], F32, name="folded1", tag="wc_dealt1", align_bytes=64)
        fold(folded, 1, whole)
        ys[1, 0] = unit(1, 0, next_banks, "y1")
        ds_dealt = dealt_tile("cos1")
        round_weight(nc.vector.tensor_copy, ds_dealt[:], ds_raw[1][:])
        deal_dc(1, "cos0")
        quantize_weight(ds_dealt, ds_codes[1], ds_planes[1])
        cos2 = cosine(folded, first, "cos2", row_pairs)
        wide = keep.tile([P, PACK, HALF], F32, name="wide", tag="wc_raw0", align_bytes=64)

        def wide_rows(rows, banks):
            for t, bank in zip(range(rows.start, rows.stop), banks):
                sine_pass(bank[:], 1, t, 0, whole, True)
                cosine_pass(bank[:], 1, t, 0, whole, True)
                nc.scalar.copy(wide[:, t, :], bank[:])
                nc.sync.dma_start(out_rows[1, :, t, whole], wide[:, t, :])

        wide_rows(row_pairs[0], wide_banks)
        cos3 = cosine(folded, second, "cos3", row_pairs)
        wide_rows(row_pairs[1], [psum.tile([P, HALF], F32, name="bank", tag="banks0") for t in range(2)])

        features(2, cos2, "ds_raw1")
        ys[2, 0] = unit(2, 0, pair_banks("banks1"), "table2")
        ys[2, 1] = unit(2, 1, pair_banks("banks1"), "tab_rows")
        features(3, cos3, "cos2")

        tags = {(0, 0): "table1", (0, 1): "cos3", (1, 0): "rounded2", (1, 1): "rounded3"}
        rounded = {key: keep.tile([P, HALF, PACK], BF16, name="rounded", tag=tags[key], align_bytes=64) for key in tags}

        def round_rows(engine_copy, words, rows):
            engine_copy(words.rearrange("p (c i) t -> p c t i", i=4), rows.rearrange("p t (c i) -> p c t i", i=4))

        def round_y(engine_copy, c, g, cols=slice(0, CHUNK)):
            h, part = divmod(c, HALF // CHUNK)
            base = CHUNK * part
            round_rows(engine_copy, rounded[h, g][:, base + cols.start : base + cols.stop, :], ys[c, g][:, :, cols])

        def quantize_y(h, g, part):
            cols = slice(HALF * h + part.start, HALF * h + part.stop)
            quantize(y_codes[:, g, cols], y_plane[:, g, cols], rounded[h, g][:, part, :].rearrange("p n t -> p (n t)"))

        def store_codes(g, cols):
            nc.sync.dma_start(out_words[:, g, cols], y_codes[:, g, cols])

        round_y(nc.scalar.copy, 2, 0, pieces[0])
        ys[3, 0] = unit(3, 0, pair_banks("banks0"), "dc_raw")
        ys[3, 1] = unit(3, 1, pair_banks("banks0"), "ds_raw0")
        round_y(nc.vector.tensor_copy, 0, 0)
        round_y(nc.vector.tensor_copy, 1, 0)
        round_y(nc.vector.tensor_copy, 2, 1)
        quantize_y(0, 0, whole)
        store_codes(0, whole)
        round_rows(nc.vector.tensor_copy, rounded[0, 1][:], wide[:])
        round_y(nc.vector.tensor_copy, 2, 0, pieces[1])
        quantize_y(1, 1, first)
        quantize_y(0, 1, whole)
        store_codes(1, slice(0, S - CHUNK))
        round_y(nc.scalar.copy, 3, 0)
        for piece in pieces:
            round_y(nc.scalar.copy, 3, 1, piece)
        quantize_y(1, 0, whole)
        store_codes(0, slice(HALF, S))
        for piece in pieces:
            quantize_y(1, 1, slice(CHUNK + piece.start, CHUNK + piece.stop))
            store_codes(1, slice(S - CHUNK + piece.start, S - CHUNK + piece.stop))
        for r in range(4):
            queue = (nc.scalar, nc.sync)[r % 2]
            queue.dma_start(out_planes[r], y_plane[r:P:QUAD, :, :].bitcast(I32))
